import numpy as np
import ml_dtypes


def mxq(x, axis, fmt="e4m3"):
    dtype, down = {"e4m3": (ml_dtypes.float8_e4m3fn, 7), "e5m2": (ml_dtypes.float8_e5m2, 14)}[fmt]
    v = np.moveaxis(np.asarray(x, np.float32).astype(ml_dtypes.bfloat16).astype(np.float64), axis, -1)
    blocks = v.reshape(v.shape[:-1] + (-1, 32))
    amax = np.abs(blocks).max(-1, keepdims=True)
    byte = np.maximum(np.where(amax > 0, np.frexp(amax)[1] - 1 + 127, 0) - down, 1)
    scale = np.exp2(byte - 127.0)
    codes = (blocks / scale).astype(np.float32).astype(dtype).astype(np.float64)
    return np.moveaxis((codes * scale).reshape(v.shape), -1, axis)


WIDE = False


def mx_kscale(k):
    if not WIDE:
        return np.ones(k)
    levels = np.array([10, -10, 5, -5, 0])
    if k % 512:
        return np.exp2(np.random.permutation(np.resize(levels, k // 32))).repeat(32)
    a = np.empty((k // 512, 16))
    for p in range(k // 512):
        a[p, :8] = np.random.permutation(np.resize(levels, 8))
        for g in range(8):
            far = levels[np.abs(levels - a[p, g]) >= 10]
            a[p, g + 8] = far[np.random.randint(len(far))]
    return np.exp2(a.ravel()).repeat(32)


def f64(x):
    return np.asarray(x).astype(np.float64)


def striped(idx):
    return np.tile(idx.reshape(-1, 16).T, (8, 1)).astype(np.uint16)


def unstriped(offs):
    return offs[:16].T.reshape(-1).astype(np.int64)


E2M1 = np.array([0.0, 0.5, 1.0, 1.5, 2.0, 3.0, 4.0, 6.0, -0.0, -0.5, -1.0, -1.5, -2.0, -3.0, -4.0, -6.0])


def pack_weight(w, fmt):
    k, n = w.shape
    w = f64(np.asarray(w, np.float32).astype(ml_dtypes.bfloat16)).reshape(k // 32, 32, n)
    amax = np.abs(w).max(1)
    if fmt == "e4m3":
        byte = np.frexp(amax)[1] - 1 + 127 - 7
    else:
        mant, ex = np.frexp(amax / 6.0)
        byte = np.where(mant > 0.5, ex, ex - 1) + 127
    byte = np.clip(np.where(amax > 0, byte, 1), 1, 254)
    scaled = (w * np.exp2(127.0 - byte)[:, None, :]).reshape(k, n).astype(np.float32)
    by_word = np.ascontiguousarray(scaled.reshape(k // 512, 128, 4, n).transpose(0, 1, 3, 2))
    if fmt == "e4m3":
        words = by_word.astype(ml_dtypes.float8_e4m3fn).view(np.uint8)
    else:
        c = by_word.astype(ml_dtypes.float4_e2m1fn).view(np.uint8) & 0xF
        words = (c[..., 0::2] | (c[..., 1::2] << 4)).reshape(k // 512, 128, 2 * n)
    return np.ascontiguousarray(words), np.ascontiguousarray(byte.astype(np.uint8).reshape(k // 512, 16, n))


def unpack_weight(words, scales, fmt):
    g, _, n = scales.shape
    words = np.ascontiguousarray(words).reshape(g, 128, n, -1)
    if fmt == "e4m3":
        vals = words.view(ml_dtypes.float8_e4m3fn).astype(np.float64)
    else:
        nib = np.empty((g, 128, n, 4), np.uint8)
        nib[..., 0::2] = words & 0xF
        nib[..., 1::2] = words >> 4
        vals = E2M1[nib]
    vals = vals * np.repeat(np.exp2(scales.astype(np.float64) - 127.0), 8, axis=1)[..., None]
    return vals.transpose(0, 1, 3, 2).reshape(g * 512, n)


def gelu(v):
    return 0.5 * v * (1.0 + np.tanh(np.sqrt(2.0 / np.pi) * (v + 0.044715 * v**3)))


def bf(x):
    return np.asarray(x, np.float32).astype(ml_dtypes.bfloat16)


def planes(Y):
    n, m = Y.shape
    b = f64(bf(Y)).reshape(n // 32, 32, m)
    amax = np.abs(b).max(1)
    byte = np.clip(np.where(amax > 0, np.frexp(amax)[1] - 1 + 127 - 7, 1), 1, 254)
    codes = (b * np.exp2(127.0 - byte)[:, None, :]).reshape(n, m).astype(np.float32).astype(ml_dtypes.float8_e4m3fn).view(np.uint8)
    words = codes.reshape(n // 512, 128, 4, m).transpose(0, 1, 3, 2)
    return np.ascontiguousarray(words), np.ascontiguousarray(byte.astype(np.uint8).reshape(n // 512, 16, m))


K, K3, H, N, T, T2, T3, S = 1024, 512, 1024, 1024, 2048, 2048, 1024, 512

def setup_inputs():
    n = np.random.standard_normal
    s = mx_kscale(K)[:, None]
    s3 = mx_kscale(K3)[:, None]
    u = mx_kscale(H)[:, None]
    tab_words, tab_scales = pack_weight(n((K, T)) * s, "e4m3")
    tab2_words, tab2_scales = pack_weight(n((K, T2)) * s, "e4m3")
    tab3_words, tab3_scales = pack_weight(n((K3, T3)) * s3, "e2m1")
    w2_words, w2_scales = pack_weight(n((K, H)) * u.T / s / np.sqrt(K), "e2m1")
    return {
        "tab_words": tab_words, "tab_scales": tab_scales,
        "tab2_words": tab2_words, "tab2_scales": tab2_scales,
        "tab3_words": tab3_words, "tab3_scales": tab3_scales,
        "offs": striped(np.random.permutation(T)[:S]),
        "offs2": striped(np.random.permutation(T2)[:S]),
        "offs3": striped(np.random.permutation(T3)[:S]),
        "w1": (n((K, H)) * u.T / s / np.sqrt(K)).astype(np.float32),
        "w2_words": w2_words, "w2_scales": w2_scales,
        "w3": (n((K3, H)) / u.T / s3 / np.sqrt(K3)).astype(np.float32),
        "bd": (0.5 * n(H) / u[:, 0]).astype(np.float32),
        "wo": (n((H, N)) / u / np.sqrt(H)).astype(np.float32),
        "go": np.exp(0.8 * n(N)).astype(np.float32),
    }

def reference(tab_words, tab_scales, tab2_words, tab2_scales, tab3_words, tab3_scales, offs, offs2, offs3, w1, w2_words, w2_scales, w3, bd, wo, go):
    v = unpack_weight(tab_words, tab_scales, "e4m3")[:, unstriped(offs)]
    v2 = unpack_weight(tab2_words, tab2_scales, "e4m3")[:, unstriped(offs2)]
    v3 = unpack_weight(tab3_words, tab3_scales, "e2m1")[:, unstriped(offs3)]
    word = mxq(f64(w1), 0, "e4m3").T @ v
    sense = unpack_weight(w2_words, w2_scales, "e2m1").T @ v2
    dom = (mxq(f64(w3), 0, "e4m3").T @ v3) + f64(bd)[:, None]
    h = word - np.tanh(word * dom) * sense
    y = f64(go)[:, None] * (mxq(f64(wo), 0, "e4m3").T @ mxq(h, 0, "e4m3"))
    words, scales = planes(y)
    return y, words, scales

@@ -1,0 +1,259 @@
+from contextlib import ExitStack
+
+import concourse.mybir as mybir
+
+K, K3, H, N, T, T2, T3, S = 1024, 512, 1024, 1024, 2048, 2048, 1024, 512
+FLOPS = 2 * S * (2 * K * H + K3 * H + H * N)
+
+F32 = mybir.dt.float32
+BF16 = mybir.dt.bfloat16
+I32 = mybir.dt.int32
+U32 = mybir.dt.uint32
+U16 = mybir.dt.uint16
+U8 = mybir.dt.uint8
+FP8X4 = mybir.dt.float8_e4m3fn_x4
+FP4X4 = mybir.dt.float4_e2m1fn_x4
+ALU = mybir.AluOpType
+ACT = mybir.ActivationFunctionType
+
+P = 128
+PACK = 4
+G = P * PACK
+QUADS = 4
+
+
+def tile_list_crossword_clue_features_kernel(
+    tc, tab_words, tab_scales, tab2_words, tab2_scales, tab3_words, tab3_scales,
+    offs, offs2, offs3, w1, w2_words, w2_scales, w3, bd, wo, go, out_0, out_1, out_2,
+):
+    nc = tc.nc
+    with ExitStack() as ctx:
+        lists = ctx.enter_context(tc.tile_pool(name="lists", bufs=1))
+        keep = ctx.enter_context(tc.tile_pool(name="keep", bufs=1))
+        raws = ctx.enter_context(tc.tile_pool(name="raws", bufs=6))
+        rounded = ctx.enter_context(tc.tile_pool(name="rounded", bufs=3))
+        wide = ctx.enter_context(tc.tile_pool(name="wide", bufs=2))
+        psum = ctx.enter_context(tc.psum_pool(name="psum", bufs=1))
+
+        def held(shape, dtype, name):
+            return keep.tile(shape, dtype, name=name, align_bytes=64)
+
+        def bank(b):
+            return psum.tile([P, S], F32, name="bank%d" % b)
+
+        list1 = lists.tile([P, S // 16], U16, name="list1")
+        list2 = lists.tile([P, S // 16], U16, name="list2")
+        list3 = lists.tile([P, S // 16], U16, name="list3")
+
+        tab_w = [held([P, T], U32, "tab_w%d" % a) for a in range(2)]
+        tab2_w = [held([P, T2], U32, "tab2_w%d" % a) for a in range(2)]
+        tab3_w = held([P, T3], U16, "tab3_w")
+        tab_s = held([P, T], U8, "tab_s")
+        tab2_s = held([P, T2], U8, "tab2_s")
+        tab3_s = held([P, T3], U8, "tab3_s")
+        w2_w = held([P, 2, H], U16, "w2_w")
+        w2_s = held([P, 2, H], U8, "w2_s")
+        bd_sb = held([P, 2, PACK], F32, "bd_sb")
+        go_sb = held([P, 2, PACK], F32, "go_sb")
+        v2_s1 = held([P, S], U8, "v2_s1")
+        warm = held([P, 8], F32, "warm")
+
+        nc.vector.memset(warm[:], 0.0)
+        nc.scalar.activation(warm[:, 0:1], warm[:, 1:2], ACT.Tanh)
+        for plane in (tab_s[:], tab3_s[:], tab2_s[:], w2_s[:].rearrange("p a c -> p (a c)"), v2_s1[:]):
+            nc.vector.memset(plane.bitcast(I32), 0)
+
+        def load_raw(w, a, g):
+            raw = raws.tile([P, PACK, G], F32, name="raw")
+            nc.sync.dma_start(
+                out=raw[:], in_=w[G * a : G * (a + 1), G * g : G * (g + 1)].rearrange("(p j) c -> p j c", j=PACK))
+            return raw
+
+        def load_words(dst, src, a):
+            nc.sync.dma_start(out=dst[:].bitcast(I32), in_=src[a].rearrange("p c i -> p (c i)").bitcast(I32))
+
+        def load_stacked_scales(queue, dst, src):
+            passes = src.shape[0]
+            for q in range(QUADS):
+                queue.dma_start(
+                    out=dst[32 * q : 32 * q + 4 * passes, :].bitcast(I32),
+                    in_=src[:, 4 * q : 4 * q + 4, :].bitcast(I32))
+
+        raw = {}
+        nc.sync.dma_start(list1[:], offs)
+        nc.sync.dma_start(list3[:], offs3)
+        nc.sync.dma_start(list2[:], offs2)
+        nc.sync.dma_start(out=bd_sb[:], in_=bd.rearrange("(g p t) -> p g t", p=P, t=PACK))
+        nc.sync.dma_start(out=go_sb[:], in_=go.rearrange("(g p t) -> p g t", p=P, t=PACK))
+        raw["w1", 0, 0] = load_raw(w1, 0, 0)
+        load_words(tab_w[0], tab_words, 0)
+        raw["w3", 0, 0] = load_raw(w3, 0, 0)
+        load_stacked_scales(nc.sync, tab_s, tab_scales)
+        nc.sync.dma_start(out=tab3_w[:].bitcast(I32), in_=tab3_words[0].bitcast(I32))
+        raw["w1", 1, 0] = load_raw(w1, 1, 0)
+        load_stacked_scales(nc.sync, tab3_s, tab3_scales)
+        load_words(tab_w[1], tab_words, 1)
+        load_words(tab2_w[0], tab2_words, 0)
+        load_stacked_scales(nc.sync, tab2_s, tab2_scales)
+        nc.sync.dma_start(
+            out=w2_w[:].bitcast(I32), in_=w2_words.bitcast(I32).rearrange("a p c -> p a c"))
+        load_words(tab2_w[1], tab2_words, 1)
+        for q in range(QUADS):
+            nc.sync.dma_start(
+                out=w2_s[32 * q : 32 * q + 4].bitcast(I32),
+                in_=w2_scales[:, 4 * q : 4 * q + 4, :].bitcast(I32).rearrange("a r c -> r a c"))
+        for name, w, a, g in (("w3", w3, 0, 1), ("w1", w1, 0, 1), ("w1", w1, 1, 1),
+                              ("wo", wo, 0, 0), ("wo", wo, 1, 0), ("wo", wo, 0, 1), ("wo", wo, 1, 1)):
+            raw[name, a, g] = load_raw(w, a, g)
+
+        grouped = {}
+        codes = {}
+        scales = {}
+
+        def deal(key, on_vector=False):
+            tile = rounded.tile([P, PACK * G], BF16, name="grouped", align_bytes=64)
+            dst = tile[:].rearrange("p (t m j) -> p m j t", t=PACK, j=PACK)
+            src = raw[key][:].rearrange("p j (m t) -> p m j t", t=PACK)
+            if on_vector:
+                nc.vector.tensor_copy(out=dst, in_=src)
+            else:
+                nc.scalar.copy(out=dst, in_=src)
+            grouped[key] = tile
+
+        def quantise(key):
+            name = "%s_%d_%d" % key
+            codes[key] = held([P, G], U32, "codes_" + name)
+            scales[key] = held([P, G], U8, "scales_" + name)
+            nc.vector.quantize_mx(out=codes[key][:].bitcast(FP8X4), scales=scales[key][:], in_=grouped[key][:])
+
+        def gather(window, offsets, dtype, name):
+            dst = held([P, S], dtype, name)
+            nc.vector.tensor_copy(dst[:], window[:].indirect(offsets[:]))
+            return dst
+
+        deal(("w1", 0, 0))
+        v_w0 = gather(tab_w[0], list1, U32, "v_w0")
+        quantise(("w1", 0, 0))
+        deal(("w3", 0, 0))
+        v_s = gather(tab_s, list1, U8, "v_s")
+        v3_w = gather(tab3_w, list3, U16, "v3_w")
+        quantise(("w3", 0, 0))
+        deal(("w1", 1, 0))
+        v3_s = gather(tab3_s, list3, U8, "v3_s")
+        v_w1 = gather(tab_w[1], list1, U32, "v_w1")
+        quantise(("w1", 1, 0))
+        v_w = [v_w0, v_w1]
+
+        word_sb = {}
+        gate = {}
+
+        def word_and_gate(g, t):
+            cols = slice(P * t, P * (t + 1))
+            if t == 0:
+                word_sb[g] = wide.tile([P, PACK, S], F32, name="word_or_y")
+                gate[g] = wide.tile([P, PACK, S], F32, name="gate")
+            dom_ps = bank(t % 2)
+            nc.tensor.matmul_mx(
+                out=dom_ps[:], lhsT=codes["w3", 0, g][:, cols].bitcast(FP8X4), lhsT_scale=scales["w3", 0, g][:, cols],
+                rhs=v3_w[:].bitcast(FP4X4), rhs_scale=v3_s[:], start=True, stop=True)
+            word_ps = bank(2 + t % 2)
+            for a in range(2):
+                nc.tensor.matmul_mx(
+                    out=word_ps[:], lhsT=codes["w1", a, g][:, cols].bitcast(FP8X4),
+                    lhsT_scale=scales["w1", a, g][:, cols],
+                    rhs=v_w[a][:].bitcast(FP8X4), rhs_scale=v_s[4 * a :, :], start=(a == 0), stop=(a == 1))
+            nc.scalar.copy(out=word_sb[g][:, t, :], in_=word_ps[:])
+            nc.vector.scalar_tensor_tensor(
+                out=gate[g][:, t, :], in0=dom_ps[:], scalar=bd_sb[:, g, t : t + 1], in1=word_sb[g][:, t, :],
+                op0=ALU.add, op1=ALU.mult)
+            nc.scalar.activation(gate[g][:, t, :], gate[g][:, t, :], ACT.Tanh)
+
+        for t in range(PACK):
+            word_and_gate(0, t)
+
+        v2_w0 = gather(tab2_w[0], list2, U32, "v2_w0")
+        v2_s0 = gather(tab2_s, list2, U8, "v2_s0")
+        nc.sync.dma_start(out=v2_s1[0:100, :].bitcast(I32), in_=v2_s0[4:104, :].bitcast(I32))
+        w2_pw = held([P, 2, 2, PACK, P], U16, "w2_pw")
+        w2_ps = held([P, 2, 2, PACK, P], U8, "w2_ps")
+        nc.vector.tensor_copy(
+            out=w2_pw[:].rearrange("p a g t m -> p (a g) m t"),
+            in_=w2_w[:].rearrange("p a (g m t) -> p (a g) m t", g=2, t=PACK))
+        nc.vector.tensor_copy(
+            out=w2_ps[:].rearrange("p a g t m -> p (a g) m t"),
+            in_=w2_s[:].rearrange("p a (g m t) -> p (a g) m t", g=2, t=PACK))
+        v2_w1 = gather(tab2_w[1], list2, U32, "v2_w1")
+        v2_w = [v2_w0, v2_w1]
+        v2_s = [v2_s0, v2_s1]
+
+        def gated_sense(g, t):
+            sense_ps = bank(4 + t)
+            for a in range(2):
+                nc.tensor.matmul_mx(
+                    out=sense_ps[:], lhsT=w2_pw[:, a, g, t, :].bitcast(FP4X4), lhsT_scale=w2_ps[:, a, g, t, :],
+                    rhs=v2_w[a][:].bitcast(FP8X4), rhs_scale=v2_s[a][:], start=(a == 0), stop=(a == 1))
+            nc.vector.tensor_tensor(out=gate[g][:, t, :], in0=sense_ps[:], in1=gate[g][:, t, :], op=ALU.mult)
+
+        def finish_h(g):
+            tile = rounded.tile([P, PACK * S], BF16, name="grouped", align_bytes=64)
+            nc.vector.tensor_tensor(
+                out=tile[:].rearrange("p (c i t) -> p c t i", i=4, t=PACK),
+                in0=word_sb[g][:].rearrange("p t (c i) -> p c t i", i=4),
+                in1=gate[g][:].rearrange("p t (c i) -> p c t i", i=4),
+                op=ALU.subtract)
+            grouped["h", g, 0] = tile
+
+        deal(("w3", 0, 1))
+        for t in range(PACK):
+            gated_sense(0, t)
+        quantise(("w3", 0, 1))
+        deal(("w1", 0, 1))
+        finish_h(0)
+        quantise(("w1", 0, 1))
+        deal(("w1", 1, 1))
+        quantise(("h", 0, 0))
+        quantise(("w1", 1, 1))
+        for t in range(PACK):
+            word_and_gate(1, t)
+            gated_sense(1, t)
+            if t < 2:
+                deal(("wo", t, 0))
+                quantise(("wo", t, 0))
+        finish_h(1)
+        deal(("wo", 0, 1))
+        quantise(("h", 1, 0))
+        deal(("wo", 1, 1), on_vector=True)
+        quantise(("wo", 0, 1))
+        quantise(("wo", 1, 1))
+
+        y_scales = held([P, 2, S], U8, "y_scales")
+        for g in range(2):
+            y_sb = wide.tile([P, PACK, S], F32, name="word_or_y")
+            rows = out_0[G * g : G * (g + 1), :].rearrange("(p t) j -> p t j", t=PACK)
+            for t in range(PACK):
+                cols = slice(P * t, P * (t + 1))
+                y_ps = bank(PACK * g + t)
+                for a in range(2):
+                    nc.tensor.matmul_mx(
+                        out=y_ps[:], lhsT=codes["wo", a, g][:, cols].bitcast(FP8X4),
+                        lhsT_scale=scales["wo", a, g][:, cols],
+                        rhs=codes["h", a, 0][:].bitcast(FP8X4), rhs_scale=scales["h", a, 0][:],
+                        start=(a == 0), stop=(a == 1))
+                if t == 1:
+                    nc.vector.tensor_scalar(
+                        out=y_sb[:, t, :], in0=y_ps[:], scalar1=go_sb[:, g, t : t + 1], scalar2=None, op0=ALU.mult)
+                else:
+                    nc.scalar.activation(y_sb[:, t, :], y_ps[:], ACT.Copy, scale=go_sb[:, g, t : t + 1])
+                if t % 2 == 1:
+                    nc.sync.dma_start(out=rows[:, t - 1 : t + 1, :], in_=y_sb[:, t - 1 : t + 1, :])
+            y_bf = rounded.tile([P, PACK * S], BF16, name="grouped", align_bytes=64)
+            nc.vector.tensor_copy(
+                out=y_bf[:].rearrange("p (c i t) -> p c t i", i=4, t=PACK),
+                in_=y_sb[:].rearrange("p t (c i) -> p c t i", i=4))
+            y_codes = held([P, S], U32, "y_codes%d" % g)
+            nc.vector.quantize_mx(out=y_codes[:].bitcast(FP8X4), scales=y_scales[:, g, :], in_=y_bf[:])
+            nc.sync.dma_start(out=out_1[g].rearrange("p m t -> p (m t)").bitcast(I32), in_=y_codes[:].bitcast(I32))
+        for q in range(QUADS):
+            nc.sync.dma_start(
+                out=out_2[:, 4 * q : 4 * q + 4, :].bitcast(I32).rearrange("g r m -> r g m"),
+                in_=y_scales[32 * q : 32 * q + 4].bitcast(I32))

@@ -20,6 +20,9 @@ P = 128
 PACK = 4
 G = P * PACK
 QUADS = 4
+Y_BANKS = ((4, 5, 0, 1), (2, 3, 6, 7))
+HW = S // 2
+QW = S // 4
 
 
 def tile_list_crossword_clue_features_kernel(
@@ -30,9 +33,9 @@ def tile_list_crossword_clue_features_kernel(
     with ExitStack() as ctx:
         lists = ctx.enter_context(tc.tile_pool(name="lists", bufs=1))
         keep = ctx.enter_context(tc.tile_pool(name="keep", bufs=1))
-        raws = ctx.enter_context(tc.tile_pool(name="raws", bufs=6))
-        rounded = ctx.enter_context(tc.tile_pool(name="rounded", bufs=3))
-        wide = ctx.enter_context(tc.tile_pool(name="wide", bufs=2))
+        raws = ctx.enter_context(tc.tile_pool(name="raws", bufs=7))
+        rounded = ctx.enter_context(tc.tile_pool(name="rounded", bufs=4))
+        small = ctx.enter_context(tc.tile_pool(name="small", bufs=4))
         psum = ctx.enter_context(tc.psum_pool(name="psum", bufs=1))
 
         def held(shape, dtype, name):
@@ -49,18 +52,17 @@ def tile_list_crossword_clue_features_kernel(
         tab2_w = [held([P, T2], U32, "tab2_w%d" % a) for a in range(2)]
         tab3_w = held([P, T3], U16, "tab3_w")
         tab_s = held([P, T], U8, "tab_s")
-        tab2_s = held([P, T2], U8, "tab2_s")
+        tab2_s = held([P, 2, T2], U8, "tab2_s")
         tab3_s = held([P, T3], U8, "tab3_s")
         w2_w = held([P, 2, H], U16, "w2_w")
         w2_s = held([P, 2, H], U8, "w2_s")
-        bd_sb = held([P, 2, PACK], F32, "bd_sb")
+        bd_sb = held([P, 2, 8], F32, "bd_sb")
         go_sb = held([P, 2, PACK], F32, "go_sb")
-        v2_s1 = held([P, S], U8, "v2_s1")
         warm = held([P, 8], F32, "warm")
 
         nc.vector.memset(warm[:], 0.0)
         nc.scalar.activation(warm[:, 0:1], warm[:, 1:2], ACT.Tanh)
-        for plane in (tab_s[:], tab3_s[:], tab2_s[:], w2_s[:].rearrange("p a c -> p (a c)"), v2_s1[:]):
+        for plane in (tab_s[:], tab3_s[:], tab2_s[:].rearrange("p a c -> p (a c)"), w2_s[:].rearrange("p a c -> p (a c)")):
             nc.vector.memset(plane.bitcast(I32), 0)
 
         def load_raw(w, a, g):
@@ -68,6 +70,18 @@ def tile_list_crossword_clue_features_kernel(
             nc.sync.dma_start(
                 out=raw[:], in_=w[G * a : G * (a + 1), G * g : G * (g + 1)].rearrange("(p j) c -> p j c", j=PACK))
             return raw
+
+        def load_raw_wo(a, g):
+            raw = raws.tile([P, PACK, G], F32, name="raw")
+            rows = wo[G * a : G * (a + 1), G * g : G * (g + 1)].rearrange("(u j i) c -> i u j c", j=PACK, i=2)
+            for i in range(2):
+                nc.sync.dma_start(out=raw[i:P:2], in_=rows[i])
+            return raw
+
+        def load_bias():
+            runs = bd.rearrange("(g u e) -> u g e", g=2, e=8)
+            for i in range(2):
+                nc.sync.dma_start(out=bd_sb[i:P:2, :, 0:7], in_=runs[:, :, i : i + 7])
 
         def load_words(dst, src, a):
             nc.sync.dma_start(out=dst[:].bitcast(I32), in_=src[a].rearrange("p c i -> p (c i)").bitcast(I32))
@@ -79,32 +93,38 @@ def tile_list_crossword_clue_features_kernel(
                     out=dst[32 * q : 32 * q + 4 * passes, :].bitcast(I32),
                     in_=src[:, 4 * q : 4 * q + 4, :].bitcast(I32))
 
+        def load_side_scales(dst, src):
+            for q in range(QUADS):
+                nc.sync.dma_start(
+                    out=dst[32 * q : 32 * q + 4].bitcast(I32),
+                    in_=src[:, 4 * q : 4 * q + 4, :].bitcast(I32).rearrange("a r c -> r a c"))
+
         raw = {}
-        nc.sync.dma_start(list1[:], offs)
         nc.sync.dma_start(list3[:], offs3)
-        nc.sync.dma_start(list2[:], offs2)
-        nc.sync.dma_start(out=bd_sb[:], in_=bd.rearrange("(g p t) -> p g t", p=P, t=PACK))
-        nc.sync.dma_start(out=go_sb[:], in_=go.rearrange("(g p t) -> p g t", p=P, t=PACK))
-        raw["w1", 0, 0] = load_raw(w1, 0, 0)
-        load_words(tab_w[0], tab_words, 0)
-        raw["w3", 0, 0] = load_raw(w3, 0, 0)
-        load_stacked_scales(nc.sync, tab_s, tab_scales)
         nc.sync.dma_start(out=tab3_w[:].bitcast(I32), in_=tab3_words[0].bitcast(I32))
-        raw["w1", 1, 0] = load_raw(w1, 1, 0)
+        nc.sync.dma_start(list1[:], offs)
+        nc.sync.dma_start(list2[:], offs2)
+        load_bias()
+        nc.sync.dma_start(out=go_sb[:], in_=go.rearrange("(g p t) -> p g t", p=P, t=PACK))
+        raw["w3", 0, 0] = load_raw(w3, 0, 0)
         load_stacked_scales(nc.sync, tab3_s, tab3_scales)
+        nc.sync.dma_start(out=w2_w[:].bitcast(I32), in_=w2_words.bitcast(I32).rearrange("a p c -> p a c"))
+        raw["w3", 0, 1] = load_raw(w3, 0, 1)
+        load_stacked_scales(nc.sync, tab_s, tab_scales)
+        raw["w1", 0, 0] = load_raw(w1, 0, 0)
+        load_side_scales(w2_s, w2_scales)
+        load_words(tab_w[0], tab_words, 0)
+        load_side_scales(tab2_s, tab2_scales)
+        raw["w1", 1, 0] = load_raw(w1, 1, 0)
         load_words(tab_w[1], tab_words, 1)
         load_words(tab2_w[0], tab2_words, 0)
-        load_stacked_scales(nc.sync, tab2_s, tab2_scales)
-        nc.sync.dma_start(
-            out=w2_w[:].bitcast(I32), in_=w2_words.bitcast(I32).rearrange("a p c -> p a c"))
         load_words(tab2_w[1], tab2_words, 1)
-        for q in range(QUADS):
-            nc.sync.dma_start(
-                out=w2_s[32 * q : 32 * q + 4].bitcast(I32),
-                in_=w2_scales[:, 4 * q : 4 * q + 4, :].bitcast(I32).rearrange("a r c -> r a c"))
-        for name, w, a, g in (("w3", w3, 0, 1), ("w1", w1, 0, 1), ("w1", w1, 1, 1),
-                              ("wo", wo, 0, 0), ("wo", wo, 1, 0), ("wo", wo, 0, 1), ("wo", wo, 1, 1)):
-            raw[name, a, g] = load_raw(w, a, g)
+        raw["w1", 0, 1] = load_raw(w1, 0, 1)
+        raw["w1", 1, 1] = load_raw(w1, 1, 1)
+        raw["wo", 0, 0] = load_raw_wo(0, 0)
+        raw["wo", 1, 0] = load_raw_wo(1, 0)
+        raw["wo", 0, 1] = load_raw_wo(0, 1)
+        raw["wo", 1, 1] = load_raw_wo(1, 1)
 
         grouped = {}
         codes = {}
@@ -112,12 +132,19 @@ def tile_list_crossword_clue_features_kernel(
 
         def deal(key, on_vector=False):
             tile = rounded.tile([P, PACK * G], BF16, name="grouped", align_bytes=64)
-            dst = tile[:].rearrange("p (t m j) -> p m j t", t=PACK, j=PACK)
-            src = raw[key][:].rearrange("p j (m t) -> p m j t", t=PACK)
-            if on_vector:
-                nc.vector.tensor_copy(out=dst, in_=src)
+            if key[0] == "wo":
+                dst = tile[:].rearrange("p (u e m j) -> p u m j e", u=2, e=2, j=PACK)
+                src = raw[key][:].rearrange("p j (m u e) -> p u m j e", u=2, e=2)
+                parts = [(dst[:, u], src[:, u]) for u in range(2)]
             else:
-                nc.scalar.copy(out=dst, in_=src)
+                dst = tile[:].rearrange("p (t u i j) -> p t u j i", t=PACK, i=2, j=PACK)
+                src = raw[key][:].rearrange("p j (u t i) -> p t u j i", t=PACK, i=2)
+                parts = [(dst[:, t : t + 2], src[:, t : t + 2]) for t in (0, 2)]
+            for d, s in parts:
+                if on_vector:
+                    nc.vector.tensor_copy(out=d, in_=s)
+                else:
+                    nc.scalar.copy(out=d, in_=s)
             grouped[key] = tile
 
         def quantise(key):
@@ -131,128 +158,220 @@ def tile_list_crossword_clue_features_kernel(
             nc.vector.tensor_copy(dst[:], window[:].indirect(offsets[:]))
             return dst
 
-        deal(("w1", 0, 0))
-        v_w0 = gather(tab_w[0], list1, U32, "v_w0")
-        quantise(("w1", 0, 0))
-        deal(("w3", 0, 0))
-        v_s = gather(tab_s, list1, U8, "v_s")
-        v3_w = gather(tab3_w, list3, U16, "v3_w")
-        quantise(("w3", 0, 0))
-        deal(("w1", 1, 0))
-        v3_s = gather(tab3_s, list3, U8, "v3_s")
-        v_w1 = gather(tab_w[1], list1, U32, "v_w1")
-        quantise(("w1", 1, 0))
-        v_w = [v_w0, v_w1]
+        w2_pw = held([P, 2, 2, PACK, P], U16, "w2_pw")
+        w2_ps = held([P, 2, 2, PACK, P], U8, "w2_ps")
 
-        word_sb = {}
-        gate = {}
+        def deal_packed(dst, src, pair):
+            nc.vector.tensor_copy(
+                out=dst[:].bitcast(pair).rearrange("p a g t u -> p (a g) t u"),
+                in_=src[:].bitcast(pair).rearrange("p a (g u t) -> p (a g) t u", g=2, t=PACK))
 
-        def word_and_gate(g, t):
+        v_w, v2_w, v2_s = {}, {}, {}
+        gate = [held([P, S // QW, PACK, QW], F32, "gate%d" % g) for g in range(2)]
+        y_sb = [held([P, 2, PACK, HW], F32, "y_sb%d" % g) for g in range(2)]
+        h_codes = [held([P, S], U32, "h_codes%d" % g) for g in range(2)]
+        h_scales = [held([P, S], U8, "h_scales%d" % g) for g in range(2)]
+        y_codes = [held([P, S], U32, "y_codes%d" % g) for g in range(2)]
+        y_scales = held([P, 2, S], U8, "y_scales")
+        word_ps, h_bf, y_ps, y_bf = {}, {}, {}, {}
+
+        def domain(g, t):
             cols = slice(P * t, P * (t + 1))
-            if t == 0:
-                word_sb[g] = wide.tile([P, PACK, S], F32, name="word_or_y")
-                gate[g] = wide.tile([P, PACK, S], F32, name="gate")
             dom_ps = bank(t % 2)
             nc.tensor.matmul_mx(
                 out=dom_ps[:], lhsT=codes["w3", 0, g][:, cols].bitcast(FP8X4), lhsT_scale=scales["w3", 0, g][:, cols],
                 rhs=v3_w[:].bitcast(FP4X4), rhs_scale=v3_s[:], start=True, stop=True)
-            word_ps = bank(2 + t % 2)
-            for a in range(2):
-                nc.tensor.matmul_mx(
-                    out=word_ps[:], lhsT=codes["w1", a, g][:, cols].bitcast(FP8X4),
-                    lhsT_scale=scales["w1", a, g][:, cols],
-                    rhs=v_w[a][:].bitcast(FP8X4), rhs_scale=v_s[4 * a :, :], start=(a == 0), stop=(a == 1))
-            nc.scalar.copy(out=word_sb[g][:, t, :], in_=word_ps[:])
-            nc.vector.scalar_tensor_tensor(
-                out=gate[g][:, t, :], in0=dom_ps[:], scalar=bd_sb[:, g, t : t + 1], in1=word_sb[g][:, t, :],
-                op0=ALU.add, op1=ALU.mult)
-            nc.scalar.activation(gate[g][:, t, :], gate[g][:, t, :], ACT.Tanh)
+            nc.scalar.activation(
+                gate[g][:, :, t, :], dom_ps[:].rearrange("p (q j) -> p q j", j=QW), ACT.Identity, bias=bd_sb[:, g, 2 * t : 2 * t + 1])
 
-        for t in range(PACK):
-            word_and_gate(0, t)
-
-        v2_w0 = gather(tab2_w[0], list2, U32, "v2_w0")
-        v2_s0 = gather(tab2_s, list2, U8, "v2_s0")
-        nc.sync.dma_start(out=v2_s1[0:100, :].bitcast(I32), in_=v2_s0[4:104, :].bitcast(I32))
-        w2_pw = held([P, 2, 2, PACK, P], U16, "w2_pw")
-        w2_ps = held([P, 2, 2, PACK, P], U8, "w2_ps")
-        nc.vector.tensor_copy(
-            out=w2_pw[:].rearrange("p a g t m -> p (a g) m t"),
-            in_=w2_w[:].rearrange("p a (g m t) -> p (a g) m t", g=2, t=PACK))
-        nc.vector.tensor_copy(
-            out=w2_ps[:].rearrange("p a g t m -> p (a g) m t"),
-            in_=w2_s[:].rearrange("p a (g m t) -> p (a g) m t", g=2, t=PACK))
-        v2_w1 = gather(tab2_w[1], list2, U32, "v2_w1")
-        v2_w = [v2_w0, v2_w1]
-        v2_s = [v2_s0, v2_s1]
-
-        def gated_sense(g, t):
-            sense_ps = bank(4 + t)
-            for a in range(2):
-                nc.tensor.matmul_mx(
-                    out=sense_ps[:], lhsT=w2_pw[:, a, g, t, :].bitcast(FP4X4), lhsT_scale=w2_ps[:, a, g, t, :],
-                    rhs=v2_w[a][:].bitcast(FP8X4), rhs_scale=v2_s[a][:], start=(a == 0), stop=(a == 1))
-            nc.vector.tensor_tensor(out=gate[g][:, t, :], in0=sense_ps[:], in1=gate[g][:, t, :], op=ALU.mult)
-
-        def finish_h(g):
-            tile = rounded.tile([P, PACK * S], BF16, name="grouped", align_bytes=64)
-            nc.vector.tensor_tensor(
-                out=tile[:].rearrange("p (c i t) -> p c t i", i=4, t=PACK),
-                in0=word_sb[g][:].rearrange("p t (c i) -> p c t i", i=4),
-                in1=gate[g][:].rearrange("p t (c i) -> p c t i", i=4),
-                op=ALU.subtract)
-            grouped["h", g, 0] = tile
-
-        deal(("w3", 0, 1))
-        for t in range(PACK):
-            gated_sense(0, t)
-        quantise(("w3", 0, 1))
-        deal(("w1", 0, 1))
-        finish_h(0)
-        quantise(("w1", 0, 1))
-        deal(("w1", 1, 1))
-        quantise(("h", 0, 0))
-        quantise(("w1", 1, 1))
-        for t in range(PACK):
-            word_and_gate(1, t)
-            gated_sense(1, t)
-            if t < 2:
-                deal(("wo", t, 0))
-                quantise(("wo", t, 0))
-        finish_h(1)
-        deal(("wo", 0, 1))
-        quantise(("h", 1, 0))
-        deal(("wo", 1, 1), on_vector=True)
-        quantise(("wo", 0, 1))
-        quantise(("wo", 1, 1))
-
-        y_scales = held([P, 2, S], U8, "y_scales")
-        for g in range(2):
-            y_sb = wide.tile([P, PACK, S], F32, name="word_or_y")
-            rows = out_0[G * g : G * (g + 1), :].rearrange("(p t) j -> p t j", t=PACK)
+        def agreement(g, q):
+            slots = slice(QW * q, QW * (q + 1))
+            word_ps[g, q] = bank((2 + q + 6 * g) % 8 if g == 0 else q)
             for t in range(PACK):
                 cols = slice(P * t, P * (t + 1))
-                y_ps = bank(PACK * g + t)
                 for a in range(2):
                     nc.tensor.matmul_mx(
-                        out=y_ps[:], lhsT=codes["wo", a, g][:, cols].bitcast(FP8X4),
-                        lhsT_scale=scales["wo", a, g][:, cols],
-                        rhs=codes["h", a, 0][:].bitcast(FP8X4), rhs_scale=scales["h", a, 0][:],
+                        out=word_ps[g, q][:, QW * t : QW * (t + 1)],
+                        lhsT=codes["w1", a, g][:, cols].bitcast(FP8X4), lhsT_scale=scales["w1", a, g][:, cols],
+                        rhs=v_w[a][:, slots].bitcast(FP8X4), rhs_scale=v_s[4 * a :, slots],
                         start=(a == 0), stop=(a == 1))
-                if t == 1:
+            part = gate[g][:, q]
+            nc.vector.tensor_tensor(
+                out=part, in0=word_ps[g, q][:].rearrange("p (t j) -> p t j", t=PACK), in1=part, op=ALU.mult)
+            nc.scalar.activation(part, part, ACT.Tanh)
+
+        def gated_sense(g, q):
+            slots = slice(QW * q, QW * (q + 1))
+            sense_ps = bank(6 + q % 2)
+            for t in range(PACK):
+                for a in range(2):
+                    nc.tensor.matmul_mx(
+                        out=sense_ps[:, QW * t : QW * (t + 1)],
+                        lhsT=w2_pw[:, a, g, t, :].bitcast(FP4X4), lhsT_scale=w2_ps[:, a, g, t, :],
+                        rhs=v2_w[a][:, slots].bitcast(FP8X4), rhs_scale=v2_s[a][:, slots],
+                        start=(a == 0), stop=(a == 1))
+            part = gate[g][:, q]
+            nc.vector.tensor_tensor(
+                out=part, in0=sense_ps[:].rearrange("p (t j) -> p t j", t=PACK), in1=part, op=ALU.mult)
+
+        def finish_h(g, q):
+            if q % 2 == 0:
+                h_bf[g, q // 2] = small.tile([P, PACK * HW], BF16, name="half", align_bytes=64)
+            dst = h_bf[g, q // 2][:, PACK * QW * (q % 2) : PACK * QW * (q % 2 + 1)]
+            nc.vector.tensor_tensor(
+                out=dst.rearrange("p (c i t) -> p c t i", i=4, t=PACK),
+                in0=word_ps[g, q][:].rearrange("p (t c i) -> p c t i", i=4, t=PACK),
+                in1=gate[g][:, q].rearrange("p t (c i) -> p c t i", i=4),
+                op=ALU.subtract)
+
+        def quantise_h(g, half):
+            slots = slice(HW * half, HW * (half + 1))
+            nc.vector.quantize_mx(
+                out=h_codes[g][:, slots].bitcast(FP8X4), scales=h_scales[g][:, slots], in_=h_bf[g, half][:])
+
+        def out_pass(half, g, pair, a):
+            slots = slice(HW * half, HW * (half + 1))
+            if a == 0:
+                y_ps[half, g, pair] = bank(Y_BANKS[half][2 * g + pair])
+            for e in range(2):
+                t = 2 * pair + e
+                cols = slice(P * t, P * (t + 1))
+                nc.tensor.matmul_mx(
+                    out=y_ps[half, g, pair][:, HW * e : HW * (e + 1)],
+                    lhsT=codes["wo", a, g][:, cols].bitcast(FP8X4), lhsT_scale=scales["wo", a, g][:, cols],
+                    rhs=h_codes[a][:, slots].bitcast(FP8X4), rhs_scale=h_scales[a][:, slots],
+                    start=(a == 0 and e == 0), stop=(a == 1 and e == 1))
+
+        def gain(half, g, pair, on_vector):
+            slots = slice(HW * half, HW * (half + 1))
+            for e in range(2):
+                t = 2 * pair + e
+                src = y_ps[half, g, pair][:, HW * e : HW * (e + 1)]
+                if on_vector:
                     nc.vector.tensor_scalar(
-                        out=y_sb[:, t, :], in0=y_ps[:], scalar1=go_sb[:, g, t : t + 1], scalar2=None, op0=ALU.mult)
+                        out=y_sb[g][:, half, t, :], in0=src, scalar1=go_sb[:, g, t : t + 1], scalar2=None, op0=ALU.mult)
                 else:
-                    nc.scalar.activation(y_sb[:, t, :], y_ps[:], ACT.Copy, scale=go_sb[:, g, t : t + 1])
-                if t % 2 == 1:
-                    nc.sync.dma_start(out=rows[:, t - 1 : t + 1, :], in_=y_sb[:, t - 1 : t + 1, :])
-            y_bf = rounded.tile([P, PACK * S], BF16, name="grouped", align_bytes=64)
-            nc.vector.tensor_copy(
-                out=y_bf[:].rearrange("p (c i t) -> p c t i", i=4, t=PACK),
-                in_=y_sb[:].rearrange("p t (c i) -> p c t i", i=4))
-            y_codes = held([P, S], U32, "y_codes%d" % g)
-            nc.vector.quantize_mx(out=y_codes[:].bitcast(FP8X4), scales=y_scales[:, g, :], in_=y_bf[:])
-            nc.sync.dma_start(out=out_1[g].rearrange("p m t -> p (m t)").bitcast(I32), in_=y_codes[:].bitcast(I32))
+                    nc.scalar.activation(y_sb[g][:, half, t, :], src, ACT.Copy, scale=go_sb[:, g, t : t + 1])
+            if pair == 1:
+                rows = out_0[G * g : G * (g + 1), slots].rearrange("(p t) j -> p t j", t=PACK)
+                nc.sync.dma_start(out=rows, in_=y_sb[g][:, half])
+
+        def round_y(half, g, on_vector):
+            y_bf[half, g] = small.tile([P, PACK * HW], BF16, name="half", align_bytes=64)
+            dst = y_bf[half, g][:].rearrange("p (c i t) -> p c t i", i=4, t=PACK)
+            src = y_sb[g][:, half].rearrange("p t (c i) -> p c t i", i=4)
+            if on_vector:
+                nc.vector.tensor_copy(out=dst, in_=src)
+            else:
+                nc.scalar.copy(out=dst, in_=src)
+
+        def quantise_y(half, g):
+            slots = slice(HW * half, HW * (half + 1))
+            nc.vector.quantize_mx(
+                out=y_codes[g][:, slots].bitcast(FP8X4), scales=y_scales[:, g, slots], in_=y_bf[half, g][:])
+            nc.sync.dma_start(
+                out=out_1[g, :, slots, :].rearrange("p m t -> p (m t)").bitcast(I32),
+                in_=y_codes[g][:, slots].bitcast(I32))
+
+        v3_w = gather(tab3_w, list3, U16, "v3_w")
+        deal(("w3", 0, 0))
+        quantise(("w3", 0, 0))
+        v3_s = gather(tab3_s, list3, U8, "v3_s")
+        domain(0, 0)
+        domain(0, 1)
+        domain(0, 2)
+        domain(0, 3)
+        deal(("w3", 0, 1))
+        quantise(("w3", 0, 1))
+        v_s = gather(tab_s, list1, U8, "v_s")
+        deal(("w1", 0, 0))
+        v_w[0] = gather(tab_w[0], list1, U32, "v_w0")
+        quantise(("w1", 0, 0))
+        deal(("w1", 1, 0))
+        v_w[1] = gather(tab_w[1], list1, U32, "v_w1")
+        quantise(("w1", 1, 0))
+        agreement(0, 0)
+        agreement(0, 1)
+        agreement(0, 2)
+        agreement(0, 3)
+        domain(1, 0)
+        domain(1, 1)
+        domain(1, 2)
+        domain(1, 3)
+        deal_packed(w2_pw, w2_w, U32)
+        deal_packed(w2_ps, w2_s, U16)
+        v2_s[0] = gather(tab2_s[:, 0, :], list2, U8, "v2_s0")
+        v2_s[1] = gather(tab2_s[:, 1, :], list2, U8, "v2_s1")
+        v2_w[0] = gather(tab2_w[0], list2, U32, "v2_w0")
+        v2_w[1] = gather(tab2_w[1], list2, U32, "v2_w1")
+        deal(("w1", 0, 1))
+        quantise(("w1", 0, 1))
+        deal(("w1", 1, 1))
+        quantise(("w1", 1, 1))
+        gated_sense(0, 0)
+        gated_sense(0, 1)
+        finish_h(0, 0)
+        gated_sense(0, 2)
+        finish_h(0, 1)
+        gated_sense(0, 3)
+        finish_h(0, 2)
+        finish_h(0, 3)
+        agreement(1, 0)
+        agreement(1, 1)
+        agreement(1, 2)
+        gated_sense(1, 0)
+        agreement(1, 3)
+        gated_sense(1, 1)
+        finish_h(1, 0)
+        gated_sense(1, 2)
+        finish_h(1, 1)
+        quantise_h(0, 0)
+        quantise_h(1, 0)
+        deal(("wo", 0, 0))
+        quantise(("wo", 0, 0))
+        deal(("wo", 1, 0))
+        quantise(("wo", 1, 0))
+        gated_sense(1, 3)
+        finish_h(1, 2)
+        finish_h(1, 3)
+        quantise_h(0, 1)
+        quantise_h(1, 1)
+        deal(("wo", 0, 1))
+        quantise(("wo", 0, 1))
+        deal(("wo", 1, 1))
+        quantise(("wo", 1, 1))
+        out_pass(0, 0, 0, 0)
+        out_pass(0, 0, 1, 0)
+        out_pass(0, 0, 0, 1)
+        gain(0, 0, 0, False)
+        out_pass(0, 0, 1, 1)
+        gain(0, 0, 1, False)
+        out_pass(0, 1, 0, 0)
+        out_pass(0, 1, 1, 0)
+        out_pass(0, 1, 0, 1)
+        gain(0, 1, 0, False)
+        out_pass(0, 1, 1, 1)
+        gain(0, 1, 1, False)
+        out_pass(1, 0, 0, 0)
+        out_pass(1, 0, 1, 0)
+        out_pass(1, 1, 0, 0)
+        out_pass(1, 1, 1, 0)
+        out_pass(1, 0, 0, 1)
+        gain(1, 0, 0, False)
+        out_pass(1, 0, 1, 1)
+        gain(1, 0, 1, False)
+        out_pass(1, 1, 0, 1)
+        gain(1, 1, 0, True)
+        out_pass(1, 1, 1, 1)
+        gain(1, 1, 1, False)
+        round_y(0, 0, True)
+        round_y(0, 1, True)
+        quantise_y(0, 0)
+        quantise_y(0, 1)
+        round_y(1, 0, True)
+        round_y(1, 1, True)
+        quantise_y(1, 0)
+        quantise_y(1, 1)
         for q in range(QUADS):
             nc.sync.dma_start(
                 out=out_2[:, 4 * q : 4 * q + 4, :].bitcast(I32).rearrange("g r m -> r g m"),

@@ -20,9 +20,15 @@ P = 128
 PACK = 4
 G = P * PACK
 QUADS = 4
-Y_BANKS = ((4, 5, 0, 1), (2, 3, 6, 7))
 HW = S // 2
 QW = S // 4
+KIB = 1024
+
+PLACE = {"bf_w3_0_0":0,"bf_wo_0_0":0,"bf_w3_0_1":4096,"bf_wo_1_0":4096,"bf_w1_0_0":8192,"bf_wo_0_1":8192,"bf_w1_1_0":12288,"bf_wo_1_1":12288,"raw_w3_0_1":16384,"dom0":16384,"raw_w1_1_0":24576,"dom1":24576,"tab2_s":32768,"codes_w1_0_0":33792,"raw_wo_1_0":36864,"gate_1_0":36864,"gate_1_1":38912,"gate_1_2":40960,"gate_1_3":43008,"raw_wo_0_1":45056,"raw_wo_1_1":53248,"y_sb_1_0":47104,"y_sb_0_0":51200}
+DOM_BANKS = (6, 7, 0, 1)
+WORD_BANKS = ((2, 3, 4, 5), (6, 7, 0, 1))
+SENSE_BANKS = ((6, 7, 0, 1), (2, 3, 4, 5))
+Y_BANKS = ((2, 3, 6, 7), (4, 5, 0, 1))
 
 
 def tile_list_crossword_clue_features_kernel(
@@ -33,12 +39,13 @@ def tile_list_crossword_clue_features_kernel(
     with ExitStack() as ctx:
         lists = ctx.enter_context(tc.tile_pool(name="lists", bufs=1))
         keep = ctx.enter_context(tc.tile_pool(name="keep", bufs=1))
-        raws = ctx.enter_context(tc.tile_pool(name="raws", bufs=7))
-        rounded = ctx.enter_context(tc.tile_pool(name="rounded", bufs=4))
-        small = ctx.enter_context(tc.tile_pool(name="small", bufs=4))
+        raws = ctx.enter_context(tc.tile_pool(name="raws", bufs=3))
+        shared = ctx.enter_context(tc.tile_pool(name="shared", bufs=1))
         psum = ctx.enter_context(tc.psum_pool(name="psum", bufs=1))
 
-        def held(shape, dtype, name):
+        def sbuf(shape, dtype, name):
+            if name in PLACE:
+                return shared.tile(shape, dtype, name=name, align_bytes=64, offset=PLACE[name])
             return keep.tile(shape, dtype, name=name, align_bytes=64)
 
         def bank(b):
@@ -48,48 +55,48 @@ def tile_list_crossword_clue_features_kernel(
         list2 = lists.tile([P, S // 16], U16, name="list2")
         list3 = lists.tile([P, S // 16], U16, name="list3")
 
-        tab_w = [held([P, T], U32, "tab_w%d" % a) for a in range(2)]
-        tab2_w = [held([P, T2], U32, "tab2_w%d" % a) for a in range(2)]
-        tab3_w = held([P, T3], U16, "tab3_w")
-        tab_s = held([P, T], U8, "tab_s")
-        tab2_s = held([P, 2, T2], U8, "tab2_s")
-        tab3_s = held([P, T3], U8, "tab3_s")
-        w2_w = held([P, 2, H], U16, "w2_w")
-        w2_s = held([P, 2, H], U8, "w2_s")
-        bd_sb = held([P, 2, 8], F32, "bd_sb")
-        go_sb = held([P, 2, PACK], F32, "go_sb")
-        warm = held([P, 8], F32, "warm")
+        tab_w = [sbuf([P, T], U32, "tab_w%d" % a) for a in range(2)]
+        tab2_w = [sbuf([P, T2], U32, "tab2_w%d" % a) for a in range(2)]
+        tab3_w = sbuf([P, T3], U16, "tab3_w")
+        tab_s = sbuf([P, T], U8, "tab_s")
+        tab2_s = sbuf([P, 2, T2], U8, "tab2_s")
+        tab3_s = sbuf([P, T3], U8, "tab3_s")
+        w2_w = sbuf([P, 2, H], U16, "w2_w")
+        w2_s = sbuf([P, 2, H], U8, "w2_s")
+        bd_sb = sbuf([P, 2, 8], F32, "bd_sb")
+        go_sb = sbuf([P, 2, PACK], F32, "go_sb")
+        warm = sbuf([P, 8], F32, "warm")
 
-        nc.vector.memset(warm[:], 0.0)
+        nc.gpsimd.memset(tab3_s[:].bitcast(I32), 0)
+        nc.gpsimd.memset(warm[:], 0.0)
         nc.scalar.activation(warm[:, 0:1], warm[:, 1:2], ACT.Tanh)
-        for plane in (tab_s[:], tab3_s[:], tab2_s[:].rearrange("p a c -> p (a c)"), w2_s[:].rearrange("p a c -> p (a c)")):
-            nc.vector.memset(plane.bitcast(I32), 0)
+        nc.gpsimd.memset(w2_s[:].rearrange("p a c -> p (a c)").bitcast(I32), 0)
+        nc.vector.memset(tab_s[:].bitcast(I32), 0)
+        nc.vector.memset(tab2_s[:].rearrange("p a c -> p (a c)").bitcast(I32), 0)
 
-        def load_raw(w, a, g):
-            raw = raws.tile([P, PACK, G], F32, name="raw")
-            nc.sync.dma_start(
-                out=raw[:], in_=w[G * a : G * (a + 1), G * g : G * (g + 1)].rearrange("(p j) c -> p j c", j=PACK))
-            return raw
+        raw = {}
 
-        def load_raw_wo(a, g):
-            raw = raws.tile([P, PACK, G], F32, name="raw")
-            rows = wo[G * a : G * (a + 1), G * g : G * (g + 1)].rearrange("(u j i) c -> i u j c", j=PACK, i=2)
-            for i in range(2):
-                nc.sync.dma_start(out=raw[i:P:2], in_=rows[i])
-            return raw
-
-        def load_bias():
-            runs = bd.rearrange("(g u e) -> u g e", g=2, e=8)
-            for i in range(2):
-                nc.sync.dma_start(out=bd_sb[i:P:2, :, 0:7], in_=runs[:, :, i : i + 7])
+        def load_weight(name, w, a, g):
+            if "raw_%s_%d_%d" % (name, a, g) in PLACE:
+                tile = sbuf([P, PACK, G], F32, "raw_%s_%d_%d" % (name, a, g))
+            else:
+                tile = raws.tile([P, PACK, G], F32, name="raw")
+            block = w[G * a : G * (a + 1), G * g : G * (g + 1)]
+            if name == "wo":
+                rows = block.rearrange("(u j i) c -> i u j c", j=PACK, i=2)
+                for i in range(2):
+                    nc.sync.dma_start(out=tile[i:P:2], in_=rows[i])
+            else:
+                nc.sync.dma_start(out=tile[:], in_=block.rearrange("(p j) c -> p j c", j=PACK))
+            raw[name, a, g] = tile
 
         def load_words(dst, src, a):
             nc.sync.dma_start(out=dst[:].bitcast(I32), in_=src[a].rearrange("p c i -> p (c i)").bitcast(I32))
 
-        def load_stacked_scales(queue, dst, src):
+        def load_stacked_scales(dst, src):
             passes = src.shape[0]
             for q in range(QUADS):
-                queue.dma_start(
+                nc.sync.dma_start(
                     out=dst[32 * q : 32 * q + 4 * passes, :].bitcast(I32),
                     in_=src[:, 4 * q : 4 * q + 4, :].bitcast(I32))
 
@@ -99,167 +106,167 @@ def tile_list_crossword_clue_features_kernel(
                     out=dst[32 * q : 32 * q + 4].bitcast(I32),
                     in_=src[:, 4 * q : 4 * q + 4, :].bitcast(I32).rearrange("a r c -> r a c"))
 
-        raw = {}
-        nc.sync.dma_start(list3[:], offs3)
+        load_weight("w3", w3, 0, 0)
         nc.sync.dma_start(out=tab3_w[:].bitcast(I32), in_=tab3_words[0].bitcast(I32))
+        nc.sync.dma_start(list3[:], offs3)
+        bd_runs = bd.rearrange("(g u e) -> u g e", g=2, e=8)
+        for i in range(2):
+            nc.sync.dma_start(out=bd_sb[i:P:2, :, 0:7], in_=bd_runs[:, :, i : i + 7])
         nc.sync.dma_start(list1[:], offs)
         nc.sync.dma_start(list2[:], offs2)
-        load_bias()
-        nc.sync.dma_start(out=go_sb[:], in_=go.rearrange("(g p t) -> p g t", p=P, t=PACK))
-        raw["w3", 0, 0] = load_raw(w3, 0, 0)
-        load_stacked_scales(nc.sync, tab3_s, tab3_scales)
-        nc.sync.dma_start(out=w2_w[:].bitcast(I32), in_=w2_words.bitcast(I32).rearrange("a p c -> p a c"))
-        raw["w3", 0, 1] = load_raw(w3, 0, 1)
-        load_stacked_scales(nc.sync, tab_s, tab_scales)
-        raw["w1", 0, 0] = load_raw(w1, 0, 0)
-        load_side_scales(w2_s, w2_scales)
+        load_stacked_scales(tab3_s, tab3_scales)
+        load_weight("w3", w3, 0, 1)
+        load_stacked_scales(tab_s, tab_scales)
         load_words(tab_w[0], tab_words, 0)
         load_side_scales(tab2_s, tab2_scales)
-        raw["w1", 1, 0] = load_raw(w1, 1, 0)
+        load_weight("w1", w1, 0, 0)
+        load_side_scales(w2_s, w2_scales)
+        load_weight("w1", w1, 1, 0)
         load_words(tab_w[1], tab_words, 1)
+        nc.sync.dma_start(out=w2_w[:].bitcast(I32), in_=w2_words.bitcast(I32).rearrange("a p c -> p a c"))
         load_words(tab2_w[0], tab2_words, 0)
         load_words(tab2_w[1], tab2_words, 1)
-        raw["w1", 0, 1] = load_raw(w1, 0, 1)
-        raw["w1", 1, 1] = load_raw(w1, 1, 1)
-        raw["wo", 0, 0] = load_raw_wo(0, 0)
-        raw["wo", 1, 0] = load_raw_wo(1, 0)
-        raw["wo", 0, 1] = load_raw_wo(0, 1)
-        raw["wo", 1, 1] = load_raw_wo(1, 1)
+        load_weight("w1", w1, 0, 1)
+        load_weight("w1", w1, 1, 1)
+        nc.sync.dma_start(out=go_sb[:], in_=go.rearrange("(g p t) -> p g t", p=P, t=PACK))
+        load_weight("wo", wo, 0, 0)
+        load_weight("wo", wo, 1, 0)
+        load_weight("wo", wo, 0, 1)
+        load_weight("wo", wo, 1, 1)
 
-        grouped = {}
-        codes = {}
-        scales = {}
+        rounded, codes, scales = {}, {}, {}
 
-        def deal(key, on_vector=False):
-            tile = rounded.tile([P, PACK * G], BF16, name="grouped", align_bytes=64)
+        def round_weight(*key):
+            tile = sbuf([P, PACK * G], BF16, "bf_%s_%d_%d" % key)
             if key[0] == "wo":
-                dst = tile[:].rearrange("p (u e m j) -> p u m j e", u=2, e=2, j=PACK)
-                src = raw[key][:].rearrange("p j (m u e) -> p u m j e", u=2, e=2)
-                parts = [(dst[:, u], src[:, u]) for u in range(2)]
+                dst = tile[:].rearrange("p (b e m j) -> p b m j e", b=2, e=2, j=PACK)
+                src = raw[key][:].rearrange("p j (m b e) -> p b m j e", b=2, e=2)
+                parts = [(dst[:, b], src[:, b]) for b in range(2)]
             else:
                 dst = tile[:].rearrange("p (t u i j) -> p t u j i", t=PACK, i=2, j=PACK)
                 src = raw[key][:].rearrange("p j (u t i) -> p t u j i", t=PACK, i=2)
                 parts = [(dst[:, t : t + 2], src[:, t : t + 2]) for t in (0, 2)]
-            for d, s in parts:
-                if on_vector:
-                    nc.vector.tensor_copy(out=d, in_=s)
-                else:
-                    nc.scalar.copy(out=d, in_=s)
-            grouped[key] = tile
+            for part_dst, part_src in parts:
+                nc.scalar.copy(out=part_dst, in_=part_src)
+            rounded[key] = tile
 
-        def quantise(key):
-            name = "%s_%d_%d" % key
-            codes[key] = held([P, G], U32, "codes_" + name)
-            scales[key] = held([P, G], U8, "scales_" + name)
-            nc.vector.quantize_mx(out=codes[key][:].bitcast(FP8X4), scales=scales[key][:], in_=grouped[key][:])
+        def quantise_weight(*key):
+            codes[key] = sbuf([P, G], U32, "codes_%s_%d_%d" % key)
+            scales[key] = sbuf([P, G], U8, "scales_%s_%d_%d" % key)
+            nc.vector.quantize_mx(out=codes[key][:].bitcast(FP8X4), scales=scales[key][:], in_=rounded[key][:])
 
         def gather(window, offsets, dtype, name):
-            dst = held([P, S], dtype, name)
-            nc.vector.tensor_copy(dst[:], window[:].indirect(offsets[:]))
+            dst = sbuf([P, S], dtype, name)
+            nc.vector.tensor_copy(dst[:], window.indirect(offsets[:]))
             return dst
 
-        w2_pw = held([P, 2, 2, PACK, P], U16, "w2_pw")
-        w2_ps = held([P, 2, 2, PACK, P], U8, "w2_ps")
-
-        def deal_packed(dst, src, pair):
+        def deal_w2(src, dtype, pair, name):
+            dst = sbuf([P, 2, 2, PACK, P], dtype, name)
             nc.vector.tensor_copy(
                 out=dst[:].bitcast(pair).rearrange("p a g t u -> p (a g) t u"),
                 in_=src[:].bitcast(pair).rearrange("p a (g u t) -> p (a g) t u", g=2, t=PACK))
+            return dst
 
         v_w, v2_w, v2_s = {}, {}, {}
-        gate = [held([P, S // QW, PACK, QW], F32, "gate%d" % g) for g in range(2)]
-        y_sb = [held([P, 2, PACK, HW], F32, "y_sb%d" % g) for g in range(2)]
-        h_codes = [held([P, S], U32, "h_codes%d" % g) for g in range(2)]
-        h_scales = [held([P, S], U8, "h_scales%d" % g) for g in range(2)]
-        y_codes = [held([P, S], U32, "y_codes%d" % g) for g in range(2)]
-        y_scales = held([P, 2, S], U8, "y_scales")
-        word_ps, h_bf, y_ps, y_bf = {}, {}, {}, {}
+        dom, gate, word_ps, sense_ps, h_bf, y_ps, y_bf = {}, {}, {}, {}, {}, {}, {}
+        h_codes, h_scales, y_sb = {}, {}, {}
+        y_scales = sbuf([P, 2, S], U8, "y_scales")
 
-        def domain(g, t):
-            cols = slice(P * t, P * (t + 1))
-            dom_ps = bank(t % 2)
-            nc.tensor.matmul_mx(
-                out=dom_ps[:], lhsT=codes["w3", 0, g][:, cols].bitcast(FP8X4), lhsT_scale=scales["w3", 0, g][:, cols],
-                rhs=v3_w[:].bitcast(FP4X4), rhs_scale=v3_s[:], start=True, stop=True)
-            nc.scalar.activation(
-                gate[g][:, :, t, :], dom_ps[:].rearrange("p (q j) -> p q j", j=QW), ACT.Identity, bias=bd_sb[:, g, 2 * t : 2 * t + 1])
-
-        def agreement(g, q):
-            slots = slice(QW * q, QW * (q + 1))
-            word_ps[g, q] = bank((2 + q + 6 * g) % 8 if g == 0 else q)
+        def domain(g):
+            dom[g] = sbuf([P, PACK, S], F32, "dom%d" % g)
             for t in range(PACK):
                 cols = slice(P * t, P * (t + 1))
-                for a in range(2):
-                    nc.tensor.matmul_mx(
-                        out=word_ps[g, q][:, QW * t : QW * (t + 1)],
-                        lhsT=codes["w1", a, g][:, cols].bitcast(FP8X4), lhsT_scale=scales["w1", a, g][:, cols],
-                        rhs=v_w[a][:, slots].bitcast(FP8X4), rhs_scale=v_s[4 * a :, slots],
-                        start=(a == 0), stop=(a == 1))
-            part = gate[g][:, q]
+                dom_ps = bank(DOM_BANKS[t])
+                nc.tensor.matmul_mx(
+                    out=dom_ps[:], lhsT=codes["w3", 0, g][:, cols].bitcast(FP8X4),
+                    lhsT_scale=scales["w3", 0, g][:, cols],
+                    rhs=v3_w[:].bitcast(FP4X4), rhs_scale=v3_s[:], start=True, stop=True)
+                nc.scalar.activation(
+                    dom[g][:, t, :], dom_ps[:], ACT.Identity,
+                    bias=bd_sb[:, g, 2 * t : 2 * t + 1])
+
+        def word_pass(g, q, a):
+            slots = slice(QW * q, QW * (q + 1))
+            if a == 0:
+                word_ps[g, q] = bank(WORD_BANKS[g][q])
+            for t in range(PACK):
+                cols = slice(P * t, P * (t + 1))
+                nc.tensor.matmul_mx(
+                    out=word_ps[g, q][:, QW * t : QW * (t + 1)],
+                    lhsT=codes["w1", a, g][:, cols].bitcast(FP8X4), lhsT_scale=scales["w1", a, g][:, cols],
+                    rhs=v_w[a][:, slots].bitcast(FP8X4), rhs_scale=v_s[4 * a :, slots],
+                    start=(a == 0 and t == 0), stop=(a == 1 and t == PACK - 1))
+
+        def sense_pass(g, q, a):
+            slots = slice(QW * q, QW * (q + 1))
+            if a == 0:
+                sense_ps[g, q] = bank(SENSE_BANKS[g][q])
+            for t in range(PACK):
+                nc.tensor.matmul_mx(
+                    out=sense_ps[g, q][:, QW * t : QW * (t + 1)],
+                    lhsT=w2_pw[:, a, g, t, :].bitcast(FP4X4), lhsT_scale=w2_ps[:, a, g, t, :],
+                    rhs=v2_w[a][:, slots].bitcast(FP8X4), rhs_scale=v2_s[a][:, slots],
+                    start=(a == 0 and t == 0), stop=(a == 1 and t == PACK - 1))
+
+        def agreement(g, q):
+            gate[g, q] = sbuf([P, PACK, QW], F32, "gate_%d_%d" % (g, q))
             nc.vector.tensor_tensor(
-                out=part, in0=word_ps[g, q][:].rearrange("p (t j) -> p t j", t=PACK), in1=part, op=ALU.mult)
-            nc.scalar.activation(part, part, ACT.Tanh)
+                out=gate[g, q][:], in0=word_ps[g, q][:].rearrange("p (t j) -> p t j", t=PACK),
+                in1=dom[g][:, :, QW * q : QW * (q + 1)], op=ALU.mult)
+            nc.scalar.activation(gate[g, q][:], gate[g, q][:], ACT.Tanh)
 
         def gated_sense(g, q):
-            slots = slice(QW * q, QW * (q + 1))
-            sense_ps = bank(6 + q % 2)
-            for t in range(PACK):
-                for a in range(2):
-                    nc.tensor.matmul_mx(
-                        out=sense_ps[:, QW * t : QW * (t + 1)],
-                        lhsT=w2_pw[:, a, g, t, :].bitcast(FP4X4), lhsT_scale=w2_ps[:, a, g, t, :],
-                        rhs=v2_w[a][:, slots].bitcast(FP8X4), rhs_scale=v2_s[a][:, slots],
-                        start=(a == 0), stop=(a == 1))
-            part = gate[g][:, q]
             nc.vector.tensor_tensor(
-                out=part, in0=sense_ps[:].rearrange("p (t j) -> p t j", t=PACK), in1=part, op=ALU.mult)
+                out=gate[g, q][:], in0=sense_ps[g, q][:].rearrange("p (t j) -> p t j", t=PACK),
+                in1=gate[g, q][:], op=ALU.mult)
 
         def finish_h(g, q):
             if q % 2 == 0:
-                h_bf[g, q // 2] = small.tile([P, PACK * HW], BF16, name="half", align_bytes=64)
+                h_bf[g, q // 2] = sbuf([P, PACK * HW], BF16, "h_bf_%d_%d" % (g, q // 2))
             dst = h_bf[g, q // 2][:, PACK * QW * (q % 2) : PACK * QW * (q % 2 + 1)]
             nc.vector.tensor_tensor(
                 out=dst.rearrange("p (c i t) -> p c t i", i=4, t=PACK),
                 in0=word_ps[g, q][:].rearrange("p (t c i) -> p c t i", i=4, t=PACK),
-                in1=gate[g][:, q].rearrange("p t (c i) -> p c t i", i=4),
+                in1=gate[g, q][:].rearrange("p t (c i) -> p c t i", i=4),
                 op=ALU.subtract)
 
         def quantise_h(g, half):
-            slots = slice(HW * half, HW * (half + 1))
+            h_codes[g, half] = sbuf([P, HW], U32, "h_codes_%d_%d" % (g, half))
+            h_scales[g, half] = sbuf([P, HW], U8, "h_scales_%d_%d" % (g, half))
             nc.vector.quantize_mx(
-                out=h_codes[g][:, slots].bitcast(FP8X4), scales=h_scales[g][:, slots], in_=h_bf[g, half][:])
+                out=h_codes[g, half][:].bitcast(FP8X4), scales=h_scales[g, half][:], in_=h_bf[g, half][:])
 
         def out_pass(half, g, pair, a):
-            slots = slice(HW * half, HW * (half + 1))
             if a == 0:
                 y_ps[half, g, pair] = bank(Y_BANKS[half][2 * g + pair])
             for e in range(2):
-                t = 2 * pair + e
-                cols = slice(P * t, P * (t + 1))
+                cols = slice(P * (2 * pair + e), P * (2 * pair + e + 1))
                 nc.tensor.matmul_mx(
                     out=y_ps[half, g, pair][:, HW * e : HW * (e + 1)],
                     lhsT=codes["wo", a, g][:, cols].bitcast(FP8X4), lhsT_scale=scales["wo", a, g][:, cols],
-                    rhs=h_codes[a][:, slots].bitcast(FP8X4), rhs_scale=h_scales[a][:, slots],
+                    rhs=h_codes[a, half][:].bitcast(FP8X4), rhs_scale=h_scales[a, half][:],
                     start=(a == 0 and e == 0), stop=(a == 1 and e == 1))
 
         def gain(half, g, pair, on_vector):
-            slots = slice(HW * half, HW * (half + 1))
+            if pair == 0:
+                y_sb[half, g] = sbuf([P, PACK, HW], F32, "y_sb_%d_%d" % (half, g))
             for e in range(2):
                 t = 2 * pair + e
                 src = y_ps[half, g, pair][:, HW * e : HW * (e + 1)]
                 if on_vector:
                     nc.vector.tensor_scalar(
-                        out=y_sb[g][:, half, t, :], in0=src, scalar1=go_sb[:, g, t : t + 1], scalar2=None, op0=ALU.mult)
+                        out=y_sb[half, g][:, t, :], in0=src, scalar1=go_sb[:, g, t : t + 1], scalar2=None,
+                        op0=ALU.mult)
                 else:
-                    nc.scalar.activation(y_sb[g][:, half, t, :], src, ACT.Copy, scale=go_sb[:, g, t : t + 1])
+                    nc.scalar.activation(y_sb[half, g][:, t, :], src, ACT.Copy, scale=go_sb[:, g, t : t + 1])
             if pair == 1:
-                rows = out_0[G * g : G * (g + 1), slots].rearrange("(p t) j -> p t j", t=PACK)
-                nc.sync.dma_start(out=rows, in_=y_sb[g][:, half])
+                rows = out_0[G * g : G * (g + 1), HW * half : HW * (half + 1)].rearrange("(p t) j -> p t j", t=PACK)
+                nc.sync.dma_start(out=rows, in_=y_sb[half, g][:])
 
         def round_y(half, g, on_vector):
-            y_bf[half, g] = small.tile([P, PACK * HW], BF16, name="half", align_bytes=64)
+            y_bf[half, g] = sbuf([P, PACK * HW], BF16, "y_bf_%d_%d" % (half, g))
             dst = y_bf[half, g][:].rearrange("p (c i t) -> p c t i", i=4, t=PACK)
-            src = y_sb[g][:, half].rearrange("p t (c i) -> p c t i", i=4)
+            src = y_sb[half, g][:].rearrange("p t (c i) -> p c t i", i=4)
             if on_vector:
                 nc.vector.tensor_copy(out=dst, in_=src)
             else:
@@ -267,111 +274,80 @@ def tile_list_crossword_clue_features_kernel(
 
         def quantise_y(half, g):
             slots = slice(HW * half, HW * (half + 1))
+            y_codes = sbuf([P, HW], U32, "y_codes_%d_%d" % (half, g))
             nc.vector.quantize_mx(
-                out=y_codes[g][:, slots].bitcast(FP8X4), scales=y_scales[:, g, slots], in_=y_bf[half, g][:])
+                out=y_codes[:].bitcast(FP8X4), scales=y_scales[:, g, slots], in_=y_bf[half, g][:])
             nc.sync.dma_start(
                 out=out_1[g, :, slots, :].rearrange("p m t -> p (m t)").bitcast(I32),
-                in_=y_codes[g][:, slots].bitcast(I32))
+                in_=y_codes[:].bitcast(I32))
 
-        v3_w = gather(tab3_w, list3, U16, "v3_w")
-        deal(("w3", 0, 0))
-        quantise(("w3", 0, 0))
-        v3_s = gather(tab3_s, list3, U8, "v3_s")
-        domain(0, 0)
-        domain(0, 1)
-        domain(0, 2)
-        domain(0, 3)
-        deal(("w3", 0, 1))
-        quantise(("w3", 0, 1))
-        v_s = gather(tab_s, list1, U8, "v_s")
-        deal(("w1", 0, 0))
-        v_w[0] = gather(tab_w[0], list1, U32, "v_w0")
-        quantise(("w1", 0, 0))
-        deal(("w1", 1, 0))
-        v_w[1] = gather(tab_w[1], list1, U32, "v_w1")
-        quantise(("w1", 1, 0))
-        agreement(0, 0)
-        agreement(0, 1)
-        agreement(0, 2)
-        agreement(0, 3)
-        domain(1, 0)
-        domain(1, 1)
-        domain(1, 2)
-        domain(1, 3)
-        deal_packed(w2_pw, w2_w, U32)
-        deal_packed(w2_ps, w2_s, U16)
-        v2_s[0] = gather(tab2_s[:, 0, :], list2, U8, "v2_s0")
-        v2_s[1] = gather(tab2_s[:, 1, :], list2, U8, "v2_s1")
-        v2_w[0] = gather(tab2_w[0], list2, U32, "v2_w0")
-        v2_w[1] = gather(tab2_w[1], list2, U32, "v2_w1")
-        deal(("w1", 0, 1))
-        quantise(("w1", 0, 1))
-        deal(("w1", 1, 1))
-        quantise(("w1", 1, 1))
-        gated_sense(0, 0)
-        gated_sense(0, 1)
-        finish_h(0, 0)
-        gated_sense(0, 2)
-        finish_h(0, 1)
-        gated_sense(0, 3)
-        finish_h(0, 2)
-        finish_h(0, 3)
-        agreement(1, 0)
-        agreement(1, 1)
-        agreement(1, 2)
-        gated_sense(1, 0)
-        agreement(1, 3)
-        gated_sense(1, 1)
-        finish_h(1, 0)
-        gated_sense(1, 2)
-        finish_h(1, 1)
-        quantise_h(0, 0)
-        quantise_h(1, 0)
-        deal(("wo", 0, 0))
-        quantise(("wo", 0, 0))
-        deal(("wo", 1, 0))
-        quantise(("wo", 1, 0))
-        gated_sense(1, 3)
-        finish_h(1, 2)
-        finish_h(1, 3)
-        quantise_h(0, 1)
-        quantise_h(1, 1)
-        deal(("wo", 0, 1))
-        quantise(("wo", 0, 1))
-        deal(("wo", 1, 1))
-        quantise(("wo", 1, 1))
-        out_pass(0, 0, 0, 0)
-        out_pass(0, 0, 1, 0)
-        out_pass(0, 0, 0, 1)
-        gain(0, 0, 0, False)
-        out_pass(0, 0, 1, 1)
-        gain(0, 0, 1, False)
-        out_pass(0, 1, 0, 0)
-        out_pass(0, 1, 1, 0)
-        out_pass(0, 1, 0, 1)
-        gain(0, 1, 0, False)
-        out_pass(0, 1, 1, 1)
-        gain(0, 1, 1, False)
-        out_pass(1, 0, 0, 0)
-        out_pass(1, 0, 1, 0)
-        out_pass(1, 1, 0, 0)
-        out_pass(1, 1, 1, 0)
-        out_pass(1, 0, 0, 1)
-        gain(1, 0, 0, False)
-        out_pass(1, 0, 1, 1)
-        gain(1, 0, 1, False)
-        out_pass(1, 1, 0, 1)
-        gain(1, 1, 0, True)
-        out_pass(1, 1, 1, 1)
-        gain(1, 1, 1, False)
-        round_y(0, 0, True)
-        round_y(0, 1, True)
-        quantise_y(0, 0)
-        quantise_y(0, 1)
-        round_y(1, 0, True)
-        round_y(1, 1, True)
-        quantise_y(1, 0)
-        quantise_y(1, 1)
+        v3_w = gather(tab3_w[:], list3, U16, "v3_w")
+        round_weight("w3", 0, 0)
+        quantise_weight("w3", 0, 0)
+        v3_s = gather(tab3_s[:], list3, U8, "v3_s")
+        round_weight("w3", 0, 1)
+        domain(0)
+        quantise_weight("w3", 0, 1)
+        round_weight("w1", 0, 0)
+        domain(1)
+        v_s = gather(tab_s[:], list1, U8, "v_s")
+        v_w[0] = gather(tab_w[0][:], list1, U32, "v_w0")
+        quantise_weight("w1", 0, 0)
+        round_weight("w1", 1, 0)
+        v_w[1] = gather(tab_w[1][:], list1, U32, "v_w1")
+        quantise_weight("w1", 1, 0)
+        w2_pw = deal_w2(w2_w, U16, U32, "w2_pw")
+        w2_ps = deal_w2(w2_s, U8, U16, "w2_ps")
+        for a in range(2):
+            v2_s[a] = gather(tab2_s[:, a, :], list2, U8, "v2_s%d" % a)
+        for q in range(4):
+            word_pass(0, q, 0)
+        v2_w[0] = gather(tab2_w[0][:], list2, U32, "v2_w0")
+        for q in range(4):
+            word_pass(0, q, 1)
+            agreement(0, q)
+        v2_w[1] = gather(tab2_w[1][:], list2, U32, "v2_w1")
+        for a in range(2):
+            round_weight("w1", a, 1)
+            quantise_weight("w1", a, 1)
+        for a in range(2):
+            for q in range(4):
+                sense_pass(0, q, a)
+        for q in range(4):
+            gated_sense(0, q)
+        for a in range(2):
+            round_weight("wo", a, 0)
+        for q in range(4):
+            word_pass(1, q, 0)
+        for q in range(4):
+            word_pass(1, q, 1)
+            agreement(1, q)
+        for q in range(4):
+            finish_h(0, q)
+            sense_pass(1, q, 0)
+            sense_pass(1, q, 1)
+        for a in range(2):
+            quantise_weight("wo", a, 0)
+        for half in range(2):
+            quantise_h(0, half)
+            for q in (2 * half, 2 * half + 1):
+                gated_sense(1, q)
+            for q in (2 * half, 2 * half + 1):
+                finish_h(1, q)
+            quantise_h(1, half)
+        for a in range(2):
+            round_weight("wo", a, 1)
+            quantise_weight("wo", a, 1)
+        for g in range(2):
+            for half in range(2):
+                for a in range(2):
+                    for pair in range(2):
+                        out_pass(half, g, pair, a)
+                for pair in range(2):
+                    gain(half, g, pair, False)
+                round_y(half, g, True)
+                quantise_y(half, g)
+
         for q in range(QUADS):
             nc.sync.dma_start(
                 out=out_2[:, 4 * q : 4 * q + 4, :].bitcast(I32).rearrange("g r m -> r g m"),

@@ -20,11 +20,28 @@ P = 128
 PACK = 4
 G = P * PACK
 QUADS = 4
-HW = S // 2
-QW = S // 4
+HALF = S // 2
+QUARTER = S // 4
 KIB = 1024
 
-PLACE = {"bf_w3_0_0":0,"bf_wo_0_0":0,"bf_w3_0_1":4096,"bf_wo_1_0":4096,"bf_w1_0_0":8192,"bf_wo_0_1":8192,"bf_w1_1_0":12288,"bf_wo_1_1":12288,"raw_w3_0_1":16384,"dom0":16384,"raw_w1_1_0":24576,"dom1":24576,"tab2_s":32768,"codes_w1_0_0":33792,"raw_wo_1_0":36864,"gate_1_0":36864,"gate_1_1":38912,"gate_1_2":40960,"gate_1_3":43008,"raw_wo_0_1":45056,"raw_wo_1_1":53248,"y_sb_1_0":47104,"y_sb_0_0":51200}
+SHARED = {
+    "bf_w3_0_0": 0, "bf_wo_0_0": 0,
+    "bf_w3_0_1": 4 * KIB, "bf_wo_1_0": 4 * KIB,
+    "bf_w1_0_0": 8 * KIB, "bf_wo_0_1": 8 * KIB,
+    "bf_w1_1_0": 12 * KIB, "bf_wo_1_1": 12 * KIB,
+    "raw_w3_0_1": 16 * KIB, "dom0": 16 * KIB,
+    "raw_w1_1_0": 24 * KIB, "dom1": 24 * KIB,
+    "tab2_s": 32 * KIB, "codes_w1_0_0": 33 * KIB,
+    "tab_w0": 60 * KIB, "codes_w3_0_1": 60 * KIB,
+    "w2_s": 68 * KIB, "scales_w1_0_0": 68 * KIB,
+    "tab2_w0": 70 * KIB, "gate_0_0": 70 * KIB, "gate_0_1": 72 * KIB,
+    "tab2_w1": 78 * KIB, "gate_0_2": 78 * KIB, "gate_0_3": 80 * KIB,
+    "raw_wo_1_0": 36 * KIB,
+    "gate_1_0": 36 * KIB, "gate_1_1": 38 * KIB, "gate_1_2": 40 * KIB, "gate_1_3": 42 * KIB,
+    "raw_wo_0_1": 44 * KIB, "raw_wo_1_1": 52 * KIB, "y_1_0": 46 * KIB, "y_0_0": 50 * KIB,
+}
+ROUNDED_ON_VECTOR = ("wo", 0, 0)
+
 DOM_BANKS = (6, 7, 0, 1)
 WORD_BANKS = ((2, 3, 4, 5), (6, 7, 0, 1))
 SENSE_BANKS = ((6, 7, 0, 1), (2, 3, 4, 5))
@@ -44,8 +61,8 @@ def tile_list_crossword_clue_features_kernel(
         psum = ctx.enter_context(tc.psum_pool(name="psum", bufs=1))
 
         def sbuf(shape, dtype, name):
-            if name in PLACE:
-                return shared.tile(shape, dtype, name=name, align_bytes=64, offset=PLACE[name])
+            if name in SHARED:
+                return shared.tile(shape, dtype, name=name, align_bytes=64, offset=SHARED[name])
             return keep.tile(shape, dtype, name=name, align_bytes=64)
 
         def bank(b):
@@ -65,11 +82,8 @@ def tile_list_crossword_clue_features_kernel(
         w2_s = sbuf([P, 2, H], U8, "w2_s")
         bd_sb = sbuf([P, 2, 8], F32, "bd_sb")
         go_sb = sbuf([P, 2, PACK], F32, "go_sb")
-        warm = sbuf([P, 8], F32, "warm")
 
         nc.gpsimd.memset(tab3_s[:].bitcast(I32), 0)
-        nc.gpsimd.memset(warm[:], 0.0)
-        nc.scalar.activation(warm[:, 0:1], warm[:, 1:2], ACT.Tanh)
         nc.gpsimd.memset(w2_s[:].rearrange("p a c -> p (a c)").bitcast(I32), 0)
         nc.vector.memset(tab_s[:].bitcast(I32), 0)
         nc.vector.memset(tab2_s[:].rearrange("p a c -> p (a c)").bitcast(I32), 0)
@@ -77,8 +91,9 @@ def tile_list_crossword_clue_features_kernel(
         raw = {}
 
         def load_weight(name, w, a, g):
-            if "raw_%s_%d_%d" % (name, a, g) in PLACE:
-                tile = sbuf([P, PACK, G], F32, "raw_%s_%d_%d" % (name, a, g))
+            own_name = "raw_%s_%d_%d" % (name, a, g)
+            if own_name in SHARED:
+                tile = sbuf([P, PACK, G], F32, own_name)
             else:
                 tile = raws.tile([P, PACK, G], F32, name="raw")
             block = w[G * a : G * (a + 1), G * g : G * (g + 1)]
@@ -93,18 +108,18 @@ def tile_list_crossword_clue_features_kernel(
         def load_words(dst, src, a):
             nc.sync.dma_start(out=dst[:].bitcast(I32), in_=src[a].rearrange("p c i -> p (c i)").bitcast(I32))
 
-        def load_stacked_scales(dst, src):
+        def load_scales_stacked(dst, src):
             passes = src.shape[0]
-            for q in range(QUADS):
+            for quad in range(QUADS):
                 nc.sync.dma_start(
-                    out=dst[32 * q : 32 * q + 4 * passes, :].bitcast(I32),
-                    in_=src[:, 4 * q : 4 * q + 4, :].bitcast(I32))
+                    out=dst[32 * quad : 32 * quad + 4 * passes, :].bitcast(I32),
+                    in_=src[:, 4 * quad : 4 * quad + 4, :].bitcast(I32))
 
-        def load_side_scales(dst, src):
-            for q in range(QUADS):
+        def load_scales_side_by_side(dst, src):
+            for quad in range(QUADS):
                 nc.sync.dma_start(
-                    out=dst[32 * q : 32 * q + 4].bitcast(I32),
-                    in_=src[:, 4 * q : 4 * q + 4, :].bitcast(I32).rearrange("a r c -> r a c"))
+                    out=dst[32 * quad : 32 * quad + 4].bitcast(I32),
+                    in_=src[:, 4 * quad : 4 * quad + 4, :].bitcast(I32).rearrange("a r c -> r a c"))
 
         load_weight("w3", w3, 0, 0)
         nc.sync.dma_start(out=tab3_w[:].bitcast(I32), in_=tab3_words[0].bitcast(I32))
@@ -114,25 +129,24 @@ def tile_list_crossword_clue_features_kernel(
             nc.sync.dma_start(out=bd_sb[i:P:2, :, 0:7], in_=bd_runs[:, :, i : i + 7])
         nc.sync.dma_start(list1[:], offs)
         nc.sync.dma_start(list2[:], offs2)
-        load_stacked_scales(tab3_s, tab3_scales)
+        load_scales_stacked(tab3_s, tab3_scales)
         load_weight("w3", w3, 0, 1)
-        load_stacked_scales(tab_s, tab_scales)
+        load_scales_stacked(tab_s, tab_scales)
         load_words(tab_w[0], tab_words, 0)
-        load_side_scales(tab2_s, tab2_scales)
+        load_scales_side_by_side(tab2_s, tab2_scales)
         load_weight("w1", w1, 0, 0)
-        load_side_scales(w2_s, w2_scales)
+        load_scales_side_by_side(w2_s, w2_scales)
         load_weight("w1", w1, 1, 0)
         load_words(tab_w[1], tab_words, 1)
         nc.sync.dma_start(out=w2_w[:].bitcast(I32), in_=w2_words.bitcast(I32).rearrange("a p c -> p a c"))
-        load_words(tab2_w[0], tab2_words, 0)
-        load_words(tab2_w[1], tab2_words, 1)
-        load_weight("w1", w1, 0, 1)
-        load_weight("w1", w1, 1, 1)
+        for a in range(2):
+            load_words(tab2_w[a], tab2_words, a)
+        for a in range(2):
+            load_weight("w1", w1, a, 1)
         nc.sync.dma_start(out=go_sb[:], in_=go.rearrange("(g p t) -> p g t", p=P, t=PACK))
-        load_weight("wo", wo, 0, 0)
-        load_weight("wo", wo, 1, 0)
-        load_weight("wo", wo, 0, 1)
-        load_weight("wo", wo, 1, 1)
+        for g in range(2):
+            for a in range(2):
+                load_weight("wo", wo, a, g)
 
         rounded, codes, scales = {}, {}, {}
 
@@ -147,7 +161,10 @@ def tile_list_crossword_clue_features_kernel(
                 src = raw[key][:].rearrange("p j (u t i) -> p t u j i", t=PACK, i=2)
                 parts = [(dst[:, t : t + 2], src[:, t : t + 2]) for t in (0, 2)]
             for part_dst, part_src in parts:
-                nc.scalar.copy(out=part_dst, in_=part_src)
+                if key == ROUNDED_ON_VECTOR:
+                    nc.vector.tensor_copy(out=part_dst, in_=part_src)
+                else:
+                    nc.scalar.copy(out=part_dst, in_=part_src)
             rounded[key] = tile
 
         def quantise_weight(*key):
@@ -163,13 +180,13 @@ def tile_list_crossword_clue_features_kernel(
         def deal_w2(src, dtype, pair, name):
             dst = sbuf([P, 2, 2, PACK, P], dtype, name)
             nc.vector.tensor_copy(
-                out=dst[:].bitcast(pair).rearrange("p a g t u -> p (a g) t u"),
-                in_=src[:].bitcast(pair).rearrange("p a (g u t) -> p (a g) t u", g=2, t=PACK))
+                out=dst[:].bitcast(pair).rearrange("p a g t u -> p (a g) u t"),
+                in_=src[:].bitcast(pair).rearrange("p a (g u t) -> p (a g) u t", g=2, t=PACK))
             return dst
 
         v_w, v2_w, v2_s = {}, {}, {}
-        dom, gate, word_ps, sense_ps, h_bf, y_ps, y_bf = {}, {}, {}, {}, {}, {}, {}
-        h_codes, h_scales, y_sb = {}, {}, {}
+        dom, gate, word_ps, sense_ps, h_bf, h_codes, h_scales = {}, {}, {}, {}, {}, {}, {}
+        y_ps, y, y_bf = {}, {}, {}
         y_scales = sbuf([P, 2, S], U8, "y_scales")
 
         def domain(g):
@@ -182,37 +199,36 @@ def tile_list_crossword_clue_features_kernel(
                     lhsT_scale=scales["w3", 0, g][:, cols],
                     rhs=v3_w[:].bitcast(FP4X4), rhs_scale=v3_s[:], start=True, stop=True)
                 nc.scalar.activation(
-                    dom[g][:, t, :], dom_ps[:], ACT.Identity,
-                    bias=bd_sb[:, g, 2 * t : 2 * t + 1])
+                    dom[g][:, t, :], dom_ps[:], ACT.Identity, bias=bd_sb[:, g, 2 * t : 2 * t + 1])
 
         def word_pass(g, q, a):
-            slots = slice(QW * q, QW * (q + 1))
+            slots = slice(QUARTER * q, QUARTER * (q + 1))
             if a == 0:
                 word_ps[g, q] = bank(WORD_BANKS[g][q])
             for t in range(PACK):
                 cols = slice(P * t, P * (t + 1))
                 nc.tensor.matmul_mx(
-                    out=word_ps[g, q][:, QW * t : QW * (t + 1)],
+                    out=word_ps[g, q][:, QUARTER * t : QUARTER * (t + 1)],
                     lhsT=codes["w1", a, g][:, cols].bitcast(FP8X4), lhsT_scale=scales["w1", a, g][:, cols],
                     rhs=v_w[a][:, slots].bitcast(FP8X4), rhs_scale=v_s[4 * a :, slots],
                     start=(a == 0 and t == 0), stop=(a == 1 and t == PACK - 1))
 
         def sense_pass(g, q, a):
-            slots = slice(QW * q, QW * (q + 1))
+            slots = slice(QUARTER * q, QUARTER * (q + 1))
             if a == 0:
                 sense_ps[g, q] = bank(SENSE_BANKS[g][q])
             for t in range(PACK):
                 nc.tensor.matmul_mx(
-                    out=sense_ps[g, q][:, QW * t : QW * (t + 1)],
-                    lhsT=w2_pw[:, a, g, t, :].bitcast(FP4X4), lhsT_scale=w2_ps[:, a, g, t, :],
+                    out=sense_ps[g, q][:, QUARTER * t : QUARTER * (t + 1)],
+                    lhsT=w2_dealt_w[:, a, g, t, :].bitcast(FP4X4), lhsT_scale=w2_dealt_s[:, a, g, t, :],
                     rhs=v2_w[a][:, slots].bitcast(FP8X4), rhs_scale=v2_s[a][:, slots],
                     start=(a == 0 and t == 0), stop=(a == 1 and t == PACK - 1))
 
         def agreement(g, q):
-            gate[g, q] = sbuf([P, PACK, QW], F32, "gate_%d_%d" % (g, q))
+            gate[g, q] = sbuf([P, PACK, QUARTER], F32, "gate_%d_%d" % (g, q))
             nc.vector.tensor_tensor(
                 out=gate[g, q][:], in0=word_ps[g, q][:].rearrange("p (t j) -> p t j", t=PACK),
-                in1=dom[g][:, :, QW * q : QW * (q + 1)], op=ALU.mult)
+                in1=dom[g][:, :, QUARTER * q : QUARTER * (q + 1)], op=ALU.mult)
             nc.scalar.activation(gate[g, q][:], gate[g, q][:], ACT.Tanh)
 
         def gated_sense(g, q):
@@ -222,17 +238,17 @@ def tile_list_crossword_clue_features_kernel(
 
         def finish_h(g, q):
             if q % 2 == 0:
-                h_bf[g, q // 2] = sbuf([P, PACK * HW], BF16, "h_bf_%d_%d" % (g, q // 2))
-            dst = h_bf[g, q // 2][:, PACK * QW * (q % 2) : PACK * QW * (q % 2 + 1)]
+                h_bf[g, q // 2] = sbuf([P, PACK * HALF], BF16, "h_bf_%d_%d" % (g, q // 2))
+            dst = h_bf[g, q // 2][:, PACK * QUARTER * (q % 2) : PACK * QUARTER * (q % 2 + 1)]
             nc.vector.tensor_tensor(
-                out=dst.rearrange("p (c i t) -> p c t i", i=4, t=PACK),
-                in0=word_ps[g, q][:].rearrange("p (t c i) -> p c t i", i=4, t=PACK),
-                in1=gate[g, q][:].rearrange("p t (c i) -> p c t i", i=4),
+                out=dst.rearrange("p (c i t) -> p c t i", i=2, t=PACK),
+                in0=word_ps[g, q][:].rearrange("p (t c i) -> p c t i", i=2, t=PACK),
+                in1=gate[g, q][:].rearrange("p t (c i) -> p c t i", i=2),
                 op=ALU.subtract)
 
         def quantise_h(g, half):
-            h_codes[g, half] = sbuf([P, HW], U32, "h_codes_%d_%d" % (g, half))
-            h_scales[g, half] = sbuf([P, HW], U8, "h_scales_%d_%d" % (g, half))
+            h_codes[g, half] = sbuf([P, HALF], U32, "h_codes_%d_%d" % (g, half))
+            h_scales[g, half] = sbuf([P, HALF], U8, "h_scales_%d_%d" % (g, half))
             nc.vector.quantize_mx(
                 out=h_codes[g, half][:].bitcast(FP8X4), scales=h_scales[g, half][:], in_=h_bf[g, half][:])
 
@@ -242,39 +258,27 @@ def tile_list_crossword_clue_features_kernel(
             for e in range(2):
                 cols = slice(P * (2 * pair + e), P * (2 * pair + e + 1))
                 nc.tensor.matmul_mx(
-                    out=y_ps[half, g, pair][:, HW * e : HW * (e + 1)],
+                    out=y_ps[half, g, pair][:, HALF * e : HALF * (e + 1)],
                     lhsT=codes["wo", a, g][:, cols].bitcast(FP8X4), lhsT_scale=scales["wo", a, g][:, cols],
                     rhs=h_codes[a, half][:].bitcast(FP8X4), rhs_scale=h_scales[a, half][:],
                     start=(a == 0 and e == 0), stop=(a == 1 and e == 1))
 
-        def gain(half, g, pair, on_vector):
-            if pair == 0:
-                y_sb[half, g] = sbuf([P, PACK, HW], F32, "y_sb_%d_%d" % (half, g))
-            for e in range(2):
-                t = 2 * pair + e
-                src = y_ps[half, g, pair][:, HW * e : HW * (e + 1)]
-                if on_vector:
-                    nc.vector.tensor_scalar(
-                        out=y_sb[half, g][:, t, :], in0=src, scalar1=go_sb[:, g, t : t + 1], scalar2=None,
-                        op0=ALU.mult)
-                else:
-                    nc.scalar.activation(y_sb[half, g][:, t, :], src, ACT.Copy, scale=go_sb[:, g, t : t + 1])
-            if pair == 1:
-                rows = out_0[G * g : G * (g + 1), HW * half : HW * (half + 1)].rearrange("(p t) j -> p t j", t=PACK)
-                nc.sync.dma_start(out=rows, in_=y_sb[half, g][:])
-
-        def round_y(half, g, on_vector):
-            y_bf[half, g] = sbuf([P, PACK * HW], BF16, "y_bf_%d_%d" % (half, g))
-            dst = y_bf[half, g][:].rearrange("p (c i t) -> p c t i", i=4, t=PACK)
-            src = y_sb[half, g][:].rearrange("p t (c i) -> p c t i", i=4)
-            if on_vector:
-                nc.vector.tensor_copy(out=dst, in_=src)
-            else:
-                nc.scalar.copy(out=dst, in_=src)
+        def gain_and_store(half, g):
+            y[half, g] = sbuf([P, PACK, HALF], F32, "y_%d_%d" % (half, g))
+            for t in range(PACK):
+                nc.scalar.activation(
+                    y[half, g][:, t, :], y_ps[half, g, t // 2][:, HALF * (t % 2) : HALF * (t % 2 + 1)],
+                    ACT.Copy, scale=go_sb[:, g, t : t + 1])
+            rows = out_0[G * g : G * (g + 1), HALF * half : HALF * (half + 1)]
+            nc.sync.dma_start(out=rows.rearrange("(p t) j -> p t j", t=PACK), in_=y[half, g][:])
 
         def quantise_y(half, g):
-            slots = slice(HW * half, HW * (half + 1))
-            y_codes = sbuf([P, HW], U32, "y_codes_%d_%d" % (half, g))
+            slots = slice(HALF * half, HALF * (half + 1))
+            y_bf[half, g] = sbuf([P, PACK * HALF], BF16, "y_bf_%d_%d" % (half, g))
+            nc.vector.tensor_copy(
+                out=y_bf[half, g][:].rearrange("p (c i t) -> p c t i", i=2, t=PACK),
+                in_=y[half, g][:].rearrange("p t (c i) -> p c t i", i=2))
+            y_codes = sbuf([P, HALF], U32, "y_codes_%d_%d" % (half, g))
             nc.vector.quantize_mx(
                 out=y_codes[:].bitcast(FP8X4), scales=y_scales[:, g, slots], in_=y_bf[half, g][:])
             nc.sync.dma_start(
@@ -287,26 +291,27 @@ def tile_list_crossword_clue_features_kernel(
         v3_s = gather(tab3_s[:], list3, U8, "v3_s")
         round_weight("w3", 0, 1)
         domain(0)
-        quantise_weight("w3", 0, 1)
-        round_weight("w1", 0, 0)
-        domain(1)
         v_s = gather(tab_s[:], list1, U8, "v_s")
         v_w[0] = gather(tab_w[0][:], list1, U32, "v_w0")
-        quantise_weight("w1", 0, 0)
-        round_weight("w1", 1, 0)
-        v_w[1] = gather(tab_w[1][:], list1, U32, "v_w1")
-        quantise_weight("w1", 1, 0)
-        w2_pw = deal_w2(w2_w, U16, U32, "w2_pw")
-        w2_ps = deal_w2(w2_s, U8, U16, "w2_ps")
+        quantise_weight("w3", 0, 1)
+        round_weight("w1", 0, 0)
         for a in range(2):
             v2_s[a] = gather(tab2_s[:, a, :], list2, U8, "v2_s%d" % a)
+        w2_dealt_s = deal_w2(w2_s, U8, U16, "w2_dealt_s")
+        quantise_weight("w1", 0, 0)
+        round_weight("w1", 1, 0)
+        domain(1)
+        v_w[1] = gather(tab_w[1][:], list1, U32, "v_w1")
+        quantise_weight("w1", 1, 0)
+        w2_dealt_w = deal_w2(w2_w, U16, U32, "w2_dealt_w")
+
         for q in range(4):
             word_pass(0, q, 0)
-        v2_w[0] = gather(tab2_w[0][:], list2, U32, "v2_w0")
-        for q in range(4):
-            word_pass(0, q, 1)
-            agreement(0, q)
-        v2_w[1] = gather(tab2_w[1][:], list2, U32, "v2_w1")
+        for a in range(2):
+            v2_w[a] = gather(tab2_w[a][:], list2, U32, "v2_w%d" % a)
+            for q in (2 * a, 2 * a + 1):
+                word_pass(0, q, 1)
+                agreement(0, q)
         for a in range(2):
             round_weight("w1", a, 1)
             quantise_weight("w1", a, 1)
@@ -317,6 +322,7 @@ def tile_list_crossword_clue_features_kernel(
             gated_sense(0, q)
         for a in range(2):
             round_weight("wo", a, 0)
+
         for q in range(4):
             word_pass(1, q, 0)
         for q in range(4):
@@ -324,8 +330,8 @@ def tile_list_crossword_clue_features_kernel(
             agreement(1, q)
         for q in range(4):
             finish_h(0, q)
-            sense_pass(1, q, 0)
-            sense_pass(1, q, 1)
+            for a in range(2):
+                sense_pass(1, q, a)
         for a in range(2):
             quantise_weight("wo", a, 0)
         for half in range(2):
@@ -338,17 +344,15 @@ def tile_list_crossword_clue_features_kernel(
         for a in range(2):
             round_weight("wo", a, 1)
             quantise_weight("wo", a, 1)
+
         for g in range(2):
             for half in range(2):
                 for a in range(2):
                     for pair in range(2):
                         out_pass(half, g, pair, a)
-                for pair in range(2):
-                    gain(half, g, pair, False)
-                round_y(half, g, True)
+                gain_and_store(half, g)
                 quantise_y(half, g)
-
-        for q in range(QUADS):
+        for quad in range(QUADS):
             nc.sync.dma_start(
-                out=out_2[:, 4 * q : 4 * q + 4, :].bitcast(I32).rearrange("g r m -> r g m"),
-                in_=y_scales[32 * q : 32 * q + 4].bitcast(I32))
+                out=out_2[:, 4 * quad : 4 * quad + 4, :].bitcast(I32).rearrange("g r m -> r g m"),
+                in_=y_scales[32 * quad : 32 * quad + 4].bitcast(I32))

@@ -80,7 +80,7 @@ def tile_list_crossword_clue_features_kernel(
         tab3_s = sbuf([P, T3], U8, "tab3_s")
         w2_w = sbuf([P, 2, H], U16, "w2_w")
         w2_s = sbuf([P, 2, H], U8, "w2_s")
-        bd_sb = sbuf([P, 2, 8], F32, "bd_sb")
+        bd_sb = sbuf([P, 2, PACK], F32, "bd_sb")
         go_sb = sbuf([P, 2, PACK], F32, "go_sb")
 
         nc.gpsimd.memset(tab3_s[:].bitcast(I32), 0)
@@ -97,12 +97,7 @@ def tile_list_crossword_clue_features_kernel(
             else:
                 tile = raws.tile([P, PACK, G], F32, name="raw")
             block = w[G * a : G * (a + 1), G * g : G * (g + 1)]
-            if name == "wo":
-                rows = block.rearrange("(u j i) c -> i u j c", j=PACK, i=2)
-                for i in range(2):
-                    nc.sync.dma_start(out=tile[i:P:2], in_=rows[i])
-            else:
-                nc.sync.dma_start(out=tile[:], in_=block.rearrange("(p j) c -> p j c", j=PACK))
+            nc.sync.dma_start(out=tile[:], in_=block.rearrange("(p j) c -> p j c", j=PACK))
             raw[name, a, g] = tile
 
         def load_words(dst, src, a):
@@ -124,9 +119,7 @@ def tile_list_crossword_clue_features_kernel(
         load_weight("w3", w3, 0, 0)
         nc.sync.dma_start(out=tab3_w[:].bitcast(I32), in_=tab3_words[0].bitcast(I32))
         nc.sync.dma_start(list3[:], offs3)
-        bd_runs = bd.rearrange("(g u e) -> u g e", g=2, e=8)
-        for i in range(2):
-            nc.sync.dma_start(out=bd_sb[i:P:2, :, 0:7], in_=bd_runs[:, :, i : i + 7])
+        nc.sync.dma_start(out=bd_sb[:], in_=bd.rearrange("(g p t) -> p g t", p=P, t=PACK))
         nc.sync.dma_start(list1[:], offs)
         nc.sync.dma_start(list2[:], offs2)
         load_scales_stacked(tab3_s, tab3_scales)
@@ -152,19 +145,13 @@ def tile_list_crossword_clue_features_kernel(
 
         def round_weight(*key):
             tile = sbuf([P, PACK * G], BF16, "bf_%s_%d_%d" % key)
-            if key[0] == "wo":
-                dst = tile[:].rearrange("p (b e m j) -> p b m j e", b=2, e=2, j=PACK)
-                src = raw[key][:].rearrange("p j (m b e) -> p b m j e", b=2, e=2)
-                parts = [(dst[:, b], src[:, b]) for b in range(2)]
-            else:
-                dst = tile[:].rearrange("p (t u i j) -> p t u j i", t=PACK, i=2, j=PACK)
-                src = raw[key][:].rearrange("p j (u t i) -> p t u j i", t=PACK, i=2)
-                parts = [(dst[:, t : t + 2], src[:, t : t + 2]) for t in (0, 2)]
-            for part_dst, part_src in parts:
+            dst = tile[:].rearrange("p (b e m j) -> p b m j e", b=2, e=2, j=PACK)
+            src = raw[key][:].rearrange("p j (m b e) -> p b m j e", b=2, e=2)
+            for b in range(2):
                 if key == ROUNDED_ON_VECTOR:
-                    nc.vector.tensor_copy(out=part_dst, in_=part_src)
+                    nc.vector.tensor_copy(out=dst[:, b], in_=src[:, b])
                 else:
-                    nc.scalar.copy(out=part_dst, in_=part_src)
+                    nc.scalar.copy(out=dst[:, b], in_=src[:, b])
             rounded[key] = tile
 
         def quantise_weight(*key):
@@ -177,11 +164,11 @@ def tile_list_crossword_clue_features_kernel(
             nc.vector.tensor_copy(dst[:], window.indirect(offsets[:]))
             return dst
 
-        def deal_w2(src, dtype, pair, name):
+        def deal_w2(src, dtype, name):
             dst = sbuf([P, 2, 2, PACK, P], dtype, name)
             nc.vector.tensor_copy(
-                out=dst[:].bitcast(pair).rearrange("p a g t u -> p (a g) u t"),
-                in_=src[:].bitcast(pair).rearrange("p a (g u t) -> p (a g) u t", g=2, t=PACK))
+                out=dst[:].rearrange("p a g t m -> p (a g) t m"),
+                in_=src[:].rearrange("p a (g m t) -> p (a g) t m", g=2, t=PACK))
             return dst
 
         v_w, v2_w, v2_s = {}, {}, {}
@@ -199,7 +186,7 @@ def tile_list_crossword_clue_features_kernel(
                     lhsT_scale=scales["w3", 0, g][:, cols],
                     rhs=v3_w[:].bitcast(FP4X4), rhs_scale=v3_s[:], start=True, stop=True)
                 nc.scalar.activation(
-                    dom[g][:, t, :], dom_ps[:], ACT.Identity, bias=bd_sb[:, g, 2 * t : 2 * t + 1])
+                    dom[g][:, t, :], dom_ps[:], ACT.Identity, bias=bd_sb[:, g, t : t + 1])
 
         def word_pass(g, q, a):
             slots = slice(QUARTER * q, QUARTER * (q + 1))
@@ -297,13 +284,13 @@ def tile_list_crossword_clue_features_kernel(
         round_weight("w1", 0, 0)
         for a in range(2):
             v2_s[a] = gather(tab2_s[:, a, :], list2, U8, "v2_s%d" % a)
-        w2_dealt_s = deal_w2(w2_s, U8, U16, "w2_dealt_s")
+        w2_dealt_s = deal_w2(w2_s, U8, "w2_dealt_s")
         quantise_weight("w1", 0, 0)
         round_weight("w1", 1, 0)
         domain(1)
         v_w[1] = gather(tab_w[1][:], list1, U32, "v_w1")
         quantise_weight("w1", 1, 0)
-        w2_dealt_w = deal_w2(w2_w, U16, U32, "w2_dealt_w")
+        w2_dealt_w = deal_w2(w2_w, U16, "w2_dealt_w")
 
         for q in range(4):
             word_pass(0, q, 0)

@@ -21,31 +21,19 @@ PACK = 4
 G = P * PACK
 QUADS = 4
 HALF = S // 2
-QUARTER = S // 4
-KIB = 1024
+
+ROUNDED_ON_VECTOR = (("w3", 0, 0), ("w3", 0, 1))
 
 SHARED = {
-    "bf_w3_0_0": 0, "bf_wo_0_0": 0,
-    "bf_w3_0_1": 4 * KIB, "bf_wo_1_0": 4 * KIB,
-    "bf_w1_0_0": 8 * KIB, "bf_wo_0_1": 8 * KIB,
-    "bf_w1_1_0": 12 * KIB, "bf_wo_1_1": 12 * KIB,
-    "raw_w3_0_1": 16 * KIB, "dom0": 16 * KIB,
-    "raw_w1_1_0": 24 * KIB, "dom1": 24 * KIB,
-    "tab2_s": 32 * KIB, "codes_w1_0_0": 33 * KIB,
-    "tab_w0": 60 * KIB, "codes_w3_0_1": 60 * KIB,
-    "w2_s": 68 * KIB, "scales_w1_0_0": 68 * KIB,
-    "tab2_w0": 70 * KIB, "gate_0_0": 70 * KIB, "gate_0_1": 72 * KIB,
-    "tab2_w1": 78 * KIB, "gate_0_2": 78 * KIB, "gate_0_3": 80 * KIB,
-    "raw_wo_1_0": 36 * KIB,
-    "gate_1_0": 36 * KIB, "gate_1_1": 38 * KIB, "gate_1_2": 40 * KIB, "gate_1_3": 42 * KIB,
-    "raw_wo_0_1": 44 * KIB, "raw_wo_1_1": 52 * KIB, "y_1_0": 46 * KIB, "y_0_0": 50 * KIB,
+    "bf_w1_0_1": 0, "h_bf_0_0": 0,
+    "bf_w1_1_1": 4096, "bf_w3_0_1": 4096, "h_bf_0_1": 4096,
 }
-ROUNDED_ON_VECTOR = ("wo", 0, 0)
 
-DOM_BANKS = (6, 7, 0, 1)
-WORD_BANKS = ((2, 3, 4, 5), (6, 7, 0, 1))
-SENSE_BANKS = ((6, 7, 0, 1), (2, 3, 4, 5))
-Y_BANKS = ((2, 3, 6, 7), (4, 5, 0, 1))
+LOW, HIGH = (0, 1, 2, 3), (4, 5, 6, 7)
+WORD_BANKS = (LOW, HIGH)
+DOM_BANKS = (HIGH, LOW)
+SENSE_BANKS = (LOW, HIGH)
+Y_BANKS = (LOW, HIGH)
 
 
 def tile_list_crossword_clue_features_kernel(
@@ -56,7 +44,8 @@ def tile_list_crossword_clue_features_kernel(
     with ExitStack() as ctx:
         lists = ctx.enter_context(tc.tile_pool(name="lists", bufs=1))
         keep = ctx.enter_context(tc.tile_pool(name="keep", bufs=1))
-        raws = ctx.enter_context(tc.tile_pool(name="raws", bufs=3))
+        raws = ctx.enter_context(tc.tile_pool(name="raws", bufs=6))
+        bfs = ctx.enter_context(tc.tile_pool(name="bfs", bufs=4))
         shared = ctx.enter_context(tc.tile_pool(name="shared", bufs=1))
         psum = ctx.enter_context(tc.psum_pool(name="psum", bufs=1))
 
@@ -83,19 +72,15 @@ def tile_list_crossword_clue_features_kernel(
         bd_sb = sbuf([P, 2, PACK], F32, "bd_sb")
         go_sb = sbuf([P, 2, PACK], F32, "go_sb")
 
-        nc.gpsimd.memset(tab3_s[:].bitcast(I32), 0)
-        nc.gpsimd.memset(w2_s[:].rearrange("p a c -> p (a c)").bitcast(I32), 0)
         nc.vector.memset(tab_s[:].bitcast(I32), 0)
+        nc.gpsimd.memset(tab3_s[:].bitcast(I32), 0)
         nc.vector.memset(tab2_s[:].rearrange("p a c -> p (a c)").bitcast(I32), 0)
+        nc.gpsimd.memset(w2_s[:].rearrange("p a c -> p (a c)").bitcast(I32), 0)
 
         raw = {}
 
         def load_weight(name, w, a, g):
-            own_name = "raw_%s_%d_%d" % (name, a, g)
-            if own_name in SHARED:
-                tile = sbuf([P, PACK, G], F32, own_name)
-            else:
-                tile = raws.tile([P, PACK, G], F32, name="raw")
+            tile = raws.tile([P, PACK, G], F32, name="raw")
             block = w[G * a : G * (a + 1), G * g : G * (g + 1)]
             nc.sync.dma_start(out=tile[:], in_=block.rearrange("(p j) c -> p j c", j=PACK))
             raw[name, a, g] = tile
@@ -116,26 +101,26 @@ def tile_list_crossword_clue_features_kernel(
                     out=dst[32 * quad : 32 * quad + 4].bitcast(I32),
                     in_=src[:, 4 * quad : 4 * quad + 4, :].bitcast(I32).rearrange("a r c -> r a c"))
 
-        load_weight("w3", w3, 0, 0)
-        nc.sync.dma_start(out=tab3_w[:].bitcast(I32), in_=tab3_words[0].bitcast(I32))
-        nc.sync.dma_start(list3[:], offs3)
-        nc.sync.dma_start(out=bd_sb[:], in_=bd.rearrange("(g p t) -> p g t", p=P, t=PACK))
         nc.sync.dma_start(list1[:], offs)
-        nc.sync.dma_start(list2[:], offs2)
-        load_scales_stacked(tab3_s, tab3_scales)
-        load_weight("w3", w3, 0, 1)
-        load_scales_stacked(tab_s, tab_scales)
-        load_words(tab_w[0], tab_words, 0)
-        load_scales_side_by_side(tab2_s, tab2_scales)
         load_weight("w1", w1, 0, 0)
-        load_scales_side_by_side(w2_s, w2_scales)
+        load_scales_stacked(tab_s, tab_scales)
+        nc.sync.dma_start(list3[:], offs3)
+        load_words(tab_w[0], tab_words, 0)
+        nc.sync.dma_start(out=tab3_w[:].bitcast(I32), in_=tab3_words[0].bitcast(I32))
+        load_scales_stacked(tab3_s, tab3_scales)
         load_weight("w1", w1, 1, 0)
+        load_scales_side_by_side(tab2_s, tab2_scales)
+        nc.sync.dma_start(list2[:], offs2)
         load_words(tab_w[1], tab_words, 1)
+        load_scales_side_by_side(w2_s, w2_scales)
+        load_weight("w3", w3, 0, 0)
+        nc.sync.dma_start(out=bd_sb[:], in_=bd.rearrange("(g p t) -> p g t", p=P, t=PACK))
         nc.sync.dma_start(out=w2_w[:].bitcast(I32), in_=w2_words.bitcast(I32).rearrange("a p c -> p a c"))
         for a in range(2):
             load_words(tab2_w[a], tab2_words, a)
         for a in range(2):
             load_weight("w1", w1, a, 1)
+        load_weight("w3", w3, 0, 1)
         nc.sync.dma_start(out=go_sb[:], in_=go.rearrange("(g p t) -> p g t", p=P, t=PACK))
         for g in range(2):
             for a in range(2):
@@ -144,13 +129,17 @@ def tile_list_crossword_clue_features_kernel(
         rounded, codes, scales = {}, {}, {}
 
         def round_weight(*key):
-            tile = sbuf([P, PACK * G], BF16, "bf_%s_%d_%d" % key)
+            own_name = "bf_%s_%d_%d" % key
+            if own_name in SHARED:
+                tile = sbuf([P, PACK * G], BF16, own_name)
+            else:
+                tile = bfs.tile([P, PACK * G], BF16, name="bf", align_bytes=64)
             dst = tile[:].rearrange("p (b e m j) -> p b m j e", b=2, e=2, j=PACK)
             src = raw[key][:].rearrange("p j (m b e) -> p b m j e", b=2, e=2)
-            for b in range(2):
-                if key == ROUNDED_ON_VECTOR:
-                    nc.vector.tensor_copy(out=dst[:, b], in_=src[:, b])
-                else:
+            if key in ROUNDED_ON_VECTOR:
+                nc.vector.tensor_copy(out=dst, in_=src)
+            else:
+                for b in range(2):
                     nc.scalar.copy(out=dst[:, b], in_=src[:, b])
             rounded[key] = tile
 
@@ -172,65 +161,63 @@ def tile_list_crossword_clue_features_kernel(
             return dst
 
         v_w, v2_w, v2_s = {}, {}, {}
-        dom, gate, word_ps, sense_ps, h_bf, h_codes, h_scales = {}, {}, {}, {}, {}, {}, {}
+        word_ps, sense_ps, word, gate, h_bf, h_codes, h_scales = {}, {}, {}, {}, {}, {}, {}
         y_ps, y, y_bf = {}, {}, {}
         y_scales = sbuf([P, 2, S], U8, "y_scales")
 
-        def domain(g):
-            dom[g] = sbuf([P, PACK, S], F32, "dom%d" % g)
+        def halves(ps):
+            return ps[:].rearrange("p (u j) -> p u j", u=2)
+
+        def word_pass(g, a):
             for t in range(PACK):
                 cols = slice(P * t, P * (t + 1))
-                dom_ps = bank(DOM_BANKS[t])
+                if a == 0:
+                    word_ps[g, t] = bank(WORD_BANKS[g][t])
+                nc.tensor.matmul_mx(
+                    out=word_ps[g, t][:],
+                    lhsT=codes["w1", a, g][:, cols].bitcast(FP8X4), lhsT_scale=scales["w1", a, g][:, cols],
+                    rhs=v_w[a][:].bitcast(FP8X4), rhs_scale=v_s[4 * a :, :], start=(a == 0), stop=(a == 1))
+
+        def keep_word(g):
+            word[g] = sbuf([P, 2, PACK, HALF], F32, "word%d" % g)
+            for t in range(PACK):
+                nc.scalar.copy(out=word[g][:, :, t, :], in_=halves(word_ps[g, t]))
+
+        def agreement(g):
+            gate[g] = sbuf([P, 2, PACK, HALF], F32, "gate%d" % g)
+            for t in range(PACK):
+                cols = slice(P * t, P * (t + 1))
+                dom_ps = bank(DOM_BANKS[g][t])
                 nc.tensor.matmul_mx(
                     out=dom_ps[:], lhsT=codes["w3", 0, g][:, cols].bitcast(FP8X4),
                     lhsT_scale=scales["w3", 0, g][:, cols],
                     rhs=v3_w[:].bitcast(FP4X4), rhs_scale=v3_s[:], start=True, stop=True)
-                nc.scalar.activation(
-                    dom[g][:, t, :], dom_ps[:], ACT.Identity, bias=bd_sb[:, g, t : t + 1])
+                nc.vector.scalar_tensor_tensor(
+                    out=gate[g][:, :, t, :], in0=halves(dom_ps), scalar=bd_sb[:, g, t : t + 1],
+                    in1=word[g][:, :, t, :], op0=ALU.add, op1=ALU.mult)
+                nc.scalar.activation(gate[g][:, :, t, :], gate[g][:, :, t, :], ACT.Tanh)
 
-        def word_pass(g, q, a):
-            slots = slice(QUARTER * q, QUARTER * (q + 1))
-            if a == 0:
-                word_ps[g, q] = bank(WORD_BANKS[g][q])
+        def sense_pass(g, a):
             for t in range(PACK):
-                cols = slice(P * t, P * (t + 1))
+                if a == 0:
+                    sense_ps[g, t] = bank(SENSE_BANKS[g][t])
                 nc.tensor.matmul_mx(
-                    out=word_ps[g, q][:, QUARTER * t : QUARTER * (t + 1)],
-                    lhsT=codes["w1", a, g][:, cols].bitcast(FP8X4), lhsT_scale=scales["w1", a, g][:, cols],
-                    rhs=v_w[a][:, slots].bitcast(FP8X4), rhs_scale=v_s[4 * a :, slots],
-                    start=(a == 0 and t == 0), stop=(a == 1 and t == PACK - 1))
-
-        def sense_pass(g, q, a):
-            slots = slice(QUARTER * q, QUARTER * (q + 1))
-            if a == 0:
-                sense_ps[g, q] = bank(SENSE_BANKS[g][q])
-            for t in range(PACK):
-                nc.tensor.matmul_mx(
-                    out=sense_ps[g, q][:, QUARTER * t : QUARTER * (t + 1)],
+                    out=sense_ps[g, t][:],
                     lhsT=w2_dealt_w[:, a, g, t, :].bitcast(FP4X4), lhsT_scale=w2_dealt_s[:, a, g, t, :],
-                    rhs=v2_w[a][:, slots].bitcast(FP8X4), rhs_scale=v2_s[a][:, slots],
-                    start=(a == 0 and t == 0), stop=(a == 1 and t == PACK - 1))
+                    rhs=v2_w[a][:].bitcast(FP8X4), rhs_scale=v2_s[a][:], start=(a == 0), stop=(a == 1))
 
-        def agreement(g, q):
-            gate[g, q] = sbuf([P, PACK, QUARTER], F32, "gate_%d_%d" % (g, q))
-            nc.vector.tensor_tensor(
-                out=gate[g, q][:], in0=word_ps[g, q][:].rearrange("p (t j) -> p t j", t=PACK),
-                in1=dom[g][:, :, QUARTER * q : QUARTER * (q + 1)], op=ALU.mult)
-            nc.scalar.activation(gate[g, q][:], gate[g, q][:], ACT.Tanh)
+        def gated_sense(g, part):
+            for t in range(PACK):
+                nc.vector.tensor_tensor(
+                    out=gate[g][:, part, t, :], in0=halves(sense_ps[g, t])[:, part, :],
+                    in1=gate[g][:, part, t, :], op=ALU.mult)
 
-        def gated_sense(g, q):
+        def finish_h(g, half):
+            h_bf[g, half] = sbuf([P, PACK * HALF], BF16, "h_bf_%d_%d" % (g, half))
             nc.vector.tensor_tensor(
-                out=gate[g, q][:], in0=sense_ps[g, q][:].rearrange("p (t j) -> p t j", t=PACK),
-                in1=gate[g, q][:], op=ALU.mult)
-
-        def finish_h(g, q):
-            if q % 2 == 0:
-                h_bf[g, q // 2] = sbuf([P, PACK * HALF], BF16, "h_bf_%d_%d" % (g, q // 2))
-            dst = h_bf[g, q // 2][:, PACK * QUARTER * (q % 2) : PACK * QUARTER * (q % 2 + 1)]
-            nc.vector.tensor_tensor(
-                out=dst.rearrange("p (c i t) -> p c t i", i=2, t=PACK),
-                in0=word_ps[g, q][:].rearrange("p (t c i) -> p c t i", i=2, t=PACK),
-                in1=gate[g, q][:].rearrange("p t (c i) -> p c t i", i=2),
+                out=h_bf[g, half][:].rearrange("p (c i t) -> p c t i", i=2, t=PACK),
+                in0=word[g][:, half].rearrange("p t (c i) -> p c t i", i=2),
+                in1=gate[g][:, half].rearrange("p t (c i) -> p c t i", i=2),
                 op=ALU.subtract)
 
         def quantise_h(g, half):
@@ -272,72 +259,61 @@ def tile_list_crossword_clue_features_kernel(
                 out=out_1[g, :, slots, :].rearrange("p m t -> p (m t)").bitcast(I32),
                 in_=y_codes[:].bitcast(I32))
 
-        v3_w = gather(tab3_w[:], list3, U16, "v3_w")
-        round_weight("w3", 0, 0)
-        quantise_weight("w3", 0, 0)
-        v3_s = gather(tab3_s[:], list3, U8, "v3_s")
-        round_weight("w3", 0, 1)
-        domain(0)
-        v_s = gather(tab_s[:], list1, U8, "v_s")
-        v_w[0] = gather(tab_w[0][:], list1, U32, "v_w0")
-        quantise_weight("w3", 0, 1)
         round_weight("w1", 0, 0)
+        v_s = gather(tab_s[:], list1, U8, "v_s")
+        quantise_weight("w1", 0, 0)
+        v_w[0] = gather(tab_w[0][:], list1, U32, "v_w0")
+        word_pass(0, 0)
+        round_weight("w1", 1, 0)
+        v3_w = gather(tab3_w[:], list3, U16, "v3_w")
+        v3_s = gather(tab3_s[:], list3, U8, "v3_s")
+        quantise_weight("w1", 1, 0)
         for a in range(2):
             v2_s[a] = gather(tab2_s[:, a, :], list2, U8, "v2_s%d" % a)
-        w2_dealt_s = deal_w2(w2_s, U8, "w2_dealt_s")
-        quantise_weight("w1", 0, 0)
-        round_weight("w1", 1, 0)
-        domain(1)
         v_w[1] = gather(tab_w[1][:], list1, U32, "v_w1")
-        quantise_weight("w1", 1, 0)
-        w2_dealt_w = deal_w2(w2_w, U16, "w2_dealt_w")
+        word_pass(0, 1)
+        keep_word(0)
+        w2_dealt_s = deal_w2(w2_s, U8, "w2_dealt_s")
+        round_weight("w3", 0, 0)
+        quantise_weight("w3", 0, 0)
+        agreement(0)
 
-        for q in range(4):
-            word_pass(0, q, 0)
+        w2_dealt_w = deal_w2(w2_w, U16, "w2_dealt_w")
         for a in range(2):
             v2_w[a] = gather(tab2_w[a][:], list2, U32, "v2_w%d" % a)
-            for q in (2 * a, 2 * a + 1):
-                word_pass(0, q, 1)
-                agreement(0, q)
+            sense_pass(0, a)
         for a in range(2):
             round_weight("w1", a, 1)
             quantise_weight("w1", a, 1)
+            word_pass(1, a)
+        keep_word(1)
+        gated_sense(0, slice(0, 2))
+        round_weight("w3", 0, 1)
+        quantise_weight("w3", 0, 1)
+        agreement(1)
         for a in range(2):
-            for q in range(4):
-                sense_pass(0, q, a)
-        for q in range(4):
-            gated_sense(0, q)
-        for a in range(2):
-            round_weight("wo", a, 0)
-
-        for q in range(4):
-            word_pass(1, q, 0)
-        for q in range(4):
-            word_pass(1, q, 1)
-            agreement(1, q)
-        for q in range(4):
-            finish_h(0, q)
-            for a in range(2):
-                sense_pass(1, q, a)
-        for a in range(2):
-            quantise_weight("wo", a, 0)
+            sense_pass(1, a)
         for half in range(2):
+            finish_h(0, half)
             quantise_h(0, half)
-            for q in (2 * half, 2 * half + 1):
-                gated_sense(1, q)
-            for q in (2 * half, 2 * half + 1):
-                finish_h(1, q)
-            quantise_h(1, half)
-        for a in range(2):
-            round_weight("wo", a, 1)
-            quantise_weight("wo", a, 1)
-
         for g in range(2):
-            for half in range(2):
-                for a in range(2):
-                    for pair in range(2):
-                        out_pass(half, g, pair, a)
+            for a in range(2):
+                round_weight("wo", a, g)
+                quantise_weight("wo", a, g)
+
+        for half in range(2):
+            gated_sense(1, slice(half, half + 1))
+            for g in range(2):
+                for pair in range(2):
+                    out_pass(half, g, pair, 0)
+            finish_h(1, half)
+            quantise_h(1, half)
+            for g in range(2):
+                for pair in range(2):
+                    out_pass(half, g, pair, 1)
                 gain_and_store(half, g)
+        for half in range(2):
+            for g in range(2):
                 quantise_y(half, g)
         for quad in range(QUADS):
             nc.sync.dma_start(

@@ -21,12 +21,15 @@ PACK = 4
 G = P * PACK
 QUADS = 4
 HALF = S // 2
+KIB = 1024
 
-ROUNDED_ON_VECTOR = (("w3", 0, 0), ("w3", 0, 1))
+ROUNDED_ON_VECTOR = {("w3", 0, 0): (1,), ("w3", 0, 1): (0, 1), ("wo", 1, 0): (0, 1)}
 
 SHARED = {
-    "bf_w1_0_1": 0, "h_bf_0_0": 0,
-    "bf_w1_1_1": 4096, "bf_w3_0_1": 4096, "h_bf_0_1": 4096,
+    "tab2_s": 0, "codes_w1_1_0": 0,
+    "tab2_w0": 4 * KIB, "gate0": 4 * KIB,
+    "bf_w1_0_1": 12 * KIB, "h_bf_0_0": 12 * KIB,
+    "bf_w1_1_1": 16 * KIB, "bf_w3_0_1": 16 * KIB, "h_bf_0_1": 16 * KIB,
 }
 
 LOW, HIGH = (0, 1, 2, 3), (4, 5, 6, 7)
@@ -111,9 +114,9 @@ def tile_list_crossword_clue_features_kernel(
         load_weight("w1", w1, 1, 0)
         load_scales_side_by_side(tab2_s, tab2_scales)
         nc.sync.dma_start(list2[:], offs2)
+        load_weight("w3", w3, 0, 0)
         load_words(tab_w[1], tab_words, 1)
         load_scales_side_by_side(w2_s, w2_scales)
-        load_weight("w3", w3, 0, 0)
         nc.sync.dma_start(out=bd_sb[:], in_=bd.rearrange("(g p t) -> p g t", p=P, t=PACK))
         nc.sync.dma_start(out=w2_w[:].bitcast(I32), in_=w2_words.bitcast(I32).rearrange("a p c -> p a c"))
         for a in range(2):
@@ -136,10 +139,10 @@ def tile_list_crossword_clue_features_kernel(
                 tile = bfs.tile([P, PACK * G], BF16, name="bf", align_bytes=64)
             dst = tile[:].rearrange("p (b e m j) -> p b m j e", b=2, e=2, j=PACK)
             src = raw[key][:].rearrange("p j (m b e) -> p b m j e", b=2, e=2)
-            if key in ROUNDED_ON_VECTOR:
-                nc.vector.tensor_copy(out=dst, in_=src)
-            else:
-                for b in range(2):
+            for b in range(2):
+                if b in ROUNDED_ON_VECTOR.get(key, ()):
+                    nc.vector.tensor_copy(out=dst[:, b], in_=src[:, b])
+                else:
                     nc.scalar.copy(out=dst[:, b], in_=src[:, b])
             rounded[key] = tile
 
@@ -162,7 +165,7 @@ def tile_list_crossword_clue_features_kernel(
 
         v_w, v2_w, v2_s = {}, {}, {}
         word_ps, sense_ps, word, gate, h_bf, h_codes, h_scales = {}, {}, {}, {}, {}, {}, {}
-        y_ps, y, y_bf = {}, {}, {}
+        dom_ps, y_ps, y, y_bf = {}, {}, {}, {}
         y_scales = sbuf([P, 2, S], U8, "y_scales")
 
         def halves(ps):
@@ -183,17 +186,20 @@ def tile_list_crossword_clue_features_kernel(
             for t in range(PACK):
                 nc.scalar.copy(out=word[g][:, :, t, :], in_=halves(word_ps[g, t]))
 
+        def domain(g):
+            for t in range(PACK):
+                cols = slice(P * t, P * (t + 1))
+                dom_ps[g, t] = bank(DOM_BANKS[g][t])
+                nc.tensor.matmul_mx(
+                    out=dom_ps[g, t][:], lhsT=codes["w3", 0, g][:, cols].bitcast(FP8X4),
+                    lhsT_scale=scales["w3", 0, g][:, cols],
+                    rhs=v3_w[:].bitcast(FP4X4), rhs_scale=v3_s[:], start=True, stop=True)
+
         def agreement(g):
             gate[g] = sbuf([P, 2, PACK, HALF], F32, "gate%d" % g)
             for t in range(PACK):
-                cols = slice(P * t, P * (t + 1))
-                dom_ps = bank(DOM_BANKS[g][t])
-                nc.tensor.matmul_mx(
-                    out=dom_ps[:], lhsT=codes["w3", 0, g][:, cols].bitcast(FP8X4),
-                    lhsT_scale=scales["w3", 0, g][:, cols],
-                    rhs=v3_w[:].bitcast(FP4X4), rhs_scale=v3_s[:], start=True, stop=True)
                 nc.vector.scalar_tensor_tensor(
-                    out=gate[g][:, :, t, :], in0=halves(dom_ps), scalar=bd_sb[:, g, t : t + 1],
+                    out=gate[g][:, :, t, :], in0=halves(dom_ps[g, t]), scalar=bd_sb[:, g, t : t + 1],
                     in1=word[g][:, :, t, :], op0=ALU.add, op1=ALU.mult)
                 nc.scalar.activation(gate[g][:, :, t, :], gate[g][:, :, t, :], ACT.Tanh)
 
@@ -267,29 +273,32 @@ def tile_list_crossword_clue_features_kernel(
         round_weight("w1", 1, 0)
         v3_w = gather(tab3_w[:], list3, U16, "v3_w")
         v3_s = gather(tab3_s[:], list3, U8, "v3_s")
-        quantise_weight("w1", 1, 0)
         for a in range(2):
             v2_s[a] = gather(tab2_s[:, a, :], list2, U8, "v2_s%d" % a)
+        quantise_weight("w1", 1, 0)
+        round_weight("w3", 0, 0)
+        quantise_weight("w3", 0, 0)
+        domain(0)
         v_w[1] = gather(tab_w[1][:], list1, U32, "v_w1")
         word_pass(0, 1)
         keep_word(0)
         w2_dealt_s = deal_w2(w2_s, U8, "w2_dealt_s")
-        round_weight("w3", 0, 0)
-        quantise_weight("w3", 0, 0)
+        w2_dealt_w = deal_w2(w2_w, U16, "w2_dealt_w")
+        v2_w[0] = gather(tab2_w[0][:], list2, U32, "v2_w0")
+        sense_pass(0, 0)
         agreement(0)
 
-        w2_dealt_w = deal_w2(w2_w, U16, "w2_dealt_w")
-        for a in range(2):
-            v2_w[a] = gather(tab2_w[a][:], list2, U32, "v2_w%d" % a)
-            sense_pass(0, a)
+        v2_w[1] = gather(tab2_w[1][:], list2, U32, "v2_w1")
+        sense_pass(0, 1)
+        gated_sense(0, slice(0, 2))
         for a in range(2):
             round_weight("w1", a, 1)
             quantise_weight("w1", a, 1)
             word_pass(1, a)
         keep_word(1)
-        gated_sense(0, slice(0, 2))
         round_weight("w3", 0, 1)
         quantise_weight("w3", 0, 1)
+        domain(1)
         agreement(1)
         for a in range(2):
             sense_pass(1, a)

@@ -1,6 +1,7 @@
 from contextlib import ExitStack
 
 import concourse.mybir as mybir
+from concourse.masks import make_identity
 
 K, K3, H, N, T, T2, T3, S = 1024, 512, 1024, 1024, 2048, 2048, 1024, 512
 FLOPS = 2 * S * (2 * K * H + K3 * H + H * N)
@@ -23,13 +24,18 @@ QUADS = 4
 HALF = S // 2
 KIB = 1024
 
-ROUNDED_ON_VECTOR = {("w3", 0, 0): (1,), ("w3", 0, 1): (0, 1), ("wo", 1, 0): (0, 1)}
+ROUNDED_ON_VECTOR = {("w3", 0, 0): (1,), ("wo", 0, 1): (0, 1)}
+RUN = 8
 
 SHARED = {
-    "tab2_s": 0, "codes_w1_1_0": 0,
-    "tab2_w0": 4 * KIB, "gate0": 4 * KIB,
-    "bf_w1_0_1": 12 * KIB, "h_bf_0_0": 12 * KIB,
-    "bf_w1_1_1": 16 * KIB, "bf_w3_0_1": 16 * KIB, "h_bf_0_1": 16 * KIB,
+    "tab2_s": 0, "codes_w1_0_0": 0,
+    "tab2_w1": 4 * KIB, "codes_w1_0_1": 4 * KIB,
+    "bf_w1_1_1": 16 * KIB, "h_bf_0_0": 16 * KIB,
+    "bf_w3_0_1": 12 * KIB, "h_bf_0_1": 12 * KIB,
+    "raw_w3_0_1": 40 * KIB, "word1": 40 * KIB,
+    "bf_wo_1_0": 36 * KIB, "h_bf_1_1": 36 * KIB,
+    "bd_sb": 2 * KIB,
+    "tab_w0": 20 * KIB, "tab_w1": 28 * KIB, "raw_wo0": 20 * KIB,
 }
 
 LOW, HIGH = (0, 1, 2, 3), (4, 5, 6, 7)
@@ -47,8 +53,8 @@ def tile_list_crossword_clue_features_kernel(
     with ExitStack() as ctx:
         lists = ctx.enter_context(tc.tile_pool(name="lists", bufs=1))
         keep = ctx.enter_context(tc.tile_pool(name="keep", bufs=1))
-        raws = ctx.enter_context(tc.tile_pool(name="raws", bufs=6))
-        bfs = ctx.enter_context(tc.tile_pool(name="bfs", bufs=4))
+        raws = ctx.enter_context(tc.tile_pool(name="raws", bufs=4))
+        bfs = ctx.enter_context(tc.tile_pool(name="bfs", bufs=3))
         shared = ctx.enter_context(tc.tile_pool(name="shared", bufs=1))
         psum = ctx.enter_context(tc.psum_pool(name="psum", bufs=1))
 
@@ -74,19 +80,42 @@ def tile_list_crossword_clue_features_kernel(
         w2_s = sbuf([P, 2, H], U8, "w2_s")
         bd_sb = sbuf([P, 2, PACK], F32, "bd_sb")
         go_sb = sbuf([P, 2, PACK], F32, "go_sb")
+        bd_rows = sbuf([P, P], F32, "bd_rows")
+        identity = sbuf([P, P], F32, "identity")
 
+        nc.vector.memset(tab3_s[:].bitcast(I32), 0)
         nc.vector.memset(tab_s[:].bitcast(I32), 0)
-        nc.gpsimd.memset(tab3_s[:].bitcast(I32), 0)
         nc.vector.memset(tab2_s[:].rearrange("p a c -> p (a c)").bitcast(I32), 0)
         nc.gpsimd.memset(w2_s[:].rearrange("p a c -> p (a c)").bitcast(I32), 0)
+        nc.gpsimd.memset(bd_rows[:], 0.0)
+        for g in range(2):
+            nc.gpsimd.dma_start(
+                out=bd_rows[PACK * g : PACK * (g + 1), :].rearrange("t (q u) -> t q u", u=RUN),
+                in_=bd[G * g : G * (g + 1)].rearrange("(q t u) -> t q u", t=PACK, u=RUN))
+        make_identity(nc, identity[:])
+        bd_ps = bank(DOM_BANKS[0][PACK - 1])
+        nc.tensor.transpose(bd_ps[:, :P], bd_rows[:], identity[:])
+        nc.vector.tensor_copy(out=bd_sb[:].rearrange("p g t -> p (g t)"), in_=bd_ps[:, : 2 * PACK])
 
         raw = {}
 
         def load_weight(name, w, a, g):
-            tile = raws.tile([P, PACK, G], F32, name="raw")
+            own_name = "raw_%s_%d_%d" % (name, a, g)
+            if own_name in SHARED:
+                tile = sbuf([P, PACK, G], F32, own_name)
+            else:
+                tile = raws.tile([P, PACK, G], F32, name="raw")
             block = w[G * a : G * (a + 1), G * g : G * (g + 1)]
             nc.sync.dma_start(out=tile[:], in_=block.rearrange("(p j) c -> p j c", j=PACK))
-            raw[name, a, g] = tile
+            raw[name, a, g] = tile[:]
+
+        def load_wo(a):
+            tile = sbuf([P, PACK, N], F32, "raw_wo%d" % a)
+            rows = wo[G * a : G * (a + 1), :].rearrange("(q j u) c -> j q u c", j=PACK, u=RUN)
+            for j in range(PACK):
+                nc.sync.dma_start(out=tile[:, j, :], in_=rows[j])
+            for g in range(2):
+                raw["wo", a, g] = tile[:, :, G * g : G * (g + 1)]
 
         def load_words(dst, src, a):
             nc.sync.dma_start(out=dst[:].bitcast(I32), in_=src[a].rearrange("p c i -> p (c i)").bitcast(I32))
@@ -104,30 +133,28 @@ def tile_list_crossword_clue_features_kernel(
                     out=dst[32 * quad : 32 * quad + 4].bitcast(I32),
                     in_=src[:, 4 * quad : 4 * quad + 4, :].bitcast(I32).rearrange("a r c -> r a c"))
 
-        nc.sync.dma_start(list1[:], offs)
-        load_weight("w1", w1, 0, 0)
-        load_scales_stacked(tab_s, tab_scales)
         nc.sync.dma_start(list3[:], offs3)
-        load_words(tab_w[0], tab_words, 0)
         nc.sync.dma_start(out=tab3_w[:].bitcast(I32), in_=tab3_words[0].bitcast(I32))
         load_scales_stacked(tab3_s, tab3_scales)
-        load_weight("w1", w1, 1, 0)
+        nc.sync.dma_start(list1[:], offs)
+        load_words(tab_w[0], tab_words, 0)
+        load_scales_stacked(tab_s, tab_scales)
+        load_weight("w1", w1, 0, 0)
         load_scales_side_by_side(tab2_s, tab2_scales)
         nc.sync.dma_start(list2[:], offs2)
+        load_weight("w1", w1, 1, 0)
         load_weight("w3", w3, 0, 0)
         load_words(tab_w[1], tab_words, 1)
         load_scales_side_by_side(w2_s, w2_scales)
-        nc.sync.dma_start(out=bd_sb[:], in_=bd.rearrange("(g p t) -> p g t", p=P, t=PACK))
+        load_weight("w1", w1, 0, 1)
         nc.sync.dma_start(out=w2_w[:].bitcast(I32), in_=w2_words.bitcast(I32).rearrange("a p c -> p a c"))
         for a in range(2):
             load_words(tab2_w[a], tab2_words, a)
-        for a in range(2):
-            load_weight("w1", w1, a, 1)
+        load_weight("w1", w1, 1, 1)
         load_weight("w3", w3, 0, 1)
         nc.sync.dma_start(out=go_sb[:], in_=go.rearrange("(g p t) -> p g t", p=P, t=PACK))
-        for g in range(2):
-            for a in range(2):
-                load_weight("wo", wo, a, g)
+        for a in range(2):
+            load_wo(a)
 
         rounded, codes, scales = {}, {}, {}
 
@@ -137,13 +164,19 @@ def tile_list_crossword_clue_features_kernel(
                 tile = sbuf([P, PACK * G], BF16, own_name)
             else:
                 tile = bfs.tile([P, PACK * G], BF16, name="bf", align_bytes=64)
-            dst = tile[:].rearrange("p (b e m j) -> p b m j e", b=2, e=2, j=PACK)
-            src = raw[key][:].rearrange("p j (m b e) -> p b m j e", b=2, e=2)
-            for b in range(2):
+            if key[0] == "wo":
+                dst = tile[:].rearrange("p (b e m j) -> p b m j e", b=2, e=2, j=PACK)
+                src = raw[key].rearrange("p j (m b e) -> p b m j e", b=2, e=2)
+                parts = [(b, dst[:, b], src[:, b]) for b in range(2)]
+            else:
+                dst = tile[:].rearrange("p (t q c i j) -> p t q c j i", t=PACK, c=RUN // 2, i=2, j=PACK)
+                src = raw[key].rearrange("p j (q t c i) -> p t q c j i", t=PACK, c=RUN // 2, i=2)
+                parts = [(t // 2, dst[:, t], src[:, t]) for t in range(PACK)]
+            for b, part_dst, part_src in parts:
                 if b in ROUNDED_ON_VECTOR.get(key, ()):
-                    nc.vector.tensor_copy(out=dst[:, b], in_=src[:, b])
+                    nc.vector.tensor_copy(out=part_dst, in_=part_src)
                 else:
-                    nc.scalar.copy(out=dst[:, b], in_=src[:, b])
+                    nc.scalar.copy(out=part_dst, in_=part_src)
             rounded[key] = tile
 
         def quantise_weight(*key):
@@ -159,8 +192,10 @@ def tile_list_crossword_clue_features_kernel(
         def deal_w2(src, dtype, name):
             dst = sbuf([P, 2, 2, PACK, P], dtype, name)
             nc.vector.tensor_copy(
-                out=dst[:].rearrange("p a g t m -> p (a g) t m"),
-                in_=src[:].rearrange("p a (g m t) -> p (a g) t m", g=2, t=PACK))
+                out=dst[:].rearrange("p a g t m -> p (a g t m)").bitcast(I32).rearrange(
+                    "p (x t q w) -> p x t q w", x=4, t=PACK, q=P // RUN),
+                in_=src[:].rearrange("p a c -> p (a c)").bitcast(I32).rearrange(
+                    "p (x q t w) -> p x t q w", x=4, t=PACK, q=P // RUN))
             return dst
 
         v_w, v2_w, v2_s = {}, {}, {}
@@ -265,16 +300,16 @@ def tile_list_crossword_clue_features_kernel(
                 out=out_1[g, :, slots, :].rearrange("p m t -> p (m t)").bitcast(I32),
                 in_=y_codes[:].bitcast(I32))
 
-        round_weight("w1", 0, 0)
-        v_s = gather(tab_s[:], list1, U8, "v_s")
-        quantise_weight("w1", 0, 0)
-        v_w[0] = gather(tab_w[0][:], list1, U32, "v_w0")
-        word_pass(0, 0)
-        round_weight("w1", 1, 0)
         v3_w = gather(tab3_w[:], list3, U16, "v3_w")
         v3_s = gather(tab3_s[:], list3, U8, "v3_s")
+        v_w[0] = gather(tab_w[0][:], list1, U32, "v_w0")
+        v_s = gather(tab_s[:], list1, U8, "v_s")
+        round_weight("w1", 0, 0)
         for a in range(2):
             v2_s[a] = gather(tab2_s[:, a, :], list2, U8, "v2_s%d" % a)
+        quantise_weight("w1", 0, 0)
+        word_pass(0, 0)
+        round_weight("w1", 1, 0)
         quantise_weight("w1", 1, 0)
         round_weight("w3", 0, 0)
         quantise_weight("w3", 0, 0)
@@ -283,18 +318,19 @@ def tile_list_crossword_clue_features_kernel(
         word_pass(0, 1)
         keep_word(0)
         w2_dealt_s = deal_w2(w2_s, U8, "w2_dealt_s")
-        w2_dealt_w = deal_w2(w2_w, U16, "w2_dealt_w")
-        v2_w[0] = gather(tab2_w[0][:], list2, U32, "v2_w0")
-        sense_pass(0, 0)
         agreement(0)
 
-        v2_w[1] = gather(tab2_w[1][:], list2, U32, "v2_w1")
-        sense_pass(0, 1)
-        gated_sense(0, slice(0, 2))
+        round_weight("w1", 0, 1)
+        w2_dealt_w = deal_w2(w2_w, U16, "w2_dealt_w")
         for a in range(2):
-            round_weight("w1", a, 1)
-            quantise_weight("w1", a, 1)
-            word_pass(1, a)
+            v2_w[a] = gather(tab2_w[a][:], list2, U32, "v2_w%d" % a)
+            sense_pass(0, a)
+        quantise_weight("w1", 0, 1)
+        word_pass(1, 0)
+        gated_sense(0, slice(0, 2))
+        round_weight("w1", 1, 1)
+        quantise_weight("w1", 1, 1)
+        word_pass(1, 1)
         keep_word(1)
         round_weight("w3", 0, 1)
         quantise_weight("w3", 0, 1)
@@ -305,24 +341,29 @@ def tile_list_crossword_clue_features_kernel(
         for half in range(2):
             finish_h(0, half)
             quantise_h(0, half)
-        for g in range(2):
-            for a in range(2):
-                round_weight("wo", a, g)
-                quantise_weight("wo", a, g)
+        for a in range(2):
+            round_weight("wo", a, 0)
+            quantise_weight("wo", a, 0)
 
         for half in range(2):
             gated_sense(1, slice(half, half + 1))
-            for g in range(2):
-                for pair in range(2):
-                    out_pass(half, g, pair, 0)
+            for pair in range(2):
+                out_pass(half, 0, pair, 0)
             finish_h(1, half)
             quantise_h(1, half)
-            for g in range(2):
-                for pair in range(2):
-                    out_pass(half, g, pair, 1)
-                gain_and_store(half, g)
+            for pair in range(2):
+                out_pass(half, 0, pair, 1)
+            round_weight("wo", half, 1)
+            quantise_weight("wo", half, 1)
+            gain_and_store(half, 0)
+
         for half in range(2):
-            for g in range(2):
+            for a in range(2):
+                for pair in range(2):
+                    out_pass(half, 1, pair, a)
+            gain_and_store(half, 1)
+        for g in range(2):
+            for half in range(2):
                 quantise_y(half, g)
         for quad in range(QUADS):
             nc.sync.dma_start(

@@ -1,7 +1,6 @@
 from contextlib import ExitStack
 
 import concourse.mybir as mybir
-from concourse.masks import make_identity
 
 K, K3, H, N, T, T2, T3, S = 1024, 512, 1024, 1024, 2048, 2048, 1024, 512
 FLOPS = 2 * S * (2 * K * H + K3 * H + H * N)
@@ -34,7 +33,6 @@ SHARED = {
     "bf_w3_0_1": 12 * KIB, "h_bf_0_1": 12 * KIB,
     "raw_w3_0_1": 40 * KIB, "word1": 40 * KIB,
     "bf_wo_1_0": 36 * KIB, "h_bf_1_1": 36 * KIB,
-    "bd_sb": 2 * KIB,
     "tab_w0": 20 * KIB, "tab_w1": 28 * KIB, "raw_wo0": 20 * KIB,
 }
 
@@ -78,24 +76,14 @@ def tile_list_crossword_clue_features_kernel(
         tab3_s = sbuf([P, T3], U8, "tab3_s")
         w2_w = sbuf([P, 2, H], U16, "w2_w")
         w2_s = sbuf([P, 2, H], U8, "w2_s")
-        bd_sb = sbuf([P, 2, PACK], F32, "bd_sb")
         go_sb = sbuf([P, 2, PACK], F32, "go_sb")
         bd_rows = sbuf([P, P], F32, "bd_rows")
-        identity = sbuf([P, P], F32, "identity")
 
         nc.vector.memset(tab3_s[:].bitcast(I32), 0)
         nc.vector.memset(tab_s[:].bitcast(I32), 0)
         nc.vector.memset(tab2_s[:].rearrange("p a c -> p (a c)").bitcast(I32), 0)
         nc.gpsimd.memset(w2_s[:].rearrange("p a c -> p (a c)").bitcast(I32), 0)
         nc.gpsimd.memset(bd_rows[:], 0.0)
-        for g in range(2):
-            nc.gpsimd.dma_start(
-                out=bd_rows[PACK * g : PACK * (g + 1), :].rearrange("t (q u) -> t q u", u=RUN),
-                in_=bd[G * g : G * (g + 1)].rearrange("(q t u) -> t q u", t=PACK, u=RUN))
-        make_identity(nc, identity[:])
-        bd_ps = bank(DOM_BANKS[0][PACK - 1])
-        nc.tensor.transpose(bd_ps[:, :P], bd_rows[:], identity[:])
-        nc.vector.tensor_copy(out=bd_sb[:].rearrange("p g t -> p (g t)"), in_=bd_ps[:, : 2 * PACK])
 
         raw = {}
 
@@ -144,6 +132,9 @@ def tile_list_crossword_clue_features_kernel(
         nc.sync.dma_start(list2[:], offs2)
         load_weight("w1", w1, 1, 0)
         load_weight("w3", w3, 0, 0)
+        for g in range(2):
+            nc.sync.dma_start(
+                out=bd_rows[g : P : 32, :], in_=bd[G * g : G * (g + 1)].rearrange("(quad c) -> quad c", quad=QUADS))
         load_words(tab_w[1], tab_words, 1)
         load_scales_side_by_side(w2_s, w2_scales)
         load_weight("w1", w1, 0, 1)
@@ -198,6 +189,15 @@ def tile_list_crossword_clue_features_kernel(
                     "p (x q t w) -> p x t q w", x=4, t=PACK, q=P // RUN))
             return dst
 
+        def place_bias():
+            sorted_rows = sbuf([P, P], F32, "bd_sorted")
+            nc.vector.tensor_copy(
+                out=sorted_rows[:].rearrange("p (t q u) -> p t q u", t=PACK, u=RUN),
+                in_=bd_rows[:].rearrange("p (q t u) -> p t q u", t=PACK, u=RUN))
+            placed = sbuf([P, P], F32, "bd_sb")
+            nc.vector.transpose(placed[:], sorted_rows[:])
+            return placed
+
         v_w, v2_w, v2_s = {}, {}, {}
         word_ps, sense_ps, word, gate, h_bf, h_codes, h_scales = {}, {}, {}, {}, {}, {}, {}
         dom_ps, y_ps, y, y_bf = {}, {}, {}, {}
@@ -234,7 +234,7 @@ def tile_list_crossword_clue_features_kernel(
             gate[g] = sbuf([P, 2, PACK, HALF], F32, "gate%d" % g)
             for t in range(PACK):
                 nc.vector.scalar_tensor_tensor(
-                    out=gate[g][:, :, t, :], in0=halves(dom_ps[g, t]), scalar=bd_sb[:, g, t : t + 1],
+                    out=gate[g][:, :, t, :], in0=halves(dom_ps[g, t]), scalar=bd_sb[:, 32 * t + g : 32 * t + g + 1],
                     in1=word[g][:, :, t, :], op0=ALU.add, op1=ALU.mult)
                 nc.scalar.activation(gate[g][:, :, t, :], gate[g][:, :, t, :], ACT.Tanh)
 
@@ -317,6 +317,7 @@ def tile_list_crossword_clue_features_kernel(
         v_w[1] = gather(tab_w[1][:], list1, U32, "v_w1")
         word_pass(0, 1)
         keep_word(0)
+        bd_sb = place_bias()
         w2_dealt_s = deal_w2(w2_s, U8, "w2_dealt_s")
         agreement(0)
 

@@ -23,17 +23,15 @@ QUADS = 4
 HALF = S // 2
 KIB = 1024
 
-ROUNDED_ON_VECTOR = {("w3", 0, 0): (1,), ("wo", 0, 1): (0, 1)}
-RUN = 8
+ROUNDED_ON_VECTOR = (("w1", 1, 0, 1), ("w3", 0, 1, 1), ("wo", 1, 0, 0), ("wo", 1, 0, 1))
+QUANTISED_IN_HALVES = (("w1", 1, 0), ("w3", 0, 1))
 
 SHARED = {
     "tab2_s": 0, "codes_w1_0_0": 0,
-    "tab2_w1": 4 * KIB, "codes_w1_0_1": 4 * KIB,
-    "bf_w1_1_1": 16 * KIB, "h_bf_0_0": 16 * KIB,
-    "bf_w3_0_1": 12 * KIB, "h_bf_0_1": 12 * KIB,
-    "raw_w3_0_1": 40 * KIB, "word1": 40 * KIB,
-    "bf_wo_1_0": 36 * KIB, "h_bf_1_1": 36 * KIB,
-    "tab_w0": 20 * KIB, "tab_w1": 28 * KIB, "raw_wo0": 20 * KIB,
+    "w2_s": 4 * KIB, "codes_w3_0_0": 4 * KIB,
+    "bf_w1_0_1": 8 * KIB, "h_bf_0_0": 8 * KIB,
+    "bf_w1_1_1": 12 * KIB, "bf_w3_0_1_1": 12 * KIB, "h_bf_0_1": 12 * KIB,
+    "bf_wo_1_1": 16 * KIB, "h_bf_1_1": 16 * KIB,
 }
 
 LOW, HIGH = (0, 1, 2, 3), (4, 5, 6, 7)
@@ -51,7 +49,7 @@ def tile_list_crossword_clue_features_kernel(
     with ExitStack() as ctx:
         lists = ctx.enter_context(tc.tile_pool(name="lists", bufs=1))
         keep = ctx.enter_context(tc.tile_pool(name="keep", bufs=1))
-        raws = ctx.enter_context(tc.tile_pool(name="raws", bufs=4))
+        raws = ctx.enter_context(tc.tile_pool(name="raws", bufs=6))
         bfs = ctx.enter_context(tc.tile_pool(name="bfs", bufs=3))
         shared = ctx.enter_context(tc.tile_pool(name="shared", bufs=1))
         psum = ctx.enter_context(tc.psum_pool(name="psum", bufs=1))
@@ -77,13 +75,12 @@ def tile_list_crossword_clue_features_kernel(
         w2_w = sbuf([P, 2, H], U16, "w2_w")
         w2_s = sbuf([P, 2, H], U8, "w2_s")
         go_sb = sbuf([P, 2, PACK], F32, "go_sb")
-        bd_rows = sbuf([P, P], F32, "bd_rows")
+        bd_sb = sbuf([P, 2, PACK], F32, "bd_sb")
 
         nc.vector.memset(tab3_s[:].bitcast(I32), 0)
         nc.vector.memset(tab_s[:].bitcast(I32), 0)
         nc.vector.memset(tab2_s[:].rearrange("p a c -> p (a c)").bitcast(I32), 0)
         nc.gpsimd.memset(w2_s[:].rearrange("p a c -> p (a c)").bitcast(I32), 0)
-        nc.gpsimd.memset(bd_rows[:], 0.0)
 
         raw = {}
 
@@ -96,14 +93,6 @@ def tile_list_crossword_clue_features_kernel(
             block = w[G * a : G * (a + 1), G * g : G * (g + 1)]
             nc.sync.dma_start(out=tile[:], in_=block.rearrange("(p j) c -> p j c", j=PACK))
             raw[name, a, g] = tile[:]
-
-        def load_wo(a):
-            tile = sbuf([P, PACK, N], F32, "raw_wo%d" % a)
-            rows = wo[G * a : G * (a + 1), :].rearrange("(q j u) c -> j q u c", j=PACK, u=RUN)
-            for j in range(PACK):
-                nc.sync.dma_start(out=tile[:, j, :], in_=rows[j])
-            for g in range(2):
-                raw["wo", a, g] = tile[:, :, G * g : G * (g + 1)]
 
         def load_words(dst, src, a):
             nc.sync.dma_start(out=dst[:].bitcast(I32), in_=src[a].rearrange("p c i -> p (c i)").bitcast(I32))
@@ -130,50 +119,52 @@ def tile_list_crossword_clue_features_kernel(
         load_weight("w1", w1, 0, 0)
         load_scales_side_by_side(tab2_s, tab2_scales)
         nc.sync.dma_start(list2[:], offs2)
-        load_weight("w1", w1, 1, 0)
         load_weight("w3", w3, 0, 0)
-        for g in range(2):
-            nc.sync.dma_start(
-                out=bd_rows[g : P : 32, :], in_=bd[G * g : G * (g + 1)].rearrange("(quad c) -> quad c", quad=QUADS))
-        load_words(tab_w[1], tab_words, 1)
         load_scales_side_by_side(w2_s, w2_scales)
-        load_weight("w1", w1, 0, 1)
+        load_weight("w1", w1, 1, 0)
+        nc.sync.dma_start(out=bd_sb[:], in_=bd.rearrange("(g p t) -> p g t", p=P, t=PACK))
+        load_words(tab_w[1], tab_words, 1)
         nc.sync.dma_start(out=w2_w[:].bitcast(I32), in_=w2_words.bitcast(I32).rearrange("a p c -> p a c"))
         for a in range(2):
             load_words(tab2_w[a], tab2_words, a)
-        load_weight("w1", w1, 1, 1)
+        for a in range(2):
+            load_weight("w1", w1, a, 1)
         load_weight("w3", w3, 0, 1)
         nc.sync.dma_start(out=go_sb[:], in_=go.rearrange("(g p t) -> p g t", p=P, t=PACK))
-        for a in range(2):
-            load_wo(a)
+        for g in range(2):
+            for a in range(2):
+                load_weight("wo", wo, a, g)
 
         rounded, codes, scales = {}, {}, {}
 
         def round_weight(*key):
-            own_name = "bf_%s_%d_%d" % key
-            if own_name in SHARED:
-                tile = sbuf([P, PACK * G], BF16, own_name)
+            name = "bf_%s_%d_%d" % key
+            if key in QUANTISED_IN_HALVES:
+                parts = [sbuf([P, 2 * G], BF16, "%s_%d" % (name, b))[:] for b in range(2)]
+                rounded[key] = parts
             else:
-                tile = bfs.tile([P, PACK * G], BF16, name="bf", align_bytes=64)
-            if key[0] == "wo":
-                dst = tile[:].rearrange("p (b e m j) -> p b m j e", b=2, e=2, j=PACK)
-                src = raw[key].rearrange("p j (m b e) -> p b m j e", b=2, e=2)
-                parts = [(b, dst[:, b], src[:, b]) for b in range(2)]
-            else:
-                dst = tile[:].rearrange("p (t q c i j) -> p t q c j i", t=PACK, c=RUN // 2, i=2, j=PACK)
-                src = raw[key].rearrange("p j (q t c i) -> p t q c j i", t=PACK, c=RUN // 2, i=2)
-                parts = [(t // 2, dst[:, t], src[:, t]) for t in range(PACK)]
-            for b, part_dst, part_src in parts:
-                if b in ROUNDED_ON_VECTOR.get(key, ()):
-                    nc.vector.tensor_copy(out=part_dst, in_=part_src)
+                if name in SHARED:
+                    tile = sbuf([P, PACK * G], BF16, name)
                 else:
-                    nc.scalar.copy(out=part_dst, in_=part_src)
-            rounded[key] = tile
+                    tile = bfs.tile([P, PACK * G], BF16, name="bf", align_bytes=64)
+                parts = [tile[:, 2 * G * b : 2 * G * (b + 1)] for b in range(2)]
+                rounded[key] = [tile[:]]
+            src = raw[key].rearrange("p j (m b e) -> p b m j e", b=2, e=2)
+            for b in range(2):
+                dst = parts[b].rearrange("p (e m j) -> p m j e", e=2, j=PACK)
+                if key + (b,) in ROUNDED_ON_VECTOR:
+                    nc.vector.tensor_copy(out=dst, in_=src[:, b])
+                else:
+                    nc.scalar.copy(out=dst, in_=src[:, b])
 
         def quantise_weight(*key):
             codes[key] = sbuf([P, G], U32, "codes_%s_%d_%d" % key)
             scales[key] = sbuf([P, G], U8, "scales_%s_%d_%d" % key)
-            nc.vector.quantize_mx(out=codes[key][:].bitcast(FP8X4), scales=scales[key][:], in_=rounded[key][:])
+            width = G // len(rounded[key])
+            for b, part in enumerate(rounded[key]):
+                cols = slice(width * b, width * (b + 1))
+                nc.vector.quantize_mx(
+                    out=codes[key][:, cols].bitcast(FP8X4), scales=scales[key][:, cols], in_=part)
 
         def gather(window, offsets, dtype, name):
             dst = sbuf([P, S], dtype, name)
@@ -183,20 +174,9 @@ def tile_list_crossword_clue_features_kernel(
         def deal_w2(src, dtype, name):
             dst = sbuf([P, 2, 2, PACK, P], dtype, name)
             nc.vector.tensor_copy(
-                out=dst[:].rearrange("p a g t m -> p (a g t m)").bitcast(I32).rearrange(
-                    "p (x t q w) -> p x t q w", x=4, t=PACK, q=P // RUN),
-                in_=src[:].rearrange("p a c -> p (a c)").bitcast(I32).rearrange(
-                    "p (x q t w) -> p x t q w", x=4, t=PACK, q=P // RUN))
+                out=dst[:].rearrange("p a g t m -> p (a g) t m"),
+                in_=src[:].rearrange("p a (g m t) -> p (a g) t m", g=2, t=PACK))
             return dst
-
-        def place_bias():
-            sorted_rows = sbuf([P, P], F32, "bd_sorted")
-            nc.vector.tensor_copy(
-                out=sorted_rows[:].rearrange("p (t q u) -> p t q u", t=PACK, u=RUN),
-                in_=bd_rows[:].rearrange("p (q t u) -> p t q u", t=PACK, u=RUN))
-            placed = sbuf([P, P], F32, "bd_sb")
-            nc.vector.transpose(placed[:], sorted_rows[:])
-            return placed
 
         v_w, v2_w, v2_s = {}, {}, {}
         word_ps, sense_ps, word, gate, h_bf, h_codes, h_scales = {}, {}, {}, {}, {}, {}, {}
@@ -234,7 +214,7 @@ def tile_list_crossword_clue_features_kernel(
             gate[g] = sbuf([P, 2, PACK, HALF], F32, "gate%d" % g)
             for t in range(PACK):
                 nc.vector.scalar_tensor_tensor(
-                    out=gate[g][:, :, t, :], in0=halves(dom_ps[g, t]), scalar=bd_sb[:, 32 * t + g : 32 * t + g + 1],
+                    out=gate[g][:, :, t, :], in0=halves(dom_ps[g, t]), scalar=bd_sb[:, g, t : t + 1],
                     in1=word[g][:, :, t, :], op0=ALU.add, op1=ALU.mult)
                 nc.scalar.activation(gate[g][:, :, t, :], gate[g][:, :, t, :], ACT.Tanh)
 
@@ -309,31 +289,28 @@ def tile_list_crossword_clue_features_kernel(
             v2_s[a] = gather(tab2_s[:, a, :], list2, U8, "v2_s%d" % a)
         quantise_weight("w1", 0, 0)
         word_pass(0, 0)
-        round_weight("w1", 1, 0)
-        quantise_weight("w1", 1, 0)
         round_weight("w3", 0, 0)
+        w2_dealt_s = deal_w2(w2_s, U8, "w2_dealt_s")
         quantise_weight("w3", 0, 0)
         domain(0)
+        round_weight("w1", 1, 0)
+        quantise_weight("w1", 1, 0)
         v_w[1] = gather(tab_w[1][:], list1, U32, "v_w1")
         word_pass(0, 1)
         keep_word(0)
-        bd_sb = place_bias()
-        w2_dealt_s = deal_w2(w2_s, U8, "w2_dealt_s")
+        w2_dealt_w = deal_w2(w2_w, U16, "w2_dealt_w")
         agreement(0)
 
-        round_weight("w1", 0, 1)
-        w2_dealt_w = deal_w2(w2_w, U16, "w2_dealt_w")
         for a in range(2):
             v2_w[a] = gather(tab2_w[a][:], list2, U32, "v2_w%d" % a)
             sense_pass(0, a)
-        quantise_weight("w1", 0, 1)
-        word_pass(1, 0)
         gated_sense(0, slice(0, 2))
-        round_weight("w1", 1, 1)
-        quantise_weight("w1", 1, 1)
-        word_pass(1, 1)
-        keep_word(1)
+        for a in range(2):
+            round_weight("w1", a, 1)
+            quantise_weight("w1", a, 1)
+            word_pass(1, a)
         round_weight("w3", 0, 1)
+        keep_word(1)
         quantise_weight("w3", 0, 1)
         domain(1)
         agreement(1)
@@ -342,29 +319,24 @@ def tile_list_crossword_clue_features_kernel(
         for half in range(2):
             finish_h(0, half)
             quantise_h(0, half)
-        for a in range(2):
-            round_weight("wo", a, 0)
-            quantise_weight("wo", a, 0)
+        for g in range(2):
+            for a in range(2):
+                round_weight("wo", a, g)
+                quantise_weight("wo", a, g)
 
         for half in range(2):
             gated_sense(1, slice(half, half + 1))
-            for pair in range(2):
-                out_pass(half, 0, pair, 0)
+            for g in range(2):
+                for pair in range(2):
+                    out_pass(half, g, pair, 0)
             finish_h(1, half)
             quantise_h(1, half)
-            for pair in range(2):
-                out_pass(half, 0, pair, 1)
-            round_weight("wo", half, 1)
-            quantise_weight("wo", half, 1)
-            gain_and_store(half, 0)
-
-        for half in range(2):
-            for a in range(2):
+            for g in range(2):
                 for pair in range(2):
-                    out_pass(half, 1, pair, a)
-            gain_and_store(half, 1)
-        for g in range(2):
-            for half in range(2):
+                    out_pass(half, g, pair, 1)
+                gain_and_store(half, g)
+        for half in range(2):
+            for g in range(2):
                 quantise_y(half, g)
         for quad in range(QUADS):
             nc.sync.dma_start(

@@ -71,13 +71,13 @@ def tile_list_crossword_clue_features_kernel(
         tab3_w = sbuf([P, T3], U16, "tab3_w")
         tab_s = sbuf([P, T], U8, "tab_s")
         tab2_s = sbuf([P, 2, T2], U8, "tab2_s")
-        tab3_s = sbuf([P, T3], U8, "tab3_s")
+        tab3_s = sbuf([P, 1, T3], U8, "tab3_s")
         w2_w = sbuf([P, 2, H], U16, "w2_w")
         w2_s = sbuf([P, 2, H], U8, "w2_s")
         go_sb = sbuf([P, 2, PACK], F32, "go_sb")
         bd_sb = sbuf([P, 2, PACK], F32, "bd_sb")
 
-        nc.vector.memset(tab3_s[:].bitcast(I32), 0)
+        nc.vector.memset(tab3_s[:, 0, :].bitcast(I32), 0)
         nc.vector.memset(tab_s[:].bitcast(I32), 0)
         nc.vector.memset(tab2_s[:].rearrange("p a c -> p (a c)").bitcast(I32), 0)
         nc.gpsimd.memset(w2_s[:].rearrange("p a c -> p (a c)").bitcast(I32), 0)
@@ -98,21 +98,19 @@ def tile_list_crossword_clue_features_kernel(
             nc.sync.dma_start(out=dst[:].bitcast(I32), in_=src[a].rearrange("p c i -> p (c i)").bitcast(I32))
 
         def load_scales_stacked(dst, src):
-            passes = src.shape[0]
             for quad in range(QUADS):
                 nc.sync.dma_start(
-                    out=dst[32 * quad : 32 * quad + 4 * passes, :].bitcast(I32),
+                    out=dst[32 * quad : 32 * quad + 8, :].bitcast(I32),
                     in_=src[:, 4 * quad : 4 * quad + 4, :].bitcast(I32))
 
         def load_scales_side_by_side(dst, src):
-            for quad in range(QUADS):
-                nc.sync.dma_start(
-                    out=dst[32 * quad : 32 * quad + 4].bitcast(I32),
-                    in_=src[:, 4 * quad : 4 * quad + 4, :].bitcast(I32).rearrange("a r c -> r a c"))
+            rows = src.bitcast(I32).rearrange("a (quad c) w -> c quad a w", c=4)
+            for c in range(4):
+                nc.sync.dma_start(out=dst[c:P:32].bitcast(I32), in_=rows[c])
 
         nc.sync.dma_start(list3[:], offs3)
         nc.sync.dma_start(out=tab3_w[:].bitcast(I32), in_=tab3_words[0].bitcast(I32))
-        load_scales_stacked(tab3_s, tab3_scales)
+        load_scales_side_by_side(tab3_s, tab3_scales)
         nc.sync.dma_start(list1[:], offs)
         load_words(tab_w[0], tab_words, 0)
         load_scales_stacked(tab_s, tab_scales)
@@ -281,7 +279,7 @@ def tile_list_crossword_clue_features_kernel(
                 in_=y_codes[:].bitcast(I32))
 
         v3_w = gather(tab3_w[:], list3, U16, "v3_w")
-        v3_s = gather(tab3_s[:], list3, U8, "v3_s")
+        v3_s = gather(tab3_s[:, 0, :], list3, U8, "v3_s")
         v_w[0] = gather(tab_w[0][:], list1, U32, "v_w0")
         v_s = gather(tab_s[:], list1, U8, "v_s")
         round_weight("w1", 0, 0)
@@ -338,7 +336,6 @@ def tile_list_crossword_clue_features_kernel(
         for half in range(2):
             for g in range(2):
                 quantise_y(half, g)
-        for quad in range(QUADS):
-            nc.sync.dma_start(
-                out=out_2[:, 4 * quad : 4 * quad + 4, :].bitcast(I32).rearrange("g r m -> r g m"),
-                in_=y_scales[32 * quad : 32 * quad + 4].bitcast(I32))
+        rows = out_2.bitcast(I32).rearrange("g (quad c) w -> c quad g w", c=4)
+        for c in range(4):
+            nc.sync.dma_start(out=rows[c], in_=y_scales[c:P:32].bitcast(I32))

@@ -23,8 +23,9 @@ QUADS = 4
 HALF = S // 2
 KIB = 1024
 
-ROUNDED_ON_VECTOR = (("w1", 1, 0, 1), ("w3", 0, 1, 1), ("wo", 1, 0, 0), ("wo", 1, 0, 1))
+ROUNDED_ON_VECTOR = ("wo", 1, 0)
 QUANTISED_IN_HALVES = (("w1", 1, 0), ("w3", 0, 1))
+ROUNDED_ROUND_THE_TANH = ("wo", 0, 0)
 
 SHARED = {
     "tab2_s": 0, "codes_w1_0_0": 0,
@@ -137,23 +138,25 @@ def tile_list_crossword_clue_features_kernel(
 
         def round_weight(*key):
             name = "bf_%s_%d_%d" % key
+            src = raw[key].rearrange("p j (m b e) -> p b m j e", b=2, e=2)
             if key in QUANTISED_IN_HALVES:
-                parts = [sbuf([P, 2 * G], BF16, "%s_%d" % (name, b))[:] for b in range(2)]
-                rounded[key] = parts
+                tiles = [sbuf([P, 2 * G], BF16, "%s_%d" % (name, b)) for b in range(2)]
+                nc.scalar.copy(out=tiles[0][:].rearrange("p (e m j) -> p m j e", e=2, j=PACK), in_=src[:, 0])
+                nc.vector.tensor_copy(out=tiles[1][:].rearrange("p (e m j) -> p m j e", e=2, j=PACK), in_=src[:, 1])
             else:
                 if name in SHARED:
-                    tile = sbuf([P, PACK * G], BF16, name)
+                    tiles = [sbuf([P, PACK * G], BF16, name)]
                 else:
-                    tile = bfs.tile([P, PACK * G], BF16, name="bf", align_bytes=64)
-                parts = [tile[:, 2 * G * b : 2 * G * (b + 1)] for b in range(2)]
-                rounded[key] = [tile[:]]
-            src = raw[key].rearrange("p j (m b e) -> p b m j e", b=2, e=2)
-            for b in range(2):
-                dst = parts[b].rearrange("p (e m j) -> p m j e", e=2, j=PACK)
-                if key + (b,) in ROUNDED_ON_VECTOR:
-                    nc.vector.tensor_copy(out=dst, in_=src[:, b])
+                    tiles = [bfs.tile([P, PACK * G], BF16, name="bf", align_bytes=64)]
+                dst = tiles[0][:].rearrange("p (b e m j) -> p b m j e", b=2, e=2, j=PACK)
+                if key == ROUNDED_ON_VECTOR:
+                    nc.vector.tensor_copy(out=dst, in_=src)
+                elif key == ROUNDED_ROUND_THE_TANH:
+                    for b in range(2):
+                        nc.scalar.copy(out=dst[:, b], in_=src[:, b])
                 else:
-                    nc.scalar.copy(out=dst, in_=src[:, b])
+                    nc.scalar.copy(out=dst, in_=src)
+            rounded[key] = [tile[:] for tile in tiles]
 
         def quantise_weight(*key):
             codes[key] = sbuf([P, G], U32, "codes_%s_%d_%d" % key)
@@ -297,11 +300,12 @@ def tile_list_crossword_clue_features_kernel(
         word_pass(0, 1)
         keep_word(0)
         w2_dealt_w = deal_w2(w2_w, U16, "w2_dealt_w")
+        v2_w[0] = gather(tab2_w[0][:], list2, U32, "v2_w0")
         agreement(0)
 
-        for a in range(2):
-            v2_w[a] = gather(tab2_w[a][:], list2, U32, "v2_w%d" % a)
-            sense_pass(0, a)
+        sense_pass(0, 0)
+        v2_w[1] = gather(tab2_w[1][:], list2, U32, "v2_w1")
+        sense_pass(0, 1)
         gated_sense(0, slice(0, 2))
         for a in range(2):
             round_weight("w1", a, 1)

@@ -29,7 +29,7 @@ ROUNDED_ROUND_THE_TANH = ("wo", 0, 0)
 
 SHARED = {
     "tab2_s": 0, "codes_w1_0_0": 0,
-    "w2_s": 4 * KIB, "codes_w3_0_0": 4 * KIB,
+    "w2_s": 4 * KIB,
     "bf_w1_0_1": 8 * KIB, "h_bf_0_0": 8 * KIB,
     "bf_w1_1_1": 12 * KIB, "bf_w3_0_1_1": 12 * KIB, "h_bf_0_1": 12 * KIB,
     "bf_wo_1_1": 16 * KIB, "h_bf_1_1": 16 * KIB,
@@ -50,7 +50,7 @@ def tile_list_crossword_clue_features_kernel(
     with ExitStack() as ctx:
         lists = ctx.enter_context(tc.tile_pool(name="lists", bufs=1))
         keep = ctx.enter_context(tc.tile_pool(name="keep", bufs=1))
-        raws = ctx.enter_context(tc.tile_pool(name="raws", bufs=6))
+        raws = ctx.enter_context(tc.tile_pool(name="raws", bufs=5))
         bfs = ctx.enter_context(tc.tile_pool(name="bfs", bufs=3))
         shared = ctx.enter_context(tc.tile_pool(name="shared", bufs=1))
         psum = ctx.enter_context(tc.psum_pool(name="psum", bufs=1))
@@ -70,7 +70,7 @@ def tile_list_crossword_clue_features_kernel(
         tab_w = [sbuf([P, T], U32, "tab_w%d" % a) for a in range(2)]
         tab2_w = [sbuf([P, T2], U32, "tab2_w%d" % a) for a in range(2)]
         tab3_w = sbuf([P, T3], U16, "tab3_w")
-        tab_s = sbuf([P, T], U8, "tab_s")
+        tab_s = sbuf([P, 1, T], U8, "tab_s")
         tab2_s = sbuf([P, 2, T2], U8, "tab2_s")
         tab3_s = sbuf([P, 1, T3], U8, "tab3_s")
         w2_w = sbuf([P, 2, H], U16, "w2_w")
@@ -78,8 +78,8 @@ def tile_list_crossword_clue_features_kernel(
         go_sb = sbuf([P, 2, PACK], F32, "go_sb")
         bd_sb = sbuf([P, 2, PACK], F32, "bd_sb")
 
-        nc.vector.memset(tab3_s[:, 0, :].bitcast(I32), 0)
-        nc.vector.memset(tab_s[:].bitcast(I32), 0)
+        nc.gpsimd.memset(tab3_s[:, 0, :].bitcast(I32), 0)
+        nc.vector.memset(tab_s[:, 0, :].bitcast(I32), 0)
         nc.vector.memset(tab2_s[:].rearrange("p a c -> p (a c)").bitcast(I32), 0)
         nc.gpsimd.memset(w2_s[:].rearrange("p a c -> p (a c)").bitcast(I32), 0)
 
@@ -98,34 +98,65 @@ def tile_list_crossword_clue_features_kernel(
         def load_words(dst, src, a):
             nc.sync.dma_start(out=dst[:].bitcast(I32), in_=src[a].rearrange("p c i -> p (c i)").bitcast(I32))
 
-        def load_scales_stacked(dst, src):
-            for quad in range(QUADS):
+        def load_scales_spread(dst, src, first):
+            nc.sync.dma_start(out=dst[first:P:8].bitcast(I32), in_=src.bitcast(I32).rearrange("a q w -> q a w"))
+
+        picked, plane = {}, {}
+
+        def pick_scales(name, window, offsets, passes):
+            picked[name] = sbuf([P, passes, S], U8, "picked_" + name)
+            plane[name] = sbuf([P, passes, S], U8, "plane_" + name)
+            for a in range(passes):
+                nc.vector.tensor_copy(picked[name][:, a, :], window[:, a, :].indirect(offsets[:]))
+            nc.vector.tensor_copy(
+                out=plane[name][:].rearrange("p a c -> p (a c)").bitcast(I32),
+                in_=picked[name][:].rearrange("p a c -> p (a c)").bitcast(I32))
+
+        def place_scales(name, first):
+            for c in range(1, 4):
                 nc.sync.dma_start(
-                    out=dst[32 * quad : 32 * quad + 8, :].bitcast(I32),
-                    in_=src[:, 4 * quad : 4 * quad + 4, :].bitcast(I32))
+                    out=plane[name][first + c : P : 32].rearrange("p a c -> p (a c)").bitcast(I32),
+                    in_=picked[name][first + 8 * c : P : 32].rearrange("p a c -> p (a c)").bitcast(I32))
+
+        def gather(window, offsets, dtype, name):
+            dst = sbuf([P, S], dtype, name)
+            nc.vector.tensor_copy(dst[:], window.indirect(offsets[:]))
+            return dst
+
+        v_w = {}
 
         def load_scales_side_by_side(dst, src):
             rows = src.bitcast(I32).rearrange("a (quad c) w -> c quad a w", c=4)
             for c in range(4):
                 nc.sync.dma_start(out=dst[c:P:32].bitcast(I32), in_=rows[c])
 
+        nc.sync.dma_start(list1[:], offs)
         nc.sync.dma_start(list3[:], offs3)
         nc.sync.dma_start(out=tab3_w[:].bitcast(I32), in_=tab3_words[0].bitcast(I32))
-        load_scales_side_by_side(tab3_s, tab3_scales)
-        nc.sync.dma_start(list1[:], offs)
-        load_words(tab_w[0], tab_words, 0)
-        load_scales_stacked(tab_s, tab_scales)
-        load_weight("w1", w1, 0, 0)
-        load_scales_side_by_side(tab2_s, tab2_scales)
-        nc.sync.dma_start(list2[:], offs2)
-        load_weight("w3", w3, 0, 0)
-        load_scales_side_by_side(w2_s, w2_scales)
-        load_weight("w1", w1, 1, 0)
-        nc.sync.dma_start(out=bd_sb[:], in_=bd.rearrange("(g p t) -> p g t", p=P, t=PACK))
-        load_words(tab_w[1], tab_words, 1)
-        nc.sync.dma_start(out=w2_w[:].bitcast(I32), in_=w2_words.bitcast(I32).rearrange("a p c -> p a c"))
         for a in range(2):
-            load_words(tab2_w[a], tab2_words, a)
+            load_scales_spread(tab_s, tab_scales[a : a + 1], 4 * a)
+        load_scales_spread(tab3_s, tab3_scales, 0)
+        load_words(tab_w[0], tab_words, 0)
+        load_weight("w1", w1, 0, 0)
+        nc.sync.dma_start(list2[:], offs2)
+        load_scales_spread(tab2_s, tab2_scales, 0)
+        load_scales_side_by_side(w2_s, w2_scales)
+        load_weight("w3", w3, 0, 0)
+        v3_w = gather(tab3_w[:], list3, U16, "v3_w")
+        pick_scales("tab", tab_s, list1, 1)
+        place_scales("tab", 0)
+        place_scales("tab", 4)
+        load_weight("w1", w1, 1, 0)
+        pick_scales("tab3", tab3_s, list3, 1)
+        place_scales("tab3", 0)
+        v_w[0] = gather(tab_w[0][:], list1, U32, "v_w0")
+        load_words(tab_w[1], tab_words, 1)
+        nc.sync.dma_start(out=bd_sb[:], in_=bd.rearrange("(g p t) -> p g t", p=P, t=PACK))
+        nc.sync.dma_start(out=w2_w[:].bitcast(I32), in_=w2_words.bitcast(I32).rearrange("a p c -> p a c"))
+        load_words(tab2_w[0], tab2_words, 0)
+        pick_scales("tab2", tab2_s, list2, 2)
+        place_scales("tab2", 0)
+        load_words(tab2_w[1], tab2_words, 1)
         for a in range(2):
             load_weight("w1", w1, a, 1)
         load_weight("w3", w3, 0, 1)
@@ -167,11 +198,6 @@ def tile_list_crossword_clue_features_kernel(
                 nc.vector.quantize_mx(
                     out=codes[key][:, cols].bitcast(FP8X4), scales=scales[key][:, cols], in_=part)
 
-        def gather(window, offsets, dtype, name):
-            dst = sbuf([P, S], dtype, name)
-            nc.vector.tensor_copy(dst[:], window.indirect(offsets[:]))
-            return dst
-
         def deal_w2(src, dtype, name):
             dst = sbuf([P, 2, 2, PACK, P], dtype, name)
             nc.vector.tensor_copy(
@@ -179,7 +205,7 @@ def tile_list_crossword_clue_features_kernel(
                 in_=src[:].rearrange("p a (g m t) -> p (a g) t m", g=2, t=PACK))
             return dst
 
-        v_w, v2_w, v2_s = {}, {}, {}
+        v2_w = {}
         word_ps, sense_ps, word, gate, h_bf, h_codes, h_scales = {}, {}, {}, {}, {}, {}, {}
         dom_ps, y_ps, y, y_bf = {}, {}, {}, {}
         y_scales = sbuf([P, 2, S], U8, "y_scales")
@@ -195,7 +221,7 @@ def tile_list_crossword_clue_features_kernel(
                 nc.tensor.matmul_mx(
                     out=word_ps[g, t][:],
                     lhsT=codes["w1", a, g][:, cols].bitcast(FP8X4), lhsT_scale=scales["w1", a, g][:, cols],
-                    rhs=v_w[a][:].bitcast(FP8X4), rhs_scale=v_s[4 * a :, :], start=(a == 0), stop=(a == 1))
+                    rhs=v_w[a][:].bitcast(FP8X4), rhs_scale=plane["tab"][4 * a :, 0, :], start=(a == 0), stop=(a == 1))
 
         def keep_word(g):
             word[g] = sbuf([P, 2, PACK, HALF], F32, "word%d" % g)
@@ -209,7 +235,7 @@ def tile_list_crossword_clue_features_kernel(
                 nc.tensor.matmul_mx(
                     out=dom_ps[g, t][:], lhsT=codes["w3", 0, g][:, cols].bitcast(FP8X4),
                     lhsT_scale=scales["w3", 0, g][:, cols],
-                    rhs=v3_w[:].bitcast(FP4X4), rhs_scale=v3_s[:], start=True, stop=True)
+                    rhs=v3_w[:].bitcast(FP4X4), rhs_scale=plane["tab3"][:, 0, :], start=True, stop=True)
 
         def agreement(g):
             gate[g] = sbuf([P, 2, PACK, HALF], F32, "gate%d" % g)
@@ -226,7 +252,7 @@ def tile_list_crossword_clue_features_kernel(
                 nc.tensor.matmul_mx(
                     out=sense_ps[g, t][:],
                     lhsT=w2_dealt_w[:, a, g, t, :].bitcast(FP4X4), lhsT_scale=w2_dealt_s[:, a, g, t, :],
-                    rhs=v2_w[a][:].bitcast(FP8X4), rhs_scale=v2_s[a][:], start=(a == 0), stop=(a == 1))
+                    rhs=v2_w[a][:].bitcast(FP8X4), rhs_scale=plane["tab2"][:, a, :], start=(a == 0), stop=(a == 1))
 
         def gated_sense(g, part):
             for t in range(PACK):
@@ -281,13 +307,7 @@ def tile_list_crossword_clue_features_kernel(
                 out=out_1[g, :, slots, :].rearrange("p m t -> p (m t)").bitcast(I32),
                 in_=y_codes[:].bitcast(I32))
 
-        v3_w = gather(tab3_w[:], list3, U16, "v3_w")
-        v3_s = gather(tab3_s[:, 0, :], list3, U8, "v3_s")
-        v_w[0] = gather(tab_w[0][:], list1, U32, "v_w0")
-        v_s = gather(tab_s[:], list1, U8, "v_s")
         round_weight("w1", 0, 0)
-        for a in range(2):
-            v2_s[a] = gather(tab2_s[:, a, :], list2, U8, "v2_s%d" % a)
         quantise_weight("w1", 0, 0)
         word_pass(0, 0)
         round_weight("w3", 0, 0)

@@ -23,16 +23,17 @@ QUADS = 4
 HALF = S // 2
 KIB = 1024
 
-ROUNDED_ON_VECTOR = ("wo", 1, 0)
+ROUNDED_ON_GPSIMD = ("wo", 0, 0)
 QUANTISED_IN_HALVES = (("w1", 1, 0), ("w3", 0, 1))
-ROUNDED_ROUND_THE_TANH = ("wo", 0, 0)
 
 SHARED = {
-    "tab2_s": 0, "codes_w1_0_0": 0,
-    "w2_s": 4 * KIB,
+    "word0": 0, "bf_wo_0_0": 0, "taken_1_0": 0,
     "bf_w1_0_1": 8 * KIB, "h_bf_0_0": 8 * KIB,
     "bf_w1_1_1": 12 * KIB, "bf_w3_0_1_1": 12 * KIB, "h_bf_0_1": 12 * KIB,
-    "bf_wo_1_1": 16 * KIB, "h_bf_1_1": 16 * KIB,
+    "bf_wo_1_0": 16 * KIB, "taken_1_1": 16 * KIB,
+    "w2_w": 20 * KIB, "gate_0_0": 20 * KIB, "gate_0_1": 22 * KIB,
+    "tab2_w0": 24 * KIB, "gate_0_2": 24 * KIB, "gate_0_3": 26 * KIB,
+    "tab_w0": 32 * KIB, "taken_0": 32 * KIB,
 }
 
 LOW, HIGH = (0, 1, 2, 3), (4, 5, 6, 7)
@@ -70,18 +71,22 @@ def tile_list_crossword_clue_features_kernel(
         tab_w = [sbuf([P, T], U32, "tab_w%d" % a) for a in range(2)]
         tab2_w = [sbuf([P, T2], U32, "tab2_w%d" % a) for a in range(2)]
         tab3_w = sbuf([P, T3], U16, "tab3_w")
-        tab_s = sbuf([P, 1, T], U8, "tab_s")
-        tab2_s = sbuf([P, 2, T2], U8, "tab2_s")
-        tab3_s = sbuf([P, 1, T3], U8, "tab3_s")
+        tab_s = sbuf([P, T], U8, "tab_s")
+        tab2_s = sbuf([P, T2], U8, "tab2_s")
+        tab3_s = sbuf([P, T3], U8, "tab3_s")
+        tab_plane = sbuf([P, S], U8, "tab_plane")
+        tab2_plane = [sbuf([P, S], U8, "tab2_plane%d" % a) for a in range(2)]
+        tab3_plane = sbuf([P, S], U8, "tab3_plane")
         w2_w = sbuf([P, 2, H], U16, "w2_w")
         w2_s = sbuf([P, 2, H], U8, "w2_s")
         go_sb = sbuf([P, 2, PACK], F32, "go_sb")
         bd_sb = sbuf([P, 2, PACK], F32, "bd_sb")
 
-        nc.gpsimd.memset(tab3_s[:, 0, :].bitcast(I32), 0)
-        nc.vector.memset(tab_s[:, 0, :].bitcast(I32), 0)
-        nc.vector.memset(tab2_s[:].rearrange("p a c -> p (a c)").bitcast(I32), 0)
+        nc.gpsimd.memset(tab_s[:].bitcast(I32), 0)
+        nc.gpsimd.memset(tab3_s[:].bitcast(I32), 0)
+        nc.vector.memset(tab2_s[:].bitcast(I32), 0)
         nc.gpsimd.memset(w2_s[:].rearrange("p a c -> p (a c)").bitcast(I32), 0)
+        nc.gpsimd.memset(tab2_plane[1][:].bitcast(I32), 0)
 
         raw = {}
 
@@ -98,25 +103,21 @@ def tile_list_crossword_clue_features_kernel(
         def load_words(dst, src, a):
             nc.sync.dma_start(out=dst[:].bitcast(I32), in_=src[a].rearrange("p c i -> p (c i)").bitcast(I32))
 
-        def load_scales_spread(dst, src, first):
-            nc.sync.dma_start(out=dst[first:P:8].bitcast(I32), in_=src.bitcast(I32).rearrange("a q w -> q a w"))
+        def load_scales_spread(dst, src):
+            for a in range(src.shape[0]):
+                nc.sync.dma_start(out=dst[4 * a : P : 8, :].bitcast(I32), in_=src[a].bitcast(I32))
 
-        picked, plane = {}, {}
+        picked = {}
 
-        def pick_scales(name, window, offsets, passes):
-            picked[name] = sbuf([P, passes, S], U8, "picked_" + name)
-            plane[name] = sbuf([P, passes, S], U8, "plane_" + name)
-            for a in range(passes):
-                nc.vector.tensor_copy(picked[name][:, a, :], window[:, a, :].indirect(offsets[:]))
-            nc.vector.tensor_copy(
-                out=plane[name][:].rearrange("p a c -> p (a c)").bitcast(I32),
-                in_=picked[name][:].rearrange("p a c -> p (a c)").bitcast(I32))
+        def pick_scales(name, window, offsets, plane):
+            picked[name] = gather(window[:], offsets, U8, "picked_" + name)
+            nc.vector.tensor_copy(out=plane.bitcast(I32), in_=picked[name][:].bitcast(I32))
 
-        def place_scales(name, first):
-            for c in range(1, 4):
+        def place_scales(name, a, rows, plane, first):
+            for c in rows:
                 nc.sync.dma_start(
-                    out=plane[name][first + c : P : 32].rearrange("p a c -> p (a c)").bitcast(I32),
-                    in_=picked[name][first + 8 * c : P : 32].rearrange("p a c -> p (a c)").bitcast(I32))
+                    out=plane[first + c : P : 32, :].bitcast(I32),
+                    in_=picked[name][8 * c + 4 * a : P : 32, :].bitcast(I32))
 
         def gather(window, offsets, dtype, name):
             dst = sbuf([P, S], dtype, name)
@@ -125,37 +126,37 @@ def tile_list_crossword_clue_features_kernel(
 
         v_w = {}
 
-        def load_scales_side_by_side(dst, src):
+        def load_scales_side_by_side(dst, src, which):
             rows = src.bitcast(I32).rearrange("a (quad c) w -> c quad a w", c=4)
-            for c in range(4):
+            for c in which:
                 nc.sync.dma_start(out=dst[c:P:32].bitcast(I32), in_=rows[c])
 
         nc.sync.dma_start(list1[:], offs)
         nc.sync.dma_start(list3[:], offs3)
+        load_scales_spread(tab_s, tab_scales)
         nc.sync.dma_start(out=tab3_w[:].bitcast(I32), in_=tab3_words[0].bitcast(I32))
-        for a in range(2):
-            load_scales_spread(tab_s, tab_scales[a : a + 1], 4 * a)
-        load_scales_spread(tab3_s, tab3_scales, 0)
-        load_words(tab_w[0], tab_words, 0)
-        load_weight("w1", w1, 0, 0)
+        load_scales_spread(tab3_s, tab3_scales)
         nc.sync.dma_start(list2[:], offs2)
-        load_scales_spread(tab2_s, tab2_scales, 0)
-        load_scales_side_by_side(w2_s, w2_scales)
-        load_weight("w3", w3, 0, 0)
+        load_weight("w1", w1, 0, 0)
+        load_scales_spread(tab2_s, tab2_scales)
+        load_scales_side_by_side(w2_s, w2_scales, (0, 1))
+        load_words(tab_w[0], tab_words, 0)
+        load_scales_side_by_side(w2_s, w2_scales, (2, 3))
+        pick_scales("tab", tab_s, list1, tab_plane[:])
         v3_w = gather(tab3_w[:], list3, U16, "v3_w")
-        pick_scales("tab", tab_s, list1, 1)
-        place_scales("tab", 0)
-        place_scales("tab", 4)
+        place_scales("tab", 0, (1, 2, 3), tab_plane, 0)
+        load_weight("w3", w3, 0, 0)
+        place_scales("tab", 1, (1, 2, 3), tab_plane, 4)
         load_weight("w1", w1, 1, 0)
-        pick_scales("tab3", tab3_s, list3, 1)
-        place_scales("tab3", 0)
-        v_w[0] = gather(tab_w[0][:], list1, U32, "v_w0")
+        pick_scales("tab3", tab3_s, list3, tab3_plane[:])
+        place_scales("tab3", 0, (1, 2, 3), tab3_plane, 0)
         load_words(tab_w[1], tab_words, 1)
         nc.sync.dma_start(out=bd_sb[:], in_=bd.rearrange("(g p t) -> p g t", p=P, t=PACK))
         nc.sync.dma_start(out=w2_w[:].bitcast(I32), in_=w2_words.bitcast(I32).rearrange("a p c -> p a c"))
+        pick_scales("tab2", tab2_s, list2, tab2_plane[0][:])
+        place_scales("tab2", 0, (1, 2, 3), tab2_plane[0], 0)
         load_words(tab2_w[0], tab2_words, 0)
-        pick_scales("tab2", tab2_s, list2, 2)
-        place_scales("tab2", 0)
+        place_scales("tab2", 1, (0, 1, 2, 3), tab2_plane[1], 0)
         load_words(tab2_w[1], tab2_words, 1)
         for a in range(2):
             load_weight("w1", w1, a, 1)
@@ -180,11 +181,13 @@ def tile_list_crossword_clue_features_kernel(
                 else:
                     tiles = [bfs.tile([P, PACK * G], BF16, name="bf", align_bytes=64)]
                 dst = tiles[0][:].rearrange("p (b e m j) -> p b m j e", b=2, e=2, j=PACK)
-                if key == ROUNDED_ON_VECTOR:
-                    nc.vector.tensor_copy(out=dst, in_=src)
-                elif key == ROUNDED_ROUND_THE_TANH:
+                if key == ROUNDED_ON_GPSIMD:
+                    by_slice = tiles[0][:].rearrange("p (t m j) -> p t m j", t=PACK, j=PACK)
+                    columns = raw[key].rearrange("p j (m t) -> p t m j", t=PACK)
                     for b in range(2):
-                        nc.scalar.copy(out=dst[:, b], in_=src[:, b])
+                        nc.gpsimd.tensor_scalar(
+                            out=by_slice[:, 2 * b : 2 * b + 2], in0=columns[:, 2 * b : 2 * b + 2],
+                            scalar1=1.0, scalar2=0.0, op0=ALU.mult, op1=ALU.add)
                 else:
                     nc.scalar.copy(out=dst, in_=src)
             rounded[key] = [tile[:] for tile in tiles]
@@ -205,7 +208,7 @@ def tile_list_crossword_clue_features_kernel(
                 in_=src[:].rearrange("p a (g m t) -> p (a g) t m", g=2, t=PACK))
             return dst
 
-        v2_w = {}
+        v2_w, taken = {}, {}
         word_ps, sense_ps, word, gate, h_bf, h_codes, h_scales = {}, {}, {}, {}, {}, {}, {}
         dom_ps, y_ps, y, y_bf = {}, {}, {}, {}
         y_scales = sbuf([P, 2, S], U8, "y_scales")
@@ -221,7 +224,7 @@ def tile_list_crossword_clue_features_kernel(
                 nc.tensor.matmul_mx(
                     out=word_ps[g, t][:],
                     lhsT=codes["w1", a, g][:, cols].bitcast(FP8X4), lhsT_scale=scales["w1", a, g][:, cols],
-                    rhs=v_w[a][:].bitcast(FP8X4), rhs_scale=plane["tab"][4 * a :, 0, :], start=(a == 0), stop=(a == 1))
+                    rhs=v_w[a][:].bitcast(FP8X4), rhs_scale=tab_plane[4 * a :, :], start=(a == 0), stop=(a == 1))
 
         def keep_word(g):
             word[g] = sbuf([P, 2, PACK, HALF], F32, "word%d" % g)
@@ -235,15 +238,15 @@ def tile_list_crossword_clue_features_kernel(
                 nc.tensor.matmul_mx(
                     out=dom_ps[g, t][:], lhsT=codes["w3", 0, g][:, cols].bitcast(FP8X4),
                     lhsT_scale=scales["w3", 0, g][:, cols],
-                    rhs=v3_w[:].bitcast(FP4X4), rhs_scale=plane["tab3"][:, 0, :], start=True, stop=True)
+                    rhs=v3_w[:].bitcast(FP4X4), rhs_scale=tab3_plane[:], start=True, stop=True)
 
-        def agreement(g):
-            gate[g] = sbuf([P, 2, PACK, HALF], F32, "gate%d" % g)
-            for t in range(PACK):
+        def agreement(g, slices):
+            for t in slices:
+                gate[g, t] = sbuf([P, 2, HALF], F32, "gate_%d_%d" % (g, t))
                 nc.vector.scalar_tensor_tensor(
-                    out=gate[g][:, :, t, :], in0=halves(dom_ps[g, t]), scalar=bd_sb[:, g, t : t + 1],
+                    out=gate[g, t][:], in0=halves(dom_ps[g, t]), scalar=bd_sb[:, g, t : t + 1],
                     in1=word[g][:, :, t, :], op0=ALU.add, op1=ALU.mult)
-                nc.scalar.activation(gate[g][:, :, t, :], gate[g][:, :, t, :], ACT.Tanh)
+                nc.scalar.activation(gate[g, t][:], gate[g, t][:], ACT.Tanh)
 
         def sense_pass(g, a):
             for t in range(PACK):
@@ -252,20 +255,29 @@ def tile_list_crossword_clue_features_kernel(
                 nc.tensor.matmul_mx(
                     out=sense_ps[g, t][:],
                     lhsT=w2_dealt_w[:, a, g, t, :].bitcast(FP4X4), lhsT_scale=w2_dealt_s[:, a, g, t, :],
-                    rhs=v2_w[a][:].bitcast(FP8X4), rhs_scale=plane["tab2"][:, a, :], start=(a == 0), stop=(a == 1))
+                    rhs=v2_w[a][:].bitcast(FP8X4), rhs_scale=tab2_plane[a][:], start=(a == 0), stop=(a == 1))
 
-        def gated_sense(g, part):
+        def gated_sense(g, half):
+            taken[g, half] = sbuf([P, PACK, HALF], F32, "taken_%d_%d" % (g, half))
             for t in range(PACK):
                 nc.vector.tensor_tensor(
-                    out=gate[g][:, part, t, :], in0=halves(sense_ps[g, t])[:, part, :],
-                    in1=gate[g][:, part, t, :], op=ALU.mult)
+                    out=taken[g, half][:, t, :], in0=halves(sense_ps[g, t])[:, half, :],
+                    in1=gate[g, t][:, half, :], op=ALU.mult)
+
+        def gated_sense_whole(g):
+            both = sbuf([P, 2, PACK, HALF], F32, "taken_%d" % g)
+            for t in range(PACK):
+                nc.vector.tensor_tensor(
+                    out=both[:, :, t, :], in0=halves(sense_ps[g, t]), in1=gate[g, t][:], op=ALU.mult)
+            for half in range(2):
+                taken[g, half] = both[:, half]
 
         def finish_h(g, half):
             h_bf[g, half] = sbuf([P, PACK * HALF], BF16, "h_bf_%d_%d" % (g, half))
             nc.vector.tensor_tensor(
                 out=h_bf[g, half][:].rearrange("p (c i t) -> p c t i", i=2, t=PACK),
                 in0=word[g][:, half].rearrange("p t (c i) -> p c t i", i=2),
-                in1=gate[g][:, half].rearrange("p t (c i) -> p c t i", i=2),
+                in1=taken[g, half][:, :, :].rearrange("p t (c i) -> p c t i", i=2),
                 op=ALU.subtract)
 
         def quantise_h(g, half):
@@ -309,9 +321,10 @@ def tile_list_crossword_clue_features_kernel(
 
         round_weight("w1", 0, 0)
         quantise_weight("w1", 0, 0)
+        v_w[0] = gather(tab_w[0][:], list1, U32, "v_w0")
         word_pass(0, 0)
-        round_weight("w3", 0, 0)
         w2_dealt_s = deal_w2(w2_s, U8, "w2_dealt_s")
+        round_weight("w3", 0, 0)
         quantise_weight("w3", 0, 0)
         domain(0)
         round_weight("w1", 1, 0)
@@ -320,13 +333,14 @@ def tile_list_crossword_clue_features_kernel(
         word_pass(0, 1)
         keep_word(0)
         w2_dealt_w = deal_w2(w2_w, U16, "w2_dealt_w")
+        agreement(0, (0, 1))
         v2_w[0] = gather(tab2_w[0][:], list2, U32, "v2_w0")
-        agreement(0)
+        agreement(0, (2, 3))
 
         sense_pass(0, 0)
         v2_w[1] = gather(tab2_w[1][:], list2, U32, "v2_w1")
         sense_pass(0, 1)
-        gated_sense(0, slice(0, 2))
+        gated_sense_whole(0)
         for a in range(2):
             round_weight("w1", a, 1)
             quantise_weight("w1", a, 1)
@@ -335,30 +349,29 @@ def tile_list_crossword_clue_features_kernel(
         keep_word(1)
         quantise_weight("w3", 0, 1)
         domain(1)
-        agreement(1)
+        for half in range(2):
+            finish_h(0, half)
+        agreement(1, range(PACK))
         for a in range(2):
             sense_pass(1, a)
         for half in range(2):
-            finish_h(0, half)
             quantise_h(0, half)
-        for g in range(2):
-            for a in range(2):
-                round_weight("wo", a, g)
-                quantise_weight("wo", a, g)
 
         for half in range(2):
-            gated_sense(1, slice(half, half + 1))
-            for g in range(2):
-                for pair in range(2):
-                    out_pass(half, g, pair, 0)
+            round_weight("wo", half, 0)
+            quantise_weight("wo", half, 0)
+            gated_sense(1, half)
             finish_h(1, half)
             quantise_h(1, half)
-            for g in range(2):
-                for pair in range(2):
-                    out_pass(half, g, pair, 1)
+        for a in range(2):
+            round_weight("wo", a, 1)
+            quantise_weight("wo", a, 1)
+        for g in range(2):
+            for half in range(2):
+                for a in range(2):
+                    for pair in range(2):
+                        out_pass(half, g, pair, a)
                 gain_and_store(half, g)
-        for half in range(2):
-            for g in range(2):
                 quantise_y(half, g)
         rows = out_2.bitcast(I32).rearrange("g (quad c) w -> c quad g w", c=4)
         for c in range(4):

@@ -23,11 +23,11 @@ QUADS = 4
 HALF = S // 2
 KIB = 1024
 
-ROUNDED_ON_GPSIMD = ("wo", 0, 0)
+ROUNDED_ON_VECTOR = ("wo", 0, 0)
 QUANTISED_IN_HALVES = (("w1", 1, 0), ("w3", 0, 1))
 
 SHARED = {
-    "word0": 0, "bf_wo_0_0": 0, "taken_1_0": 0,
+    "bf_wo_0_0": 0, "taken_1_0": 0,
     "bf_w1_0_1": 8 * KIB, "h_bf_0_0": 8 * KIB,
     "bf_w1_1_1": 12 * KIB, "bf_w3_0_1_1": 12 * KIB, "h_bf_0_1": 12 * KIB,
     "bf_wo_1_0": 16 * KIB, "taken_1_1": 16 * KIB,
@@ -181,13 +181,8 @@ def tile_list_crossword_clue_features_kernel(
                 else:
                     tiles = [bfs.tile([P, PACK * G], BF16, name="bf", align_bytes=64)]
                 dst = tiles[0][:].rearrange("p (b e m j) -> p b m j e", b=2, e=2, j=PACK)
-                if key == ROUNDED_ON_GPSIMD:
-                    by_slice = tiles[0][:].rearrange("p (t m j) -> p t m j", t=PACK, j=PACK)
-                    columns = raw[key].rearrange("p j (m t) -> p t m j", t=PACK)
-                    for b in range(2):
-                        nc.gpsimd.tensor_scalar(
-                            out=by_slice[:, 2 * b : 2 * b + 2], in0=columns[:, 2 * b : 2 * b + 2],
-                            scalar1=1.0, scalar2=0.0, op0=ALU.mult, op1=ALU.add)
+                if key == ROUNDED_ON_VECTOR:
+                    nc.vector.tensor_copy(out=dst, in_=src)
                 else:
                     nc.scalar.copy(out=dst, in_=src)
             rounded[key] = [tile[:] for tile in tiles]

@@ -23,14 +23,14 @@ QUADS = 4
 HALF = S // 2
 KIB = 1024
 
-ROUNDED_ON_VECTOR = ("wo", 0, 0)
+ROUNDED_ON_VECTOR = ("wo", 1, 0)
+ROUNDED_ROUND_THE_TANH = ("wo", 0, 0)
 QUANTISED_IN_HALVES = (("w1", 1, 0), ("w3", 0, 1))
 
 SHARED = {
-    "bf_wo_0_0": 0, "taken_1_0": 0,
     "bf_w1_0_1": 8 * KIB, "h_bf_0_0": 8 * KIB,
     "bf_w1_1_1": 12 * KIB, "bf_w3_0_1_1": 12 * KIB, "h_bf_0_1": 12 * KIB,
-    "bf_wo_1_0": 16 * KIB, "taken_1_1": 16 * KIB,
+    "bf_wo_1_1": 16 * KIB, "h_bf_1_1": 16 * KIB, "taken_1_0": 0, "taken_1_1": 4 * KIB,
     "w2_w": 20 * KIB, "gate_0_0": 20 * KIB, "gate_0_1": 22 * KIB,
     "tab2_w0": 24 * KIB, "gate_0_2": 24 * KIB, "gate_0_3": 26 * KIB,
     "tab_w0": 32 * KIB, "taken_0": 32 * KIB,
@@ -183,6 +183,9 @@ def tile_list_crossword_clue_features_kernel(
                 dst = tiles[0][:].rearrange("p (b e m j) -> p b m j e", b=2, e=2, j=PACK)
                 if key == ROUNDED_ON_VECTOR:
                     nc.vector.tensor_copy(out=dst, in_=src)
+                elif key == ROUNDED_ROUND_THE_TANH:
+                    for b in range(2):
+                        nc.scalar.copy(out=dst[:, b], in_=src[:, b])
                 else:
                     nc.scalar.copy(out=dst, in_=src)
             rounded[key] = [tile[:] for tile in tiles]
@@ -344,29 +347,30 @@ def tile_list_crossword_clue_features_kernel(
         keep_word(1)
         quantise_weight("w3", 0, 1)
         domain(1)
-        for half in range(2):
-            finish_h(0, half)
         agreement(1, range(PACK))
         for a in range(2):
             sense_pass(1, a)
         for half in range(2):
+            finish_h(0, half)
             quantise_h(0, half)
+        for g in range(2):
+            for a in range(2):
+                round_weight("wo", a, g)
+                quantise_weight("wo", a, g)
 
         for half in range(2):
-            round_weight("wo", half, 0)
-            quantise_weight("wo", half, 0)
             gated_sense(1, half)
+            for g in range(2):
+                for pair in range(2):
+                    out_pass(half, g, pair, 0)
             finish_h(1, half)
             quantise_h(1, half)
-        for a in range(2):
-            round_weight("wo", a, 1)
-            quantise_weight("wo", a, 1)
-        for g in range(2):
-            for half in range(2):
-                for a in range(2):
-                    for pair in range(2):
-                        out_pass(half, g, pair, a)
+            for g in range(2):
+                for pair in range(2):
+                    out_pass(half, g, pair, 1)
                 gain_and_store(half, g)
+        for half in range(2):
+            for g in range(2):
                 quantise_y(half, g)
         rows = out_2.bitcast(I32).rearrange("g (quad c) w -> c quad g w", c=4)
         for c in range(4):

@@ -119,6 +119,13 @@ def tile_list_crossword_clue_features_kernel(
                     out=plane[first + c : P : 32, :].bitcast(I32),
                     in_=picked[name][8 * c + 4 * a : P : 32, :].bitcast(I32))
 
+        def deal_w2(src, dtype, name):
+            dst = sbuf([P, 2, 2, PACK, P], dtype, name)
+            nc.vector.tensor_copy(
+                out=dst[:].rearrange("p a g t m -> p (a g) t m"),
+                in_=src[:].rearrange("p a (g m t) -> p (a g) t m", g=2, t=PACK))
+            return dst
+
         def gather(window, offsets, dtype, name):
             dst = sbuf([P, S], dtype, name)
             nc.vector.tensor_copy(dst[:], window.indirect(offsets[:]))
@@ -126,22 +133,17 @@ def tile_list_crossword_clue_features_kernel(
 
         v_w = {}
 
-        def load_scales_side_by_side(dst, src, which):
-            rows = src.bitcast(I32).rearrange("a (quad c) w -> c quad a w", c=4)
-            for c in which:
-                nc.sync.dma_start(out=dst[c:P:32].bitcast(I32), in_=rows[c])
-
         nc.sync.dma_start(list1[:], offs)
         nc.sync.dma_start(list3[:], offs3)
         load_scales_spread(tab_s, tab_scales)
         nc.sync.dma_start(out=tab3_w[:].bitcast(I32), in_=tab3_words[0].bitcast(I32))
         load_scales_spread(tab3_s, tab3_scales)
-        nc.sync.dma_start(list2[:], offs2)
+        nc.sync.dma_start(out=bd_sb[:], in_=bd.rearrange("(g p t) -> p g t", p=P, t=PACK))
         load_weight("w1", w1, 0, 0)
+        nc.sync.dma_start(list2[:], offs2)
         load_scales_spread(tab2_s, tab2_scales)
-        load_scales_side_by_side(w2_s, w2_scales, (0, 1))
+        nc.sync.dma_start(out=w2_s[0:P:8].bitcast(I32), in_=w2_scales.bitcast(I32).rearrange("a q w -> q a w"))
         load_words(tab_w[0], tab_words, 0)
-        load_scales_side_by_side(w2_s, w2_scales, (2, 3))
         pick_scales("tab", tab_s, list1, tab_plane[:])
         v3_w = gather(tab3_w[:], list3, U16, "v3_w")
         place_scales("tab", 0, (1, 2, 3), tab_plane, 0)
@@ -151,20 +153,23 @@ def tile_list_crossword_clue_features_kernel(
         pick_scales("tab3", tab3_s, list3, tab3_plane[:])
         place_scales("tab3", 0, (1, 2, 3), tab3_plane, 0)
         load_words(tab_w[1], tab_words, 1)
-        nc.sync.dma_start(out=bd_sb[:], in_=bd.rearrange("(g p t) -> p g t", p=P, t=PACK))
-        nc.sync.dma_start(out=w2_w[:].bitcast(I32), in_=w2_words.bitcast(I32).rearrange("a p c -> p a c"))
         pick_scales("tab2", tab2_s, list2, tab2_plane[0][:])
         place_scales("tab2", 0, (1, 2, 3), tab2_plane[0], 0)
+        nc.sync.dma_start(out=w2_w[:].bitcast(I32), in_=w2_words.bitcast(I32).rearrange("a p c -> p a c"))
+        w2_dealt_s = deal_w2(w2_s, U8, "w2_dealt_s")
+        dealt_rows = w2_dealt_s[:].rearrange("p a g t m -> p (a g t m)").bitcast(I32)
+        for c in range(1, 4):
+            nc.sync.dma_start(out=dealt_rows[c:P:32], in_=dealt_rows[8 * c : P : 32])
         load_words(tab2_w[0], tab2_words, 0)
         place_scales("tab2", 1, (0, 1, 2, 3), tab2_plane[1], 0)
         load_words(tab2_w[1], tab2_words, 1)
         for a in range(2):
             load_weight("w1", w1, a, 1)
         load_weight("w3", w3, 0, 1)
-        nc.sync.dma_start(out=go_sb[:], in_=go.rearrange("(g p t) -> p g t", p=P, t=PACK))
         for g in range(2):
             for a in range(2):
                 load_weight("wo", wo, a, g)
+        nc.sync.dma_start(out=go_sb[:], in_=go.rearrange("(g p t) -> p g t", p=P, t=PACK))
 
         rounded, codes, scales = {}, {}, {}
 
@@ -198,13 +203,6 @@ def tile_list_crossword_clue_features_kernel(
                 cols = slice(width * b, width * (b + 1))
                 nc.vector.quantize_mx(
                     out=codes[key][:, cols].bitcast(FP8X4), scales=scales[key][:, cols], in_=part)
-
-        def deal_w2(src, dtype, name):
-            dst = sbuf([P, 2, 2, PACK, P], dtype, name)
-            nc.vector.tensor_copy(
-                out=dst[:].rearrange("p a g t m -> p (a g) t m"),
-                in_=src[:].rearrange("p a (g m t) -> p (a g) t m", g=2, t=PACK))
-            return dst
 
         v2_w, taken = {}, {}
         word_ps, sense_ps, word, gate, h_bf, h_codes, h_scales = {}, {}, {}, {}, {}, {}, {}
@@ -321,7 +319,6 @@ def tile_list_crossword_clue_features_kernel(
         quantise_weight("w1", 0, 0)
         v_w[0] = gather(tab_w[0][:], list1, U32, "v_w0")
         word_pass(0, 0)
-        w2_dealt_s = deal_w2(w2_s, U8, "w2_dealt_s")
         round_weight("w3", 0, 0)
         quantise_weight("w3", 0, 0)
         domain(0)
@@ -374,4 +371,5 @@ def tile_list_crossword_clue_features_kernel(
                 quantise_y(half, g)
         rows = out_2.bitcast(I32).rearrange("g (quad c) w -> c quad g w", c=4)
         for c in range(4):
-            nc.sync.dma_start(out=rows[c], in_=y_scales[c:P:32].bitcast(I32))
+            queue = nc.scalar if c % 2 else nc.sync
+            queue.dma_start(out=rows[c], in_=y_scales[c:P:32].bitcast(I32))

@@ -34,6 +34,7 @@ SHARED = {
     "w2_w": 20 * KIB, "gate_0_0": 20 * KIB, "gate_0_1": 22 * KIB,
     "tab2_w0": 24 * KIB, "gate_0_2": 24 * KIB, "gate_0_3": 26 * KIB,
     "tab_w0": 32 * KIB, "taken_0": 32 * KIB,
+    "tab_s": 40 * KIB, "v3_w": 40 * KIB,
 }
 
 LOW, HIGH = (0, 1, 2, 3), (4, 5, 6, 7)
@@ -133,13 +134,13 @@ def tile_list_crossword_clue_features_kernel(
 
         v_w = {}
 
-        nc.sync.dma_start(list1[:], offs)
         nc.sync.dma_start(list3[:], offs3)
-        load_scales_spread(tab_s, tab_scales)
         nc.sync.dma_start(out=tab3_w[:].bitcast(I32), in_=tab3_words[0].bitcast(I32))
+        nc.sync.dma_start(list1[:], offs)
+        load_scales_spread(tab_s, tab_scales)
+        load_weight("w1", w1, 0, 0)
         load_scales_spread(tab3_s, tab3_scales)
         nc.sync.dma_start(out=bd_sb[:], in_=bd.rearrange("(g p t) -> p g t", p=P, t=PACK))
-        load_weight("w1", w1, 0, 0)
         nc.sync.dma_start(list2[:], offs2)
         load_scales_spread(tab2_s, tab2_scales)
         nc.sync.dma_start(out=w2_s[0:P:8].bitcast(I32), in_=w2_scales.bitcast(I32).rearrange("a q w -> q a w"))
@@ -152,9 +153,9 @@ def tile_list_crossword_clue_features_kernel(
         load_weight("w1", w1, 1, 0)
         pick_scales("tab3", tab3_s, list3, tab3_plane[:])
         place_scales("tab3", 0, (1, 2, 3), tab3_plane, 0)
-        load_words(tab_w[1], tab_words, 1)
         pick_scales("tab2", tab2_s, list2, tab2_plane[0][:])
         place_scales("tab2", 0, (1, 2, 3), tab2_plane[0], 0)
+        load_words(tab_w[1], tab_words, 1)
         nc.sync.dma_start(out=w2_w[:].bitcast(I32), in_=w2_words.bitcast(I32).rearrange("a p c -> p a c"))
         w2_dealt_s = deal_w2(w2_s, U8, "w2_dealt_s")
         dealt_rows = w2_dealt_s[:].rearrange("p a g t m -> p (a g t m)").bitcast(I32)

@@ -30,7 +30,9 @@ QUANTISED_IN_HALVES = (("w1", 1, 0), ("w3", 0, 1))
 SHARED = {
     "bf_w1_0_1": 8 * KIB, "h_bf_0_0": 8 * KIB,
     "bf_w1_1_1": 12 * KIB, "bf_w3_0_1_1": 12 * KIB, "h_bf_0_1": 12 * KIB,
-    "bf_wo_1_1": 16 * KIB, "h_bf_1_1": 16 * KIB, "taken_1_0": 0, "taken_1_1": 4 * KIB,
+    "bf_wo_1_1": 16 * KIB, "h_bf_1_1": 16 * KIB, "bf_wo_1_0": 0, "taken_1_0": 0, "taken_1_1": 2 * KIB,
+    "raw_wo_1_1": 44 * KIB, "y_0_0": 44 * KIB,
+    "raw_wo_0_0": 52 * KIB, "gate_1": 52 * KIB, "tab_w1": 60 * KIB, "agree_1": 60 * KIB,
     "w2_w": 20 * KIB, "gate_0_0": 20 * KIB, "gate_0_1": 22 * KIB,
     "tab2_w0": 24 * KIB, "gate_0_2": 24 * KIB, "gate_0_3": 26 * KIB,
     "tab_w0": 32 * KIB, "taken_0": 32 * KIB,
@@ -52,7 +54,7 @@ def tile_list_crossword_clue_features_kernel(
     with ExitStack() as ctx:
         lists = ctx.enter_context(tc.tile_pool(name="lists", bufs=1))
         keep = ctx.enter_context(tc.tile_pool(name="keep", bufs=1))
-        raws = ctx.enter_context(tc.tile_pool(name="raws", bufs=5))
+        raws = ctx.enter_context(tc.tile_pool(name="raws", bufs=3))
         bfs = ctx.enter_context(tc.tile_pool(name="bfs", bufs=3))
         shared = ctx.enter_context(tc.tile_pool(name="shared", bufs=1))
         psum = ctx.enter_context(tc.psum_pool(name="psum", bufs=1))
@@ -81,7 +83,7 @@ def tile_list_crossword_clue_features_kernel(
         w2_w = sbuf([P, 2, H], U16, "w2_w")
         w2_s = sbuf([P, 2, H], U8, "w2_s")
         go_sb = sbuf([P, 2, PACK], F32, "go_sb")
-        bd_sb = sbuf([P, 2, PACK], F32, "bd_sb")
+        bd_sb = sbuf([P, 2, 2 * PACK], F32, "bd_sb")
 
         nc.gpsimd.memset(tab_s[:].bitcast(I32), 0)
         nc.gpsimd.memset(tab3_s[:].bitcast(I32), 0)
@@ -98,7 +100,12 @@ def tile_list_crossword_clue_features_kernel(
             else:
                 tile = raws.tile([P, PACK, G], F32, name="raw")
             block = w[G * a : G * (a + 1), G * g : G * (g + 1)]
-            nc.sync.dma_start(out=tile[:], in_=block.rearrange("(p j) c -> p j c", j=PACK))
+            if name == "wo":
+                rows = block.rearrange("(u t i) c -> i u t c", t=PACK, i=2)
+                for i in range(2):
+                    nc.sync.dma_start(out=tile[i:P:2], in_=rows[i])
+            else:
+                nc.sync.dma_start(out=tile[:], in_=block.rearrange("(p j) c -> p j c", j=PACK))
             raw[name, a, g] = tile[:]
 
         def load_words(dst, src, a):
@@ -120,11 +127,11 @@ def tile_list_crossword_clue_features_kernel(
                     out=plane[first + c : P : 32, :].bitcast(I32),
                     in_=picked[name][8 * c + 4 * a : P : 32, :].bitcast(I32))
 
-        def deal_w2(src, dtype, name):
+        def deal_w2(src, dtype, pair_dtype, name):
             dst = sbuf([P, 2, 2, PACK, P], dtype, name)
             nc.vector.tensor_copy(
-                out=dst[:].rearrange("p a g t m -> p (a g) t m"),
-                in_=src[:].rearrange("p a (g m t) -> p (a g) t m", g=2, t=PACK))
+                out=dst[:].rearrange("p a g t m -> p (a g) t m").bitcast(pair_dtype),
+                in_=src[:].rearrange("p a c -> p (a c)").bitcast(pair_dtype).rearrange("p (x u t) -> p x t u", x=4, t=PACK))
             return dst
 
         def gather(window, offsets, dtype, name):
@@ -140,7 +147,6 @@ def tile_list_crossword_clue_features_kernel(
         load_scales_spread(tab_s, tab_scales)
         load_weight("w1", w1, 0, 0)
         load_scales_spread(tab3_s, tab3_scales)
-        nc.sync.dma_start(out=bd_sb[:], in_=bd.rearrange("(g p t) -> p g t", p=P, t=PACK))
         nc.sync.dma_start(list2[:], offs2)
         load_scales_spread(tab2_s, tab2_scales)
         nc.sync.dma_start(out=w2_s[0:P:8].bitcast(I32), in_=w2_scales.bitcast(I32).rearrange("a q w -> q a w"))
@@ -156,8 +162,11 @@ def tile_list_crossword_clue_features_kernel(
         pick_scales("tab2", tab2_s, list2, tab2_plane[0][:])
         place_scales("tab2", 0, (1, 2, 3), tab2_plane[0], 0)
         load_words(tab_w[1], tab_words, 1)
+        for i in range(2):
+            runs = bd.rearrange("(g u e) -> u g e", g=2, e=2 * PACK)[:, :, i : i + 7]
+            nc.sync.dma_start(out=bd_sb[i:P:2, :, 0:7], in_=runs)
         nc.sync.dma_start(out=w2_w[:].bitcast(I32), in_=w2_words.bitcast(I32).rearrange("a p c -> p a c"))
-        w2_dealt_s = deal_w2(w2_s, U8, "w2_dealt_s")
+        w2_dealt_s = deal_w2(w2_s, U8, U16, "w2_dealt_s")
         dealt_rows = w2_dealt_s[:].rearrange("p a g t m -> p (a g t m)").bitcast(I32)
         for c in range(1, 4):
             nc.sync.dma_start(out=dealt_rows[c:P:32], in_=dealt_rows[8 * c : P : 32])
@@ -176,12 +185,8 @@ def tile_list_crossword_clue_features_kernel(
 
         def round_weight(*key):
             name = "bf_%s_%d_%d" % key
-            src = raw[key].rearrange("p j (m b e) -> p b m j e", b=2, e=2)
-            if key in QUANTISED_IN_HALVES:
-                tiles = [sbuf([P, 2 * G], BF16, "%s_%d" % (name, b)) for b in range(2)]
-                nc.scalar.copy(out=tiles[0][:].rearrange("p (e m j) -> p m j e", e=2, j=PACK), in_=src[:, 0])
-                nc.vector.tensor_copy(out=tiles[1][:].rearrange("p (e m j) -> p m j e", e=2, j=PACK), in_=src[:, 1])
-            else:
+            if key[0] == "wo":
+                src = raw[key].rearrange("p j (m b e) -> p b m j e", b=2, e=2)
                 if name in SHARED:
                     tiles = [sbuf([P, PACK * G], BF16, name)]
                 else:
@@ -194,6 +199,19 @@ def tile_list_crossword_clue_features_kernel(
                         nc.scalar.copy(out=dst[:, b], in_=src[:, b])
                 else:
                     nc.scalar.copy(out=dst, in_=src)
+            else:
+                src = raw[key].rearrange("p j (u t i) -> p u t j i", t=PACK, i=2)
+                if key in QUANTISED_IN_HALVES:
+                    tiles = [sbuf([P, 2 * G], BF16, "%s_%d" % (name, b)) for b in range(2)]
+                    dsts = [tile[:].rearrange("p (t u i j) -> p u t j i", t=2, i=2, j=PACK) for tile in tiles]
+                    nc.scalar.copy(out=dsts[0], in_=src[:, :, 0:2])
+                    nc.vector.tensor_copy(out=dsts[1], in_=src[:, :, 2:4])
+                else:
+                    if name in SHARED:
+                        tiles = [sbuf([P, PACK * G], BF16, name)]
+                    else:
+                        tiles = [bfs.tile([P, PACK * G], BF16, name="bf", align_bytes=64)]
+                    nc.scalar.copy(out=tiles[0][:].rearrange("p (t u i j) -> p u t j i", t=PACK, i=2, j=PACK), in_=src)
             rounded[key] = [tile[:] for tile in tiles]
 
         def quantise_weight(*key):
@@ -209,6 +227,14 @@ def tile_list_crossword_clue_features_kernel(
         word_ps, sense_ps, word, gate, h_bf, h_codes, h_scales = {}, {}, {}, {}, {}, {}, {}
         dom_ps, y_ps, y, y_bf = {}, {}, {}, {}
         y_scales = sbuf([P, 2, S], U8, "y_scales")
+
+        agree = {}
+        agree_whole = sbuf([P, 2, PACK, HALF], F32, "agree_1")
+        gate_whole = sbuf([P, 2, PACK, HALF], F32, "gate_1")
+        for t in range(PACK):
+            gate[0, t] = agree[0, t] = sbuf([P, 2, HALF], F32, "gate_0_%d" % t)[:]
+            gate[1, t] = gate_whole[:, :, t, :]
+            agree[1, t] = agree_whole[:, :, t, :]
 
         def halves(ps):
             return ps[:].rearrange("p (u j) -> p u j", u=2)
@@ -239,11 +265,10 @@ def tile_list_crossword_clue_features_kernel(
 
         def agreement(g, slices):
             for t in slices:
-                gate[g, t] = sbuf([P, 2, HALF], F32, "gate_%d_%d" % (g, t))
                 nc.vector.scalar_tensor_tensor(
-                    out=gate[g, t][:], in0=halves(dom_ps[g, t]), scalar=bd_sb[:, g, t : t + 1],
+                    out=agree[g, t], in0=halves(dom_ps[g, t]), scalar=bd_sb[:, g, 2 * t : 2 * t + 1],
                     in1=word[g][:, :, t, :], op0=ALU.add, op1=ALU.mult)
-                nc.scalar.activation(gate[g, t][:], gate[g, t][:], ACT.Tanh)
+                nc.scalar.activation(gate[g, t], agree[g, t], ACT.Tanh)
 
         def sense_pass(g, a):
             for t in range(PACK):
@@ -254,18 +279,33 @@ def tile_list_crossword_clue_features_kernel(
                     lhsT=w2_dealt_w[:, a, g, t, :].bitcast(FP4X4), lhsT_scale=w2_dealt_s[:, a, g, t, :],
                     rhs=v2_w[a][:].bitcast(FP8X4), rhs_scale=tab2_plane[a][:], start=(a == 0), stop=(a == 1))
 
+        def sense_by_halves(g):
+            for half in range(2):
+                slots = slice(HALF * half, HALF * (half + 1))
+                for pair in range(2):
+                    sense_ps[g, half, pair] = bank(SENSE_BANKS[g][2 * half + pair])
+                    for a in range(2):
+                        for e in range(2):
+                            t = 2 * pair + e
+                            nc.tensor.matmul_mx(
+                                out=sense_ps[g, half, pair][:, HALF * e : HALF * (e + 1)],
+                                lhsT=w2_dealt_w[:, a, g, t, :].bitcast(FP4X4), lhsT_scale=w2_dealt_s[:, a, g, t, :],
+                                rhs=v2_w[a][:, slots].bitcast(FP8X4), rhs_scale=tab2_plane[a][:, slots],
+                                start=(a == 0 and e == 0), stop=(a == 1 and e == 1))
+
         def gated_sense(g, half):
             taken[g, half] = sbuf([P, PACK, HALF], F32, "taken_%d_%d" % (g, half))
-            for t in range(PACK):
+            for pair in range(2):
+                slices = slice(2 * pair, 2 * pair + 2)
                 nc.vector.tensor_tensor(
-                    out=taken[g, half][:, t, :], in0=halves(sense_ps[g, t])[:, half, :],
-                    in1=gate[g, t][:, half, :], op=ALU.mult)
+                    out=taken[g, half][:, slices, :], in0=halves(sense_ps[g, half, pair]),
+                    in1=gate_whole[:, half, slices, :], op=ALU.mult)
 
         def gated_sense_whole(g):
             both = sbuf([P, 2, PACK, HALF], F32, "taken_%d" % g)
             for t in range(PACK):
                 nc.vector.tensor_tensor(
-                    out=both[:, :, t, :], in0=halves(sense_ps[g, t]), in1=gate[g, t][:], op=ALU.mult)
+                    out=both[:, :, t, :], in0=halves(sense_ps[g, t]), in1=gate[g, t], op=ALU.mult)
             for half in range(2):
                 taken[g, half] = both[:, half]
 
@@ -328,7 +368,7 @@ def tile_list_crossword_clue_features_kernel(
         v_w[1] = gather(tab_w[1][:], list1, U32, "v_w1")
         word_pass(0, 1)
         keep_word(0)
-        w2_dealt_w = deal_w2(w2_w, U16, "w2_dealt_w")
+        w2_dealt_w = deal_w2(w2_w, U16, I32, "w2_dealt_w")
         agreement(0, (0, 1))
         v2_w[0] = gather(tab2_w[0][:], list2, U32, "v2_w0")
         agreement(0, (2, 3))
@@ -346,22 +386,27 @@ def tile_list_crossword_clue_features_kernel(
         quantise_weight("w3", 0, 1)
         domain(1)
         agreement(1, range(PACK))
-        for a in range(2):
-            sense_pass(1, a)
+        sense_by_halves(1)
         for half in range(2):
             finish_h(0, half)
             quantise_h(0, half)
         for g in range(2):
             for a in range(2):
                 round_weight("wo", a, g)
-                quantise_weight("wo", a, g)
+        for a in range(2):
+            quantise_weight("wo", a, 0)
 
         for half in range(2):
             gated_sense(1, half)
+            if half == 0:
+                finish_h(1, half)
+                for a in range(2):
+                    quantise_weight("wo", a, 1)
             for g in range(2):
                 for pair in range(2):
                     out_pass(half, g, pair, 0)
-            finish_h(1, half)
+            if half == 1:
+                finish_h(1, half)
             quantise_h(1, half)
             for g in range(2):
                 for pair in range(2):

@@ -30,9 +30,9 @@ QUANTISED_IN_HALVES = (("w1", 1, 0), ("w3", 0, 1))
 SHARED = {
     "bf_w1_0_1": 8 * KIB, "h_bf_0_0": 8 * KIB,
     "bf_w1_1_1": 12 * KIB, "bf_w3_0_1_1": 12 * KIB, "h_bf_0_1": 12 * KIB,
-    "bf_wo_1_1": 16 * KIB, "h_bf_1_1": 16 * KIB, "bf_wo_1_0": 0, "taken_1_0": 0, "taken_1_1": 2 * KIB,
+    "bf_wo_1_1": 16 * KIB, "h_bf_1_1": 16 * KIB, "y_bf_0_0": 16 * KIB, "bf_wo_1_0": 0, "codes_wo_0_0": 0, "taken_1_0": 2 * KIB, "taken_1_1": 4 * KIB,
     "raw_wo_1_1": 44 * KIB, "y_0_0": 44 * KIB,
-    "raw_wo_0_0": 52 * KIB, "gate_1": 52 * KIB, "tab_w1": 60 * KIB, "agree_1": 60 * KIB,
+    "gate_1": 52 * KIB, "tab_w1": 60 * KIB, "agree_1": 60 * KIB,
     "w2_w": 20 * KIB, "gate_0_0": 20 * KIB, "gate_0_1": 22 * KIB,
     "tab2_w0": 24 * KIB, "gate_0_2": 24 * KIB, "gate_0_3": 26 * KIB,
     "tab_w0": 32 * KIB, "taken_0": 32 * KIB,
@@ -147,10 +147,13 @@ def tile_list_crossword_clue_features_kernel(
         load_scales_spread(tab_s, tab_scales)
         load_weight("w1", w1, 0, 0)
         load_scales_spread(tab3_s, tab3_scales)
+        for i in range(2):
+            runs = bd.rearrange("(g u e) -> u g e", g=2, e=2 * PACK)[:, :, i : i + 7]
+            nc.sync.dma_start(out=bd_sb[i:P:2, :, 0:7], in_=runs)
         nc.sync.dma_start(list2[:], offs2)
         load_scales_spread(tab2_s, tab2_scales)
-        nc.sync.dma_start(out=w2_s[0:P:8].bitcast(I32), in_=w2_scales.bitcast(I32).rearrange("a q w -> q a w"))
         load_words(tab_w[0], tab_words, 0)
+        nc.sync.dma_start(out=w2_s[0:P:8].bitcast(I32), in_=w2_scales.bitcast(I32).rearrange("a q w -> q a w"))
         pick_scales("tab", tab_s, list1, tab_plane[:])
         v3_w = gather(tab3_w[:], list3, U16, "v3_w")
         place_scales("tab", 0, (1, 2, 3), tab_plane, 0)
@@ -162,9 +165,6 @@ def tile_list_crossword_clue_features_kernel(
         pick_scales("tab2", tab2_s, list2, tab2_plane[0][:])
         place_scales("tab2", 0, (1, 2, 3), tab2_plane[0], 0)
         load_words(tab_w[1], tab_words, 1)
-        for i in range(2):
-            runs = bd.rearrange("(g u e) -> u g e", g=2, e=2 * PACK)[:, :, i : i + 7]
-            nc.sync.dma_start(out=bd_sb[i:P:2, :, 0:7], in_=runs)
         nc.sync.dma_start(out=w2_w[:].bitcast(I32), in_=w2_words.bitcast(I32).rearrange("a p c -> p a c"))
         w2_dealt_s = deal_w2(w2_s, U8, U16, "w2_dealt_s")
         dealt_rows = w2_dealt_s[:].rearrange("p a g t m -> p (a g t m)").bitcast(I32)
@@ -176,16 +176,25 @@ def tile_list_crossword_clue_features_kernel(
         for a in range(2):
             load_weight("w1", w1, a, 1)
         load_weight("w3", w3, 0, 1)
-        for g in range(2):
-            for a in range(2):
-                load_weight("wo", wo, a, g)
+        first_wo = [sbuf([P, PACK, G // 2], F32, "first_wo%d" % u) for u in range(2)]
+        for u in range(2):
+            rows = wo[0:G, G // 2 * u : G // 2 * (u + 1)].rearrange("(u t i) c -> i u t c", t=PACK, i=2)
+            for i in range(2):
+                nc.sync.dma_start(out=first_wo[u][i:P:2], in_=rows[i])
+        for a, g in ((1, 0), (0, 1), (1, 1)):
+            load_weight("wo", wo, a, g)
         nc.sync.dma_start(out=go_sb[:], in_=go.rearrange("(g p t) -> p g t", p=P, t=PACK))
 
         rounded, codes, scales = {}, {}, {}
 
         def round_weight(*key):
             name = "bf_%s_%d_%d" % key
-            if key[0] == "wo":
+            if key == ROUNDED_ROUND_THE_TANH:
+                tiles = [bfs.tile([P, PACK * G], BF16, name="bf", align_bytes=64)]
+                dst = tiles[0][:].rearrange("p (b e u m j) -> p u b m j e", b=2, e=2, u=2, j=PACK)
+                for u in range(2):
+                    nc.scalar.copy(out=dst[:, u], in_=first_wo[u][:].rearrange("p j (m b e) -> p b m j e", b=2, e=2))
+            elif key[0] == "wo":
                 src = raw[key].rearrange("p j (m b e) -> p b m j e", b=2, e=2)
                 if name in SHARED:
                     tiles = [sbuf([P, PACK * G], BF16, name)]
@@ -194,9 +203,6 @@ def tile_list_crossword_clue_features_kernel(
                 dst = tiles[0][:].rearrange("p (b e m j) -> p b m j e", b=2, e=2, j=PACK)
                 if key == ROUNDED_ON_VECTOR:
                     nc.vector.tensor_copy(out=dst, in_=src)
-                elif key == ROUNDED_ROUND_THE_TANH:
-                    for b in range(2):
-                        nc.scalar.copy(out=dst[:, b], in_=src[:, b])
                 else:
                     nc.scalar.copy(out=dst, in_=src)
             else:
@@ -393,12 +399,12 @@ def tile_list_crossword_clue_features_kernel(
         for g in range(2):
             for a in range(2):
                 round_weight("wo", a, g)
-        for a in range(2):
-            quantise_weight("wo", a, 0)
+        quantise_weight("wo", 1, 0)
 
         for half in range(2):
             gated_sense(1, half)
             if half == 0:
+                quantise_weight("wo", 0, 0)
                 finish_h(1, half)
                 for a in range(2):
                     quantise_weight("wo", a, 1)

@@ -318,9 +318,9 @@ def tile_list_crossword_clue_features_kernel(
         def finish_h(g, half):
             h_bf[g, half] = sbuf([P, PACK * HALF], BF16, "h_bf_%d_%d" % (g, half))
             nc.vector.tensor_tensor(
-                out=h_bf[g, half][:].rearrange("p (c i t) -> p c t i", i=2, t=PACK),
-                in0=word[g][:, half].rearrange("p t (c i) -> p c t i", i=2),
-                in1=taken[g, half][:, :, :].rearrange("p t (c i) -> p c t i", i=2),
+                out=h_bf[g, half][:].rearrange("p (c i t) -> p c t i", i=4, t=PACK),
+                in0=word[g][:, half].rearrange("p t (c i) -> p c t i", i=4),
+                in1=taken[g, half][:, :, :].rearrange("p t (c i) -> p c t i", i=4),
                 op=ALU.subtract)
 
         def quantise_h(g, half):
@@ -353,8 +353,8 @@ def tile_list_crossword_clue_features_kernel(
             slots = slice(HALF * half, HALF * (half + 1))
             y_bf[half, g] = sbuf([P, PACK * HALF], BF16, "y_bf_%d_%d" % (half, g))
             nc.vector.tensor_copy(
-                out=y_bf[half, g][:].rearrange("p (c i t) -> p c t i", i=2, t=PACK),
-                in_=y[half, g][:].rearrange("p t (c i) -> p c t i", i=2))
+                out=y_bf[half, g][:].rearrange("p (c i t) -> p c t i", i=4, t=PACK),
+                in_=y[half, g][:].rearrange("p t (c i) -> p c t i", i=4))
             y_codes = sbuf([P, HALF], U32, "y_codes_%d_%d" % (half, g))
             nc.vector.quantize_mx(
                 out=y_codes[:].bitcast(FP8X4), scales=y_scales[:, g, slots], in_=y_bf[half, g][:])

@@ -19,31 +19,24 @@ ACT = mybir.ActivationFunctionType
 P = 128
 PACK = 4
 G = P * PACK
-QUADS = 4
 HALF = S // 2
 KIB = 1024
 
-ROUNDED_ON_VECTOR = ("wo", 1, 0)
-ROUNDED_ROUND_THE_TANH = ("wo", 0, 0)
-QUANTISED_IN_HALVES = (("w1", 1, 0), ("w3", 0, 1))
-
 SHARED = {
-    "bf_w1_0_1": 8 * KIB, "h_bf_0_0": 8 * KIB,
-    "bf_w1_1_1": 12 * KIB, "bf_w3_0_1_1": 12 * KIB, "h_bf_0_1": 12 * KIB,
-    "bf_wo_1_1": 16 * KIB, "h_bf_1_1": 16 * KIB, "y_bf_0_0": 16 * KIB, "bf_wo_1_0": 0, "codes_wo_0_0": 0, "taken_1_0": 2 * KIB, "taken_1_1": 4 * KIB,
-    "raw_wo_1_1": 44 * KIB, "y_0_0": 44 * KIB,
-    "gate_1": 52 * KIB, "tab_w1": 60 * KIB, "agree_1": 60 * KIB,
-    "w2_w": 20 * KIB, "gate_0_0": 20 * KIB, "gate_0_1": 22 * KIB,
-    "tab2_w0": 24 * KIB, "gate_0_2": 24 * KIB, "gate_0_3": 26 * KIB,
-    "tab_w0": 32 * KIB, "taken_0": 32 * KIB,
-    "tab_s": 40 * KIB, "v3_w": 40 * KIB,
+    "bf_w3_0_1": 0, "h_bf_0_0": 0,
+    "bf_w1_1_1_0": 4 * KIB, "bf_w1_1_1_1": 6 * KIB, "h_bf_0_1": 5 * KIB,
+    "raw_wo_1_0_0": 8 * KIB, "word1": 8 * KIB,
+    "raw_wo_0_0": 16 * KIB, "taken_1_0": 16 * KIB, "taken_1_1": 20 * KIB,
+    "bf_wo_0_0": 24 * KIB, "codes_wo_1_0": 24 * KIB,
+    "bf_wo_1_1": 28 * KIB, "h_bf_1_1": 28 * KIB, "y_bf_0_0": 28 * KIB,
+    "raw_wo_1_1": 32 * KIB, "y_0_0": 32 * KIB,
+    "tab_w0": 40 * KIB, "taken_0": 40 * KIB,
+    "tab_w1": 48 * KIB, "gate_1": 48 * KIB,
+    "tab2_w0": 56 * KIB, "gate_0_1_1": 56 * KIB, "y_0_1": 56 * KIB, "y_1_0": 60 * KIB,
+    "tab2_w1": 64 * KIB, "y_1_1": 64 * KIB,
 }
 
 LOW, HIGH = (0, 1, 2, 3), (4, 5, 6, 7)
-WORD_BANKS = (LOW, HIGH)
-DOM_BANKS = (HIGH, LOW)
-SENSE_BANKS = (LOW, HIGH)
-Y_BANKS = (LOW, HIGH)
 
 
 def tile_list_crossword_clue_features_kernel(
@@ -59,13 +52,24 @@ def tile_list_crossword_clue_features_kernel(
         shared = ctx.enter_context(tc.tile_pool(name="shared", bufs=1))
         psum = ctx.enter_context(tc.psum_pool(name="psum", bufs=1))
 
-        def sbuf(shape, dtype, name):
+        def sbuf(shape, dtype, name, ring=None):
             if name in SHARED:
                 return shared.tile(shape, dtype, name=name, align_bytes=64, offset=SHARED[name])
+            if ring is not None:
+                return ring.tile(shape, dtype, name="ring", align_bytes=64)
             return keep.tile(shape, dtype, name=name, align_bytes=64)
 
         def bank(b):
             return psum.tile([P, S], F32, name="bank%d" % b)
+
+        def two(ps):
+            return ps[:].rearrange("p (u j) -> p u j", u=2)
+
+        def slots(half):
+            return slice(HALF * half, HALF * (half + 1))
+
+        def cols(t):
+            return slice(P * t, P * (t + 1))
 
         list1 = lists.tile([P, S // 16], U16, name="list1")
         list2 = lists.tile([P, S // 16], U16, name="list2")
@@ -77,7 +81,7 @@ def tile_list_crossword_clue_features_kernel(
         tab_s = sbuf([P, T], U8, "tab_s")
         tab2_s = sbuf([P, T2], U8, "tab2_s")
         tab3_s = sbuf([P, T3], U8, "tab3_s")
-        tab_plane = sbuf([P, S], U8, "tab_plane")
+        tab_plane = [sbuf([P, S], U8, "tab_plane%d" % a) for a in range(2)]
         tab2_plane = [sbuf([P, S], U8, "tab2_plane%d" % a) for a in range(2)]
         tab3_plane = sbuf([P, S], U8, "tab3_plane")
         w2_w = sbuf([P, 2, H], U16, "w2_w")
@@ -85,41 +89,46 @@ def tile_list_crossword_clue_features_kernel(
         go_sb = sbuf([P, 2, PACK], F32, "go_sb")
         bd_sb = sbuf([P, 2, 2 * PACK], F32, "bd_sb")
 
-        nc.gpsimd.memset(tab_s[:].bitcast(I32), 0)
         nc.gpsimd.memset(tab3_s[:].bitcast(I32), 0)
+        nc.gpsimd.memset(tab_s[:].bitcast(I32), 0)
         nc.vector.memset(tab2_s[:].bitcast(I32), 0)
         nc.gpsimd.memset(w2_s[:].rearrange("p a c -> p (a c)").bitcast(I32), 0)
         nc.gpsimd.memset(tab2_plane[1][:].bitcast(I32), 0)
 
-        raw = {}
+        raw, picked = {}, {}
 
         def load_weight(name, w, a, g):
-            own_name = "raw_%s_%d_%d" % (name, a, g)
-            if own_name in SHARED:
-                tile = sbuf([P, PACK, G], F32, own_name)
-            else:
-                tile = raws.tile([P, PACK, G], F32, name="raw")
+            raw[name, a, g] = sbuf([P, PACK, G], F32, "raw_%s_%d_%d" % (name, a, g), raws)
             block = w[G * a : G * (a + 1), G * g : G * (g + 1)]
-            if name == "wo":
-                rows = block.rearrange("(u t i) c -> i u t c", t=PACK, i=2)
-                for i in range(2):
-                    nc.sync.dma_start(out=tile[i:P:2], in_=rows[i])
-            else:
-                nc.sync.dma_start(out=tile[:], in_=block.rearrange("(p j) c -> p j c", j=PACK))
-            raw[name, a, g] = tile[:]
+            nc.sync.dma_start(out=raw[name, a, g][:], in_=block.rearrange("(p j) c -> p j c", j=PACK))
+
+        def load_wo(tile, a, first, width):
+            rows = wo[G * a : G * (a + 1), first : first + width].rearrange("(u t i) c -> i u t c", t=PACK, i=2)
+            for i in range(2):
+                nc.sync.dma_start(out=tile[i:P:2], in_=rows[i])
 
         def load_words(dst, src, a):
             nc.sync.dma_start(out=dst[:].bitcast(I32), in_=src[a].rearrange("p c i -> p (c i)").bitcast(I32))
 
-        def load_scales_spread(dst, src):
-            for a in range(src.shape[0]):
-                nc.sync.dma_start(out=dst[4 * a : P : 8, :].bitcast(I32), in_=src[a].bitcast(I32))
+        def load_scale_rows(dst, src, a):
+            nc.sync.dma_start(out=dst[4 * a : P : 8, :].bitcast(I32), in_=src[a].bitcast(I32))
 
-        picked = {}
+        def load_bias(i):
+            runs = bd.rearrange("(g u e) -> u g e", g=2, e=2 * PACK)[:, :, i : i + 7]
+            nc.sync.dma_start(out=bd_sb[i:P:2, :, 0:7], in_=runs)
+
+        def gather(window, offsets, dtype, name):
+            dst = sbuf([P, S], dtype, name)
+            nc.vector.tensor_copy(dst[:], window[:].indirect(offsets[:]))
+            return dst
+
+        def gather_half(dst, window, offsets, half):
+            entries = slice(HALF // 16 * half, HALF // 16 * (half + 1))
+            nc.vector.tensor_copy(dst[:, slots(half)], window[:].indirect(offsets[:, entries]))
 
         def pick_scales(name, window, offsets, plane):
-            picked[name] = gather(window[:], offsets, U8, "picked_" + name)
-            nc.vector.tensor_copy(out=plane.bitcast(I32), in_=picked[name][:].bitcast(I32))
+            picked[name] = gather(window, offsets, U8, "picked_" + name)
+            nc.vector.tensor_copy(out=plane[:].bitcast(I32), in_=picked[name][:].bitcast(I32))
 
         def place_scales(name, a, rows, plane, first):
             for c in rows:
@@ -127,200 +136,162 @@ def tile_list_crossword_clue_features_kernel(
                     out=plane[first + c : P : 32, :].bitcast(I32),
                     in_=picked[name][8 * c + 4 * a : P : 32, :].bitcast(I32))
 
-        def deal_w2(src, dtype, pair_dtype, name):
+        def deal_w2(src, dtype, pair_dtype, name, copy):
             dst = sbuf([P, 2, 2, PACK, P], dtype, name)
-            nc.vector.tensor_copy(
+            copy(
                 out=dst[:].rearrange("p a g t m -> p (a g) t m").bitcast(pair_dtype),
                 in_=src[:].rearrange("p a c -> p (a c)").bitcast(pair_dtype).rearrange("p (x u t) -> p x t u", x=4, t=PACK))
             return dst
 
-        def gather(window, offsets, dtype, name):
-            dst = sbuf([P, S], dtype, name)
-            nc.vector.tensor_copy(dst[:], window.indirect(offsets[:]))
-            return dst
-
-        v_w = {}
-
         nc.sync.dma_start(list3[:], offs3)
         nc.sync.dma_start(out=tab3_w[:].bitcast(I32), in_=tab3_words[0].bitcast(I32))
+        load_scale_rows(tab3_s, tab3_scales, 0)
         nc.sync.dma_start(list1[:], offs)
-        load_scales_spread(tab_s, tab_scales)
-        load_weight("w1", w1, 0, 0)
-        load_scales_spread(tab3_s, tab3_scales)
-        for i in range(2):
-            runs = bd.rearrange("(g u e) -> u g e", g=2, e=2 * PACK)[:, :, i : i + 7]
-            nc.sync.dma_start(out=bd_sb[i:P:2, :, 0:7], in_=runs)
-        nc.sync.dma_start(list2[:], offs2)
-        load_scales_spread(tab2_s, tab2_scales)
-        load_words(tab_w[0], tab_words, 0)
-        nc.sync.dma_start(out=w2_s[0:P:8].bitcast(I32), in_=w2_scales.bitcast(I32).rearrange("a q w -> q a w"))
-        pick_scales("tab", tab_s, list1, tab_plane[:])
-        v3_w = gather(tab3_w[:], list3, U16, "v3_w")
-        place_scales("tab", 0, (1, 2, 3), tab_plane, 0)
+        for a in range(2):
+            load_scale_rows(tab_s, tab_scales, a)
         load_weight("w3", w3, 0, 0)
-        place_scales("tab", 1, (1, 2, 3), tab_plane, 4)
-        load_weight("w1", w1, 1, 0)
-        pick_scales("tab3", tab3_s, list3, tab3_plane[:])
+        nc.sync.dma_start(list2[:], offs2)
+        for a in range(2):
+            load_scale_rows(tab2_s, tab2_scales, a)
+        for i in range(2):
+            load_bias(i)
+        load_weight("w1", w1, 0, 0)
+        nc.sync.dma_start(out=w2_s[0:P:8].bitcast(I32), in_=w2_scales.bitcast(I32).rearrange("a q w -> q a w"))
+        v3_w = gather(tab3_w, list3, U16, "v3_w")
+        pick_scales("tab3", tab3_s, list3, tab3_plane)
+        pick_scales("tab", tab_s, list1, tab_plane[0])
+        nc.vector.tensor_copy(out=tab_plane[1][:].bitcast(I32), in_=picked["tab"][:].bitcast(I32))
+        pick_scales("tab2", tab2_s, list2, tab2_plane[0])
         place_scales("tab3", 0, (1, 2, 3), tab3_plane, 0)
-        pick_scales("tab2", tab2_s, list2, tab2_plane[0][:])
-        place_scales("tab2", 0, (1, 2, 3), tab2_plane[0], 0)
+        load_words(tab_w[0], tab_words, 0)
+        place_scales("tab", 0, (1, 2, 3), tab_plane[0], 0)
+        place_scales("tab", 1, (1,), tab_plane[1], 4)
+        load_weight("w1", w1, 1, 0)
+        place_scales("tab", 1, (2, 3), tab_plane[1], 4)
+        place_scales("tab2", 0, (1, 2), tab2_plane[0], 0)
         load_words(tab_w[1], tab_words, 1)
         nc.sync.dma_start(out=w2_w[:].bitcast(I32), in_=w2_words.bitcast(I32).rearrange("a p c -> p a c"))
-        w2_dealt_s = deal_w2(w2_s, U8, U16, "w2_dealt_s")
+        place_scales("tab2", 0, (3,), tab2_plane[0], 0)
+        w2_dealt_s = deal_w2(w2_s, U8, U16, "w2_dealt_s", nc.vector.tensor_copy)
         dealt_rows = w2_dealt_s[:].rearrange("p a g t m -> p (a g t m)").bitcast(I32)
         for c in range(1, 4):
             nc.sync.dma_start(out=dealt_rows[c:P:32], in_=dealt_rows[8 * c : P : 32])
+        place_scales("tab2", 1, (0,), tab2_plane[1], 0)
         load_words(tab2_w[0], tab2_words, 0)
-        place_scales("tab2", 1, (0, 1, 2, 3), tab2_plane[1], 0)
+        place_scales("tab2", 1, (1, 2, 3), tab2_plane[1], 0)
         load_words(tab2_w[1], tab2_words, 1)
+        load_weight("w3", w3, 0, 1)
         for a in range(2):
             load_weight("w1", w1, a, 1)
-        load_weight("w3", w3, 0, 1)
-        first_wo = [sbuf([P, PACK, G // 2], F32, "first_wo%d" % u) for u in range(2)]
+        wo_split = [sbuf([P, PACK, G // 2], F32, "raw_wo_1_0_%d" % u) for u in range(2)]
         for u in range(2):
-            rows = wo[0:G, G // 2 * u : G // 2 * (u + 1)].rearrange("(u t i) c -> i u t c", t=PACK, i=2)
-            for i in range(2):
-                nc.sync.dma_start(out=first_wo[u][i:P:2], in_=rows[i])
-        for a, g in ((1, 0), (0, 1), (1, 1)):
-            load_weight("wo", wo, a, g)
+            load_wo(wo_split[u], 1, G // 2 * u, G // 2)
+        for a, g in ((0, 0), (0, 1), (1, 1)):
+            raw["wo", a, g] = sbuf([P, PACK, G], F32, "raw_wo_%d_%d" % (a, g), raws)
+            load_wo(raw["wo", a, g], a, G * g, G)
         nc.sync.dma_start(out=go_sb[:], in_=go.rearrange("(g p t) -> p g t", p=P, t=PACK))
 
         rounded, codes, scales = {}, {}, {}
 
-        def round_weight(*key):
-            name = "bf_%s_%d_%d" % key
-            if key == ROUNDED_ROUND_THE_TANH:
-                tiles = [bfs.tile([P, PACK * G], BF16, name="bf", align_bytes=64)]
-                dst = tiles[0][:].rearrange("p (b e u m j) -> p u b m j e", b=2, e=2, u=2, j=PACK)
-                for u in range(2):
-                    nc.scalar.copy(out=dst[:, u], in_=first_wo[u][:].rearrange("p j (m b e) -> p b m j e", b=2, e=2))
-            elif key[0] == "wo":
-                src = raw[key].rearrange("p j (m b e) -> p b m j e", b=2, e=2)
-                if name in SHARED:
-                    tiles = [sbuf([P, PACK * G], BF16, name)]
-                else:
-                    tiles = [bfs.tile([P, PACK * G], BF16, name="bf", align_bytes=64)]
-                dst = tiles[0][:].rearrange("p (b e m j) -> p b m j e", b=2, e=2, j=PACK)
-                if key == ROUNDED_ON_VECTOR:
-                    nc.vector.tensor_copy(out=dst, in_=src)
-                else:
-                    nc.scalar.copy(out=dst, in_=src)
-            else:
-                src = raw[key].rearrange("p j (u t i) -> p u t j i", t=PACK, i=2)
-                if key in QUANTISED_IN_HALVES:
-                    tiles = [sbuf([P, 2 * G], BF16, "%s_%d" % (name, b)) for b in range(2)]
-                    dsts = [tile[:].rearrange("p (t u i j) -> p u t j i", t=2, i=2, j=PACK) for tile in tiles]
-                    nc.scalar.copy(out=dsts[0], in_=src[:, :, 0:2])
-                    nc.vector.tensor_copy(out=dsts[1], in_=src[:, :, 2:4])
-                else:
-                    if name in SHARED:
-                        tiles = [sbuf([P, PACK * G], BF16, name)]
-                    else:
-                        tiles = [bfs.tile([P, PACK * G], BF16, name="bf", align_bytes=64)]
-                    nc.scalar.copy(out=tiles[0][:].rearrange("p (t u i j) -> p u t j i", t=PACK, i=2, j=PACK), in_=src)
-            rounded[key] = [tile[:] for tile in tiles]
+        def round_first_stage(*key):
+            src = raw[key][:].rearrange("p j (u t i) -> p u t j i", t=PACK, i=2)
+            tile = sbuf([P, PACK * G], BF16, "bf_%s_%d_%d" % key, bfs)
+            nc.scalar.copy(out=tile[:].rearrange("p (t u i j) -> p u t j i", t=PACK, i=2, j=PACK), in_=src)
+            rounded[key] = [tile]
+
+        def round_on_both(*key):
+            src = raw[key][:].rearrange("p j (u t i) -> p u t j i", t=PACK, i=2)
+            tiles = [sbuf([P, 2 * G], BF16, "bf_%s_%d_%d_%d" % (key + (b,))) for b in range(2)]
+            dsts = [tile[:].rearrange("p (t u i j) -> p u t j i", t=2, i=2, j=PACK) for tile in tiles]
+            nc.scalar.copy(out=dsts[0], in_=src[:, :, 0:2])
+            nc.vector.tensor_copy(out=dsts[1], in_=src[:, :, 2:4])
+            rounded[key] = tiles
+
+        def round_wo(a, g, copy):
+            tile = sbuf([P, PACK * G], BF16, "bf_wo_%d_%d" % (a, g), bfs)
+            copy(out=tile[:].rearrange("p (b e m j) -> p b m j e", b=2, e=2, j=PACK),
+                 in_=raw["wo", a, g][:].rearrange("p j (m b e) -> p b m j e", b=2, e=2))
+            rounded["wo", a, g] = [tile]
+
+        def round_wo_part(tile, u, copy):
+            dst = tile[:].rearrange("p (b e u m j) -> p u b m j e", b=2, e=2, u=2, j=PACK)
+            copy(out=dst[:, u], in_=wo_split[u][:].rearrange("p j (m b e) -> p b m j e", b=2, e=2))
 
         def quantise_weight(*key):
             codes[key] = sbuf([P, G], U32, "codes_%s_%d_%d" % key)
             scales[key] = sbuf([P, G], U8, "scales_%s_%d_%d" % key)
             width = G // len(rounded[key])
             for b, part in enumerate(rounded[key]):
-                cols = slice(width * b, width * (b + 1))
-                nc.vector.quantize_mx(
-                    out=codes[key][:, cols].bitcast(FP8X4), scales=scales[key][:, cols], in_=part)
+                span = slice(width * b, width * (b + 1))
+                nc.vector.quantize_mx(out=codes[key][:, span].bitcast(FP8X4), scales=scales[key][:, span], in_=part[:])
 
-        v2_w, taken = {}, {}
-        word_ps, sense_ps, word, gate, h_bf, h_codes, h_scales = {}, {}, {}, {}, {}, {}, {}
-        dom_ps, y_ps, y, y_bf = {}, {}, {}, {}
+        def weight(key, t):
+            return dict(lhsT=codes[key][:, cols(t)].bitcast(FP8X4), lhsT_scale=scales[key][:, cols(t)])
+
+        v_w = [sbuf([P, S], U32, "v_w%d" % a) for a in range(2)]
+        v2_w = [sbuf([P, S], U32, "v2_w%d" % a) for a in range(2)]
+        word = [sbuf([P, 2, PACK, HALF], F32, "word%d" % g) for g in range(2)]
+        gate_1 = sbuf([P, 2, PACK, HALF], F32, "gate_1")
+        gate = {}
+        for half in range(2):
+            for pair in range(2):
+                gate[0, half, pair] = sbuf([P, 2, HALF], F32, "gate_0_%d_%d" % (half, pair))[:]
+                gate[1, half, pair] = gate_1[:, half, 2 * pair : 2 * pair + 2, :]
+        dom0 = sbuf([P, 2, PACK, HALF], F32, "dom0")
         y_scales = sbuf([P, 2, S], U8, "y_scales")
-
-        agree = {}
-        agree_whole = sbuf([P, 2, PACK, HALF], F32, "agree_1")
-        gate_whole = sbuf([P, 2, PACK, HALF], F32, "gate_1")
-        for t in range(PACK):
-            gate[0, t] = agree[0, t] = sbuf([P, 2, HALF], F32, "gate_0_%d" % t)[:]
-            gate[1, t] = gate_whole[:, :, t, :]
-            agree[1, t] = agree_whole[:, :, t, :]
-
-        def halves(ps):
-            return ps[:].rearrange("p (u j) -> p u j", u=2)
-
-        def word_pass(g, a):
-            for t in range(PACK):
-                cols = slice(P * t, P * (t + 1))
-                if a == 0:
-                    word_ps[g, t] = bank(WORD_BANKS[g][t])
-                nc.tensor.matmul_mx(
-                    out=word_ps[g, t][:],
-                    lhsT=codes["w1", a, g][:, cols].bitcast(FP8X4), lhsT_scale=scales["w1", a, g][:, cols],
-                    rhs=v_w[a][:].bitcast(FP8X4), rhs_scale=tab_plane[4 * a :, :], start=(a == 0), stop=(a == 1))
-
-        def keep_word(g):
-            word[g] = sbuf([P, 2, PACK, HALF], F32, "word%d" % g)
-            for t in range(PACK):
-                nc.scalar.copy(out=word[g][:, :, t, :], in_=halves(word_ps[g, t]))
+        word_ps, dom_ps, sense_ps, y_ps = {}, {}, {}, {}
+        taken, h_bf, h_codes, h_scales, y, y_bf = {}, {}, {}, {}, {}, {}
 
         def domain(g):
             for t in range(PACK):
-                cols = slice(P * t, P * (t + 1))
-                dom_ps[g, t] = bank(DOM_BANKS[g][t])
+                dom_ps[g, t] = bank(HIGH[t])
                 nc.tensor.matmul_mx(
-                    out=dom_ps[g, t][:], lhsT=codes["w3", 0, g][:, cols].bitcast(FP8X4),
-                    lhsT_scale=scales["w3", 0, g][:, cols],
+                    out=dom_ps[g, t][:], **weight(("w3", 0, g), t),
                     rhs=v3_w[:].bitcast(FP4X4), rhs_scale=tab3_plane[:], start=True, stop=True)
 
-        def agreement(g, slices):
-            for t in slices:
-                nc.vector.scalar_tensor_tensor(
-                    out=agree[g, t], in0=halves(dom_ps[g, t]), scalar=bd_sb[:, g, 2 * t : 2 * t + 1],
-                    in1=word[g][:, :, t, :], op0=ALU.add, op1=ALU.mult)
-                nc.scalar.activation(gate[g, t], agree[g, t], ACT.Tanh)
+        def word0_pass(a, half):
+            for pair in range(2):
+                if a == 0:
+                    word_ps[0, half, pair] = bank(LOW[2 * half + pair])
+                for e in range(2):
+                    nc.tensor.matmul_mx(
+                        out=word_ps[0, half, pair][:, slots(e)], **weight(("w1", a, 0), 2 * pair + e),
+                        rhs=v_w[a][:, slots(half)].bitcast(FP8X4), rhs_scale=tab_plane[a][4 * a :, slots(half)],
+                        start=(a == 0 and e == 0), stop=(a == 1 and e == 1))
 
-        def sense_pass(g, a):
+        def word1_pass(a):
             for t in range(PACK):
                 if a == 0:
-                    sense_ps[g, t] = bank(SENSE_BANKS[g][t])
+                    word_ps[1, t] = bank(LOW[t])
                 nc.tensor.matmul_mx(
-                    out=sense_ps[g, t][:],
-                    lhsT=w2_dealt_w[:, a, g, t, :].bitcast(FP4X4), lhsT_scale=w2_dealt_s[:, a, g, t, :],
-                    rhs=v2_w[a][:].bitcast(FP8X4), rhs_scale=tab2_plane[a][:], start=(a == 0), stop=(a == 1))
+                    out=word_ps[1, t][:], **weight(("w1", a, 1), t),
+                    rhs=v_w[a][:].bitcast(FP8X4), rhs_scale=tab_plane[a][4 * a :, :], start=(a == 0), stop=(a == 1))
 
-        def sense_by_halves(g):
-            for half in range(2):
-                slots = slice(HALF * half, HALF * (half + 1))
-                for pair in range(2):
-                    sense_ps[g, half, pair] = bank(SENSE_BANKS[g][2 * half + pair])
-                    for a in range(2):
-                        for e in range(2):
-                            t = 2 * pair + e
-                            nc.tensor.matmul_mx(
-                                out=sense_ps[g, half, pair][:, HALF * e : HALF * (e + 1)],
-                                lhsT=w2_dealt_w[:, a, g, t, :].bitcast(FP4X4), lhsT_scale=w2_dealt_s[:, a, g, t, :],
-                                rhs=v2_w[a][:, slots].bitcast(FP8X4), rhs_scale=tab2_plane[a][:, slots],
-                                start=(a == 0 and e == 0), stop=(a == 1 and e == 1))
+        def sense_pass(g, a, half, banks):
+            for pair in range(2):
+                if a == 0:
+                    sense_ps[g, half, pair] = bank(banks[2 * half + pair])
+                for e in range(2):
+                    t = 2 * pair + e
+                    nc.tensor.matmul_mx(
+                        out=sense_ps[g, half, pair][:, slots(e)],
+                        lhsT=w2_dealt_w[:, a, g, t, :].bitcast(FP4X4), lhsT_scale=w2_dealt_s[:, a, g, t, :],
+                        rhs=v2_w[a][:, slots(half)].bitcast(FP8X4), rhs_scale=tab2_plane[a][:, slots(half)],
+                        start=(a == 0 and e == 0), stop=(a == 1 and e == 1))
 
         def gated_sense(g, half):
-            taken[g, half] = sbuf([P, PACK, HALF], F32, "taken_%d_%d" % (g, half))
             for pair in range(2):
-                slices = slice(2 * pair, 2 * pair + 2)
+                both = slice(2 * pair, 2 * pair + 2)
                 nc.vector.tensor_tensor(
-                    out=taken[g, half][:, slices, :], in0=halves(sense_ps[g, half, pair]),
-                    in1=gate_whole[:, half, slices, :], op=ALU.mult)
-
-        def gated_sense_whole(g):
-            both = sbuf([P, 2, PACK, HALF], F32, "taken_%d" % g)
-            for t in range(PACK):
-                nc.vector.tensor_tensor(
-                    out=both[:, :, t, :], in0=halves(sense_ps[g, t]), in1=gate[g, t], op=ALU.mult)
-            for half in range(2):
-                taken[g, half] = both[:, half]
+                    out=taken[g, half][:, both, :], in0=two(sense_ps[g, half, pair]),
+                    in1=gate[g, half, pair], op=ALU.mult)
 
         def finish_h(g, half):
             h_bf[g, half] = sbuf([P, PACK * HALF], BF16, "h_bf_%d_%d" % (g, half))
             nc.vector.tensor_tensor(
                 out=h_bf[g, half][:].rearrange("p (c i t) -> p c t i", i=4, t=PACK),
                 in0=word[g][:, half].rearrange("p t (c i) -> p c t i", i=4),
-                in1=taken[g, half][:, :, :].rearrange("p t (c i) -> p c t i", i=4),
+                in1=taken[g, half].rearrange("p t (c i) -> p c t i", i=4),
                 op=ALU.subtract)
 
         def quantise_h(g, half):
@@ -329,94 +300,127 @@ def tile_list_crossword_clue_features_kernel(
             nc.vector.quantize_mx(
                 out=h_codes[g, half][:].bitcast(FP8X4), scales=h_scales[g, half][:], in_=h_bf[g, half][:])
 
-        def out_pass(half, g, pair, a):
-            if a == 0:
-                y_ps[half, g, pair] = bank(Y_BANKS[half][2 * g + pair])
-            for e in range(2):
-                cols = slice(P * (2 * pair + e), P * (2 * pair + e + 1))
-                nc.tensor.matmul_mx(
-                    out=y_ps[half, g, pair][:, HALF * e : HALF * (e + 1)],
-                    lhsT=codes["wo", a, g][:, cols].bitcast(FP8X4), lhsT_scale=scales["wo", a, g][:, cols],
-                    rhs=h_codes[a, half][:].bitcast(FP8X4), rhs_scale=h_scales[a, half][:],
-                    start=(a == 0 and e == 0), stop=(a == 1 and e == 1))
+        def out_pass(half, g, a):
+            for pair in range(2):
+                if a == 0:
+                    y_ps[half, g, pair] = bank((HIGH, LOW)[half][2 * g + pair])
+                for e in range(2):
+                    nc.tensor.matmul_mx(
+                        out=y_ps[half, g, pair][:, slots(e)], **weight(("wo", a, g), 2 * pair + e),
+                        rhs=h_codes[a, half][:].bitcast(FP8X4), rhs_scale=h_scales[a, half][:],
+                        start=(a == 0 and e == 0), stop=(a == 1 and e == 1))
 
         def gain_and_store(half, g):
             y[half, g] = sbuf([P, PACK, HALF], F32, "y_%d_%d" % (half, g))
             for t in range(PACK):
                 nc.scalar.activation(
-                    y[half, g][:, t, :], y_ps[half, g, t // 2][:, HALF * (t % 2) : HALF * (t % 2 + 1)],
+                    y[half, g][:, t, :], y_ps[half, g, t // 2][:, slots(t % 2)],
                     ACT.Copy, scale=go_sb[:, g, t : t + 1])
-            rows = out_0[G * g : G * (g + 1), HALF * half : HALF * (half + 1)]
+            rows = out_0[G * g : G * (g + 1), slots(half)]
             nc.sync.dma_start(out=rows.rearrange("(p t) j -> p t j", t=PACK), in_=y[half, g][:])
 
         def quantise_y(half, g):
-            slots = slice(HALF * half, HALF * (half + 1))
             y_bf[half, g] = sbuf([P, PACK * HALF], BF16, "y_bf_%d_%d" % (half, g))
             nc.vector.tensor_copy(
                 out=y_bf[half, g][:].rearrange("p (c i t) -> p c t i", i=4, t=PACK),
                 in_=y[half, g][:].rearrange("p t (c i) -> p c t i", i=4))
             y_codes = sbuf([P, HALF], U32, "y_codes_%d_%d" % (half, g))
             nc.vector.quantize_mx(
-                out=y_codes[:].bitcast(FP8X4), scales=y_scales[:, g, slots], in_=y_bf[half, g][:])
+                out=y_codes[:].bitcast(FP8X4), scales=y_scales[:, g, slots(half)], in_=y_bf[half, g][:])
             nc.sync.dma_start(
-                out=out_1[g, :, slots, :].rearrange("p m t -> p (m t)").bitcast(I32),
+                out=out_1[g, :, slots(half), :].rearrange("p m t -> p (m t)").bitcast(I32),
                 in_=y_codes[:].bitcast(I32))
 
-        round_weight("w1", 0, 0)
-        quantise_weight("w1", 0, 0)
-        v_w[0] = gather(tab_w[0][:], list1, U32, "v_w0")
-        word_pass(0, 0)
-        round_weight("w3", 0, 0)
-        quantise_weight("w3", 0, 0)
+        for key in (("w3", 0, 0), ("w1", 0, 0)):
+            round_first_stage(*key)
+            quantise_weight(*key)
         domain(0)
-        round_weight("w1", 1, 0)
+        for t in range(PACK):
+            nc.scalar.activation(
+                dom0[:, :, t, :], two(dom_ps[0, t]), ACT.Identity, bias=bd_sb[:, 0, 2 * t : 2 * t + 1])
+        nc.vector.tensor_copy(v_w[0][:], tab_w[0][:].indirect(list1[:]))
+        for half in range(2):
+            word0_pass(0, half)
+        round_on_both("w1", 1, 0)
         quantise_weight("w1", 1, 0)
-        v_w[1] = gather(tab_w[1][:], list1, U32, "v_w1")
-        word_pass(0, 1)
-        keep_word(0)
-        w2_dealt_w = deal_w2(w2_w, U16, I32, "w2_dealt_w")
-        agreement(0, (0, 1))
-        v2_w[0] = gather(tab2_w[0][:], list2, U32, "v2_w0")
-        agreement(0, (2, 3))
+        for half in range(2):
+            gather_half(v_w[1], tab_w[1], list1, half)
+            word0_pass(1, half)
+        w2_dealt_w = deal_w2(w2_w, U16, U32, "w2_dealt_w", nc.scalar.copy)
+        for half in range(2):
+            for pair in range(2):
+                if half == 1 and pair == 1:
+                    for u in range(2):
+                        gather_half(v2_w[0], tab2_w[0], list2, u)
+                        sense_pass(0, 0, u, HIGH)
+                nc.vector.tensor_tensor(
+                    out=gate[0, half, pair], in0=two(word_ps[0, half, pair]),
+                    in1=dom0[:, half, 2 * pair : 2 * pair + 2, :], op=ALU.mult)
+                nc.scalar.activation(gate[0, half, pair], gate[0, half, pair], ACT.Tanh)
+        for half in range(2):
+            for pair in range(2):
+                nc.scalar.copy(out=word[0][:, half, 2 * pair : 2 * pair + 2, :], in_=two(word_ps[0, half, pair]))
+        for half in range(2):
+            gather_half(v2_w[1], tab2_w[1], list2, half)
+            sense_pass(0, 1, half, HIGH)
+        taken_0 = sbuf([P, 2, PACK, HALF], F32, "taken_0")
+        for half in range(2):
+            taken[0, half] = taken_0[:, half]
+            gated_sense(0, half)
 
-        sense_pass(0, 0)
-        v2_w[1] = gather(tab2_w[1][:], list2, U32, "v2_w1")
-        sense_pass(0, 1)
-        gated_sense_whole(0)
-        for a in range(2):
-            round_weight("w1", a, 1)
-            quantise_weight("w1", a, 1)
-            word_pass(1, a)
-        round_weight("w3", 0, 1)
-        keep_word(1)
+        round_first_stage("w3", 0, 1)
         quantise_weight("w3", 0, 1)
         domain(1)
-        agreement(1, range(PACK))
-        sense_by_halves(1)
+        finish_h(0, 0)
+        round_first_stage("w1", 0, 1)
+        quantise_weight("w1", 0, 1)
+        word1_pass(0)
+        quantise_h(0, 0)
+        round_on_both("w1", 1, 1)
+        quantise_weight("w1", 1, 1)
+        word1_pass(1)
+        finish_h(0, 1)
+        quantise_h(0, 1)
+        bf_wo_split = sbuf([P, PACK * G], BF16, "bf_wo_1_0", bfs)
+        rounded["wo", 1, 0] = [bf_wo_split]
+        round_wo_part(bf_wo_split, 0, nc.scalar.copy)
+        for t in range(PACK):
+            nc.scalar.copy(out=word[1][:, :, t, :], in_=two(word_ps[1, t]))
+        for t in range(PACK):
+            nc.vector.scalar_tensor_tensor(
+                out=gate_1[:, :, t, :], in0=two(dom_ps[1, t]), scalar=bd_sb[:, 1, 2 * t : 2 * t + 1],
+                in1=word[1][:, :, t, :], op0=ALU.add, op1=ALU.mult)
+            nc.scalar.activation(gate_1[:, :, t, :], gate_1[:, :, t, :], ACT.Tanh)
         for half in range(2):
-            finish_h(0, half)
-            quantise_h(0, half)
-        for g in range(2):
             for a in range(2):
-                round_weight("wo", a, g)
-        quantise_weight("wo", 1, 0)
+                sense_pass(1, a, half, LOW)
+        round_wo_part(bf_wo_split, 1, nc.vector.tensor_copy)
+        round_wo(0, 0, nc.vector.tensor_copy)
+        for a in range(2):
+            round_wo(a, 1, nc.scalar.copy)
 
         for half in range(2):
-            gated_sense(1, half)
-            if half == 0:
-                quantise_weight("wo", 0, 0)
-                finish_h(1, half)
-                for a in range(2):
-                    quantise_weight("wo", a, 1)
+            taken[1, half] = sbuf([P, PACK, HALF], F32, "taken_1_%d" % half)[:]
+        gated_sense(1, 0)
+        quantise_weight("wo", 0, 0)
+        for half in range(2):
+            out_pass(half, 0, 0)
+        finish_h(1, 0)
+        quantise_weight("wo", 1, 0)
+        quantise_h(1, 0)
+        out_pass(0, 0, 1)
+        gated_sense(1, 1)
+        quantise_weight("wo", 0, 1)
+        for half in range(2):
+            out_pass(half, 1, 0)
+        quantise_weight("wo", 1, 1)
+        out_pass(0, 1, 1)
+        finish_h(1, 1)
+        quantise_h(1, 1)
+        for g in range(2):
+            out_pass(1, g, 1)
+        for half in range(2):
             for g in range(2):
-                for pair in range(2):
-                    out_pass(half, g, pair, 0)
-            if half == 1:
-                finish_h(1, half)
-            quantise_h(1, half)
-            for g in range(2):
-                for pair in range(2):
-                    out_pass(half, g, pair, 1)
                 gain_and_store(half, g)
         for half in range(2):
             for g in range(2):

@@ -23,7 +23,7 @@ HALF = S // 2
 KIB = 1024
 
 SHARED = {
-    "bf_w3_0_1": 0, "h_bf_0_0": 0,
+    "bf_w3_0_1": 0, "h_codes_0_0": 0,
     "bf_w1_1_1_0": 4 * KIB, "bf_w1_1_1_1": 6 * KIB, "h_bf_0_1": 5 * KIB,
     "raw_wo_1_0_0": 8 * KIB, "word1": 8 * KIB,
     "raw_wo_0_0": 16 * KIB, "taken_1_0": 16 * KIB, "taken_1_1": 20 * KIB,
@@ -368,14 +368,14 @@ def tile_list_crossword_clue_features_kernel(
             taken[0, half] = taken_0[:, half]
             gated_sense(0, half)
 
+        finish_h(0, 0)
         round_first_stage("w3", 0, 1)
         quantise_weight("w3", 0, 1)
         domain(1)
-        finish_h(0, 0)
+        quantise_h(0, 0)
         round_first_stage("w1", 0, 1)
         quantise_weight("w1", 0, 1)
         word1_pass(0)
-        quantise_h(0, 0)
         round_on_both("w1", 1, 1)
         quantise_weight("w1", 1, 1)
         word1_pass(1)
@@ -394,7 +394,7 @@ def tile_list_crossword_clue_features_kernel(
         for half in range(2):
             for a in range(2):
                 sense_pass(1, a, half, LOW)
-        round_wo_part(bf_wo_split, 1, nc.vector.tensor_copy)
+        round_wo_part(bf_wo_split, 1, nc.scalar.copy)
         round_wo(0, 0, nc.vector.tensor_copy)
         for a in range(2):
             round_wo(a, 1, nc.scalar.copy)

@@ -84,7 +84,7 @@ def tile_list_crossword_clue_features_kernel(
         tab_plane = [sbuf([P, S], U8, "tab_plane%d" % a) for a in range(2)]
         tab2_plane = [sbuf([P, S], U8, "tab2_plane%d" % a) for a in range(2)]
         tab3_plane = sbuf([P, S], U8, "tab3_plane")
-        w2_w = sbuf([P, 2, H], U16, "w2_w")
+        w2_w = [sbuf([P, 2, G], U16, "w2_w%d" % g) for g in range(2)]
         w2_s = sbuf([P, 2, H], U8, "w2_s")
         go_sb = sbuf([P, 2, PACK], F32, "go_sb")
         bd_sb = sbuf([P, 2, 2 * PACK], F32, "bd_sb")
@@ -136,11 +136,17 @@ def tile_list_crossword_clue_features_kernel(
                     out=plane[first + c : P : 32, :].bitcast(I32),
                     in_=picked[name][8 * c + 4 * a : P : 32, :].bitcast(I32))
 
-        def deal_w2(src, dtype, pair_dtype, name, copy):
-            dst = sbuf([P, 2, 2, PACK, P], dtype, name)
+        def load_w2_words(g):
+            rows = w2_words.bitcast(I32).rearrange("a p (g c) -> g p a c", g=2)
+            nc.sync.dma_start(out=w2_w[g][:].bitcast(I32), in_=rows[g])
+
+        def deal_w2(src, dtype, pair_dtype, name, copy, run):
+            blocks = src.shape[1] * src.shape[2] // G
+            dst = sbuf([P, blocks, PACK, P], dtype, name)
+            pairs_in = src[:].rearrange("p a c -> p (a c)").bitcast(pair_dtype)
             copy(
-                out=dst[:].rearrange("p a g t m -> p (a g) t m").bitcast(pair_dtype),
-                in_=src[:].rearrange("p a c -> p (a c)").bitcast(pair_dtype).rearrange("p (x u t) -> p x t u", x=4, t=PACK))
+                out=dst[:].bitcast(pair_dtype).rearrange("p x t (c i) -> p x c t i", i=run),
+                in_=pairs_in.rearrange("p (x c i t) -> p x c t i", x=blocks, i=run, t=PACK))
             return dst
 
         nc.sync.dma_start(list3[:], offs3)
@@ -170,10 +176,10 @@ def tile_list_crossword_clue_features_kernel(
         place_scales("tab", 1, (2, 3), tab_plane[1], 4)
         place_scales("tab2", 0, (1, 2), tab2_plane[0], 0)
         load_words(tab_w[1], tab_words, 1)
-        nc.sync.dma_start(out=w2_w[:].bitcast(I32), in_=w2_words.bitcast(I32).rearrange("a p c -> p a c"))
+        load_w2_words(0)
         place_scales("tab2", 0, (3,), tab2_plane[0], 0)
-        w2_dealt_s = deal_w2(w2_s, U8, U16, "w2_dealt_s", nc.vector.tensor_copy)
-        dealt_rows = w2_dealt_s[:].rearrange("p a g t m -> p (a g t m)").bitcast(I32)
+        w2_dealt_s = deal_w2(w2_s, U8, U16, "w2_dealt_s", nc.vector.tensor_copy, 8)
+        dealt_rows = w2_dealt_s[:].rearrange("p x t m -> p (x t m)").bitcast(I32)
         for c in range(1, 4):
             nc.sync.dma_start(out=dealt_rows[c:P:32], in_=dealt_rows[8 * c : P : 32])
         place_scales("tab2", 1, (0,), tab2_plane[1], 0)
@@ -183,6 +189,7 @@ def tile_list_crossword_clue_features_kernel(
         load_weight("w3", w3, 0, 1)
         for a in range(2):
             load_weight("w1", w1, a, 1)
+        load_w2_words(1)
         wo_split = [sbuf([P, PACK, G // 2], F32, "raw_wo_1_0_%d" % u) for u in range(2)]
         for u in range(2):
             load_wo(wo_split[u], 1, G // 2 * u, G // 2)
@@ -275,7 +282,7 @@ def tile_list_crossword_clue_features_kernel(
                     t = 2 * pair + e
                     nc.tensor.matmul_mx(
                         out=sense_ps[g, half, pair][:, slots(e)],
-                        lhsT=w2_dealt_w[:, a, g, t, :].bitcast(FP4X4), lhsT_scale=w2_dealt_s[:, a, g, t, :],
+                        lhsT=w2_dealt_w[g][:, a, t, :].bitcast(FP4X4), lhsT_scale=w2_dealt_s[:, 2 * a + g, t, :],
                         rhs=v2_w[a][:, slots(half)].bitcast(FP8X4), rhs_scale=tab2_plane[a][:, slots(half)],
                         start=(a == 0 and e == 0), stop=(a == 1 and e == 1))
 
@@ -346,7 +353,7 @@ def tile_list_crossword_clue_features_kernel(
         for half in range(2):
             gather_half(v_w[1], tab_w[1], list1, half)
             word0_pass(1, half)
-        w2_dealt_w = deal_w2(w2_w, U16, U32, "w2_dealt_w", nc.scalar.copy)
+        w2_dealt_w = [deal_w2(w2_w[0], U16, U32, "w2_dealt_w0", nc.scalar.copy, 4)]
         for half in range(2):
             for pair in range(2):
                 if half == 1 and pair == 1:
@@ -380,6 +387,7 @@ def tile_list_crossword_clue_features_kernel(
         quantise_weight("w1", 1, 1)
         word1_pass(1)
         finish_h(0, 1)
+        w2_dealt_w.append(deal_w2(w2_w[1], U16, I32, "w2_dealt_w1", nc.vector.tensor_copy, 4))
         quantise_h(0, 1)
         bf_wo_split = sbuf([P, PACK * G], BF16, "bf_wo_1_0", bfs)
         rounded["wo", 1, 0] = [bf_wo_split]

@@ -30,6 +30,7 @@ SHARED = {
     "bf_wo_0_0": 24 * KIB, "codes_wo_1_0": 24 * KIB,
     "bf_wo_1_1": 28 * KIB, "h_bf_1_1": 28 * KIB, "y_bf_0_0": 28 * KIB,
     "raw_wo_1_1": 32 * KIB, "y_0_0": 32 * KIB,
+    "tab_s": 72 * KIB, "v3_w": 72 * KIB,
     "tab_w0": 40 * KIB, "taken_0": 40 * KIB,
     "tab_w1": 48 * KIB, "gate_1": 48 * KIB,
     "tab2_w0": 56 * KIB, "gate_0_1_1": 56 * KIB, "y_0_1": 56 * KIB, "y_1_0": 60 * KIB,
@@ -81,7 +82,7 @@ def tile_list_crossword_clue_features_kernel(
         tab_s = sbuf([P, T], U8, "tab_s")
         tab2_s = sbuf([P, T2], U8, "tab2_s")
         tab3_s = sbuf([P, T3], U8, "tab3_s")
-        tab_plane = [sbuf([P, S], U8, "tab_plane%d" % a) for a in range(2)]
+        tab_plane = sbuf([P, S], U8, "tab_plane")
         tab2_plane = [sbuf([P, S], U8, "tab2_plane%d" % a) for a in range(2)]
         tab3_plane = sbuf([P, S], U8, "tab3_plane")
         w2_w = [sbuf([P, 2, G], U16, "w2_w%d" % g) for g in range(2)]
@@ -89,8 +90,8 @@ def tile_list_crossword_clue_features_kernel(
         go_sb = sbuf([P, 2, PACK], F32, "go_sb")
         bd_sb = sbuf([P, 2, 2 * PACK], F32, "bd_sb")
 
-        nc.gpsimd.memset(tab3_s[:].bitcast(I32), 0)
         nc.gpsimd.memset(tab_s[:].bitcast(I32), 0)
+        nc.gpsimd.memset(tab3_s[:].bitcast(I32), 0)
         nc.vector.memset(tab2_s[:].bitcast(I32), 0)
         nc.gpsimd.memset(w2_s[:].rearrange("p a c -> p (a c)").bitcast(I32), 0)
         nc.gpsimd.memset(tab2_plane[1][:].bitcast(I32), 0)
@@ -151,40 +152,36 @@ def tile_list_crossword_clue_features_kernel(
 
         nc.sync.dma_start(list3[:], offs3)
         nc.sync.dma_start(out=tab3_w[:].bitcast(I32), in_=tab3_words[0].bitcast(I32))
-        load_scale_rows(tab3_s, tab3_scales, 0)
         nc.sync.dma_start(list1[:], offs)
         for a in range(2):
             load_scale_rows(tab_s, tab_scales, a)
-        load_weight("w3", w3, 0, 0)
+        load_weight("w1", w1, 0, 0)
+        load_scale_rows(tab3_s, tab3_scales, 0)
+        for i in range(2):
+            load_bias(i)
         nc.sync.dma_start(list2[:], offs2)
         for a in range(2):
             load_scale_rows(tab2_s, tab2_scales, a)
-        for i in range(2):
-            load_bias(i)
-        load_weight("w1", w1, 0, 0)
-        nc.sync.dma_start(out=w2_s[0:P:8].bitcast(I32), in_=w2_scales.bitcast(I32).rearrange("a q w -> q a w"))
-        v3_w = gather(tab3_w, list3, U16, "v3_w")
-        pick_scales("tab3", tab3_s, list3, tab3_plane)
-        pick_scales("tab", tab_s, list1, tab_plane[0])
-        nc.vector.tensor_copy(out=tab_plane[1][:].bitcast(I32), in_=picked["tab"][:].bitcast(I32))
-        pick_scales("tab2", tab2_s, list2, tab2_plane[0])
-        place_scales("tab3", 0, (1, 2, 3), tab3_plane, 0)
         load_words(tab_w[0], tab_words, 0)
-        place_scales("tab", 0, (1, 2, 3), tab_plane[0], 0)
-        place_scales("tab", 1, (1,), tab_plane[1], 4)
+        nc.sync.dma_start(out=w2_s[0:P:8].bitcast(I32), in_=w2_scales.bitcast(I32).rearrange("a q w -> q a w"))
+        pick_scales("tab", tab_s, list1, tab_plane)
+        v3_w = gather(tab3_w, list3, U16, "v3_w")
+        place_scales("tab", 0, (1, 2, 3), tab_plane, 0)
+        load_weight("w3", w3, 0, 0)
+        place_scales("tab", 1, (1, 2, 3), tab_plane, 4)
         load_weight("w1", w1, 1, 0)
-        place_scales("tab", 1, (2, 3), tab_plane[1], 4)
-        place_scales("tab2", 0, (1, 2), tab2_plane[0], 0)
+        pick_scales("tab3", tab3_s, list3, tab3_plane)
+        place_scales("tab3", 0, (1, 2, 3), tab3_plane, 0)
+        pick_scales("tab2", tab2_s, list2, tab2_plane[0])
+        place_scales("tab2", 0, (1, 2, 3), tab2_plane[0], 0)
         load_words(tab_w[1], tab_words, 1)
         load_w2_words(0)
-        place_scales("tab2", 0, (3,), tab2_plane[0], 0)
         w2_dealt_s = deal_w2(w2_s, U8, U16, "w2_dealt_s", nc.vector.tensor_copy, 8)
         dealt_rows = w2_dealt_s[:].rearrange("p x t m -> p (x t m)").bitcast(I32)
         for c in range(1, 4):
             nc.sync.dma_start(out=dealt_rows[c:P:32], in_=dealt_rows[8 * c : P : 32])
-        place_scales("tab2", 1, (0,), tab2_plane[1], 0)
         load_words(tab2_w[0], tab2_words, 0)
-        place_scales("tab2", 1, (1, 2, 3), tab2_plane[1], 0)
+        place_scales("tab2", 1, (0, 1, 2, 3), tab2_plane[1], 0)
         load_words(tab2_w[1], tab2_words, 1)
         load_weight("w3", w3, 0, 1)
         for a in range(2):
@@ -263,7 +260,7 @@ def tile_list_crossword_clue_features_kernel(
                 for e in range(2):
                     nc.tensor.matmul_mx(
                         out=word_ps[0, half, pair][:, slots(e)], **weight(("w1", a, 0), 2 * pair + e),
-                        rhs=v_w[a][:, slots(half)].bitcast(FP8X4), rhs_scale=tab_plane[a][4 * a :, slots(half)],
+                        rhs=v_w[a][:, slots(half)].bitcast(FP8X4), rhs_scale=tab_plane[4 * a :, slots(half)],
                         start=(a == 0 and e == 0), stop=(a == 1 and e == 1))
 
         def word1_pass(a):
@@ -272,7 +269,7 @@ def tile_list_crossword_clue_features_kernel(
                     word_ps[1, t] = bank(LOW[t])
                 nc.tensor.matmul_mx(
                     out=word_ps[1, t][:], **weight(("w1", a, 1), t),
-                    rhs=v_w[a][:].bitcast(FP8X4), rhs_scale=tab_plane[a][4 * a :, :], start=(a == 0), stop=(a == 1))
+                    rhs=v_w[a][:].bitcast(FP8X4), rhs_scale=tab_plane[4 * a :, :], start=(a == 0), stop=(a == 1))
 
         def sense_pass(g, a, half, banks):
             for pair in range(2):
@@ -338,18 +335,19 @@ def tile_list_crossword_clue_features_kernel(
                 out=out_1[g, :, slots(half), :].rearrange("p m t -> p (m t)").bitcast(I32),
                 in_=y_codes[:].bitcast(I32))
 
-        for key in (("w3", 0, 0), ("w1", 0, 0)):
-            round_first_stage(*key)
-            quantise_weight(*key)
-        domain(0)
-        for t in range(PACK):
-            nc.scalar.activation(
-                dom0[:, :, t, :], two(dom_ps[0, t]), ACT.Identity, bias=bd_sb[:, 0, 2 * t : 2 * t + 1])
+        round_first_stage("w1", 0, 0)
+        quantise_weight("w1", 0, 0)
         nc.vector.tensor_copy(v_w[0][:], tab_w[0][:].indirect(list1[:]))
         for half in range(2):
             word0_pass(0, half)
+        round_first_stage("w3", 0, 0)
+        quantise_weight("w3", 0, 0)
+        domain(0)
         round_on_both("w1", 1, 0)
         quantise_weight("w1", 1, 0)
+        for t in range(PACK):
+            nc.scalar.activation(
+                dom0[:, :, t, :], two(dom_ps[0, t]), ACT.Identity, bias=bd_sb[:, 0, 2 * t : 2 * t + 1])
         for half in range(2):
             gather_half(v_w[1], tab_w[1], list1, half)
             word0_pass(1, half)

@@ -23,14 +23,14 @@ HALF = S // 2
 KIB = 1024
 
 SHARED = {
-    "bf_w3_0_1": 0, "h_codes_0_0": 0,
+    "bf_w3_0_1": 0, "h_bf_0_0": 0, "bf_w1_0_1": 76 * KIB, "h_codes_0_0": 76 * KIB,
     "bf_w1_1_1_0": 4 * KIB, "bf_w1_1_1_1": 6 * KIB, "h_bf_0_1": 5 * KIB,
     "raw_wo_1_0_0": 8 * KIB, "word1": 8 * KIB,
     "raw_wo_0_0": 16 * KIB, "taken_1_0": 16 * KIB, "taken_1_1": 20 * KIB,
     "bf_wo_0_0": 24 * KIB, "codes_wo_1_0": 24 * KIB,
     "bf_wo_1_1": 28 * KIB, "h_bf_1_1": 28 * KIB, "y_bf_0_0": 28 * KIB,
     "raw_wo_1_1": 32 * KIB, "y_0_0": 32 * KIB,
-    "tab_s": 72 * KIB, "v3_w": 72 * KIB,
+    "tab_s": 72 * KIB, "v3_w": 72 * KIB, "tab2_s": 74 * KIB, "codes_w1_0_0": 74 * KIB,
     "tab_w0": 40 * KIB, "taken_0": 40 * KIB,
     "tab_w1": 48 * KIB, "gate_1": 48 * KIB,
     "tab2_w0": 56 * KIB, "gate_0_1_1": 56 * KIB, "y_0_1": 56 * KIB, "y_1_0": 60 * KIB,
@@ -90,11 +90,9 @@ def tile_list_crossword_clue_features_kernel(
         go_sb = sbuf([P, 2, PACK], F32, "go_sb")
         bd_sb = sbuf([P, 2, 2 * PACK], F32, "bd_sb")
 
-        nc.gpsimd.memset(tab_s[:].bitcast(I32), 0)
-        nc.gpsimd.memset(tab3_s[:].bitcast(I32), 0)
-        nc.vector.memset(tab2_s[:].bitcast(I32), 0)
-        nc.gpsimd.memset(w2_s[:].rearrange("p a c -> p (a c)").bitcast(I32), 0)
-        nc.gpsimd.memset(tab2_plane[1][:].bitcast(I32), 0)
+        for tile in (tab_s, tab3_s, tab2_s, tab2_plane[1]):
+            nc.vector.memset(tile[:].bitcast(I32), 0)
+        nc.vector.memset(w2_s[:].rearrange("p a c -> p (a c)").bitcast(I32), 0)
 
         raw, picked = {}, {}
 
@@ -373,14 +371,14 @@ def tile_list_crossword_clue_features_kernel(
             taken[0, half] = taken_0[:, half]
             gated_sense(0, half)
 
-        finish_h(0, 0)
         round_first_stage("w3", 0, 1)
         quantise_weight("w3", 0, 1)
         domain(1)
-        quantise_h(0, 0)
+        finish_h(0, 0)
         round_first_stage("w1", 0, 1)
         quantise_weight("w1", 0, 1)
         word1_pass(0)
+        quantise_h(0, 0)
         round_on_both("w1", 1, 1)
         quantise_weight("w1", 1, 1)
         word1_pass(1)

@@ -23,8 +23,8 @@ HALF = S // 2
 KIB = 1024
 
 SHARED = {
-    "bf_w3_0_1": 0, "h_bf_0_0": 0, "bf_w1_0_1": 76 * KIB, "h_codes_0_0": 76 * KIB,
-    "bf_w1_1_1_0": 4 * KIB, "bf_w1_1_1_1": 6 * KIB, "h_bf_0_1": 5 * KIB,
+    "bf_w3_0_1": 0, "h_bf_0_0": 0,
+    "bf_w1_1_1_0": 4 * KIB, "bf_w1_1_1_1": 6 * KIB, "h_bf_0_1": 5 * KIB, "h_codes_0_0": 4 * KIB,
     "raw_wo_1_0_0": 8 * KIB, "word1": 8 * KIB,
     "raw_wo_0_0": 16 * KIB, "taken_1_0": 16 * KIB, "taken_1_1": 20 * KIB,
     "bf_wo_0_0": 24 * KIB, "codes_wo_1_0": 24 * KIB,
@@ -174,7 +174,7 @@ def tile_list_crossword_clue_features_kernel(
         place_scales("tab2", 0, (1, 2, 3), tab2_plane[0], 0)
         load_words(tab_w[1], tab_words, 1)
         load_w2_words(0)
-        w2_dealt_s = deal_w2(w2_s, U8, U16, "w2_dealt_s", nc.vector.tensor_copy, 8)
+        w2_dealt_s = deal_w2(w2_s, U8, U16, "w2_dealt_s", nc.scalar.copy, 8)
         dealt_rows = w2_dealt_s[:].rearrange("p x t m -> p (x t m)").bitcast(I32)
         for c in range(1, 4):
             nc.sync.dma_start(out=dealt_rows[c:P:32], in_=dealt_rows[8 * c : P : 32])
@@ -341,7 +341,7 @@ def tile_list_crossword_clue_features_kernel(
         round_first_stage("w3", 0, 0)
         quantise_weight("w3", 0, 0)
         domain(0)
-        round_on_both("w1", 1, 0)
+        round_first_stage("w1", 1, 0)
         quantise_weight("w1", 1, 0)
         for t in range(PACK):
             nc.scalar.activation(
@@ -378,13 +378,13 @@ def tile_list_crossword_clue_features_kernel(
         round_first_stage("w1", 0, 1)
         quantise_weight("w1", 0, 1)
         word1_pass(0)
-        quantise_h(0, 0)
         round_on_both("w1", 1, 1)
         quantise_weight("w1", 1, 1)
         word1_pass(1)
         finish_h(0, 1)
-        w2_dealt_w.append(deal_w2(w2_w[1], U16, I32, "w2_dealt_w1", nc.vector.tensor_copy, 4))
-        quantise_h(0, 1)
+        for half in range(2):
+            quantise_h(0, half)
+        w2_dealt_w.append(deal_w2(w2_w[1], U16, U32, "w2_dealt_w1", nc.scalar.copy, 4))
         bf_wo_split = sbuf([P, PACK * G], BF16, "bf_wo_1_0", bfs)
         rounded["wo", 1, 0] = [bf_wo_split]
         round_wo_part(bf_wo_split, 0, nc.scalar.copy)

@@ -30,7 +30,7 @@ SHARED = {
     "bf_wo_0_0": 24 * KIB, "codes_wo_1_0": 24 * KIB,
     "bf_wo_1_1": 28 * KIB, "h_bf_1_1": 28 * KIB, "y_bf_0_0": 28 * KIB,
     "raw_wo_1_1": 32 * KIB, "y_0_0": 32 * KIB,
-    "tab_s": 72 * KIB, "v3_w": 72 * KIB, "tab2_s": 74 * KIB, "codes_w1_0_0": 74 * KIB,
+    "tab_s": 72 * KIB, "v3_w": 72 * KIB,
     "tab_w0": 40 * KIB, "taken_0": 40 * KIB,
     "tab_w1": 48 * KIB, "gate_1": 48 * KIB,
     "tab2_w0": 56 * KIB, "gate_0_1_1": 56 * KIB, "y_0_1": 56 * KIB, "y_1_0": 60 * KIB,
@@ -80,19 +80,20 @@ def tile_list_crossword_clue_features_kernel(
         tab2_w = [sbuf([P, T2], U32, "tab2_w%d" % a) for a in range(2)]
         tab3_w = sbuf([P, T3], U16, "tab3_w")
         tab_s = sbuf([P, T], U8, "tab_s")
-        tab2_s = sbuf([P, T2], U8, "tab2_s")
+        tab2_s = sbuf([P, 2, T2], U8, "tab2_s")
         tab3_s = sbuf([P, T3], U8, "tab3_s")
         tab_plane = sbuf([P, S], U8, "tab_plane")
-        tab2_plane = [sbuf([P, S], U8, "tab2_plane%d" % a) for a in range(2)]
+        tab2_plane = sbuf([P, 2, S], U8, "tab2_plane")
         tab3_plane = sbuf([P, S], U8, "tab3_plane")
         w2_w = [sbuf([P, 2, G], U16, "w2_w%d" % g) for g in range(2)]
         w2_s = sbuf([P, 2, H], U8, "w2_s")
         go_sb = sbuf([P, 2, PACK], F32, "go_sb")
         bd_sb = sbuf([P, 2, 2 * PACK], F32, "bd_sb")
 
-        for tile in (tab_s, tab3_s, tab2_s, tab2_plane[1]):
+        for tile in (tab_s, tab3_s):
             nc.vector.memset(tile[:].bitcast(I32), 0)
-        nc.vector.memset(w2_s[:].rearrange("p a c -> p (a c)").bitcast(I32), 0)
+        for tile in (tab2_s, w2_s):
+            nc.vector.memset(tile[:].rearrange("p a c -> p (a c)").bitcast(I32), 0)
 
         raw, picked = {}, {}
 
@@ -158,8 +159,7 @@ def tile_list_crossword_clue_features_kernel(
         for i in range(2):
             load_bias(i)
         nc.sync.dma_start(list2[:], offs2)
-        for a in range(2):
-            load_scale_rows(tab2_s, tab2_scales, a)
+        nc.sync.dma_start(out=tab2_s[0:P:8].bitcast(I32), in_=tab2_scales.bitcast(I32).rearrange("a q w -> q a w"))
         load_words(tab_w[0], tab_words, 0)
         nc.sync.dma_start(out=w2_s[0:P:8].bitcast(I32), in_=w2_scales.bitcast(I32).rearrange("a q w -> q a w"))
         pick_scales("tab", tab_s, list1, tab_plane)
@@ -170,16 +170,21 @@ def tile_list_crossword_clue_features_kernel(
         load_weight("w1", w1, 1, 0)
         pick_scales("tab3", tab3_s, list3, tab3_plane)
         place_scales("tab3", 0, (1, 2, 3), tab3_plane, 0)
-        pick_scales("tab2", tab2_s, list2, tab2_plane[0])
-        place_scales("tab2", 0, (1, 2, 3), tab2_plane[0], 0)
-        load_words(tab_w[1], tab_words, 1)
-        load_w2_words(0)
+        picked2 = sbuf([P, 2, S], U8, "picked_tab2")
+        for a in range(2):
+            nc.vector.tensor_copy(picked2[:, a, :], tab2_s[:, a, :].indirect(list2[:]))
+        picked_rows = picked2[:].rearrange("p a j -> p (a j)").bitcast(I32)
+        plane_rows = tab2_plane[:].rearrange("p a j -> p (a j)").bitcast(I32)
+        nc.vector.tensor_copy(out=plane_rows, in_=picked_rows)
         w2_dealt_s = deal_w2(w2_s, U8, U16, "w2_dealt_s", nc.scalar.copy, 8)
         dealt_rows = w2_dealt_s[:].rearrange("p x t m -> p (x t m)").bitcast(I32)
         for c in range(1, 4):
             nc.sync.dma_start(out=dealt_rows[c:P:32], in_=dealt_rows[8 * c : P : 32])
+        load_words(tab_w[1], tab_words, 1)
+        load_w2_words(0)
+        for c in range(1, 4):
+            nc.sync.dma_start(out=plane_rows[c:P:32], in_=picked_rows[8 * c : P : 32])
         load_words(tab2_w[0], tab2_words, 0)
-        place_scales("tab2", 1, (0, 1, 2, 3), tab2_plane[1], 0)
         load_words(tab2_w[1], tab2_words, 1)
         load_weight("w3", w3, 0, 1)
         for a in range(2):
@@ -278,7 +283,7 @@ def tile_list_crossword_clue_features_kernel(
                     nc.tensor.matmul_mx(
                         out=sense_ps[g, half, pair][:, slots(e)],
                         lhsT=w2_dealt_w[g][:, a, t, :].bitcast(FP4X4), lhsT_scale=w2_dealt_s[:, 2 * a + g, t, :],
-                        rhs=v2_w[a][:, slots(half)].bitcast(FP8X4), rhs_scale=tab2_plane[a][:, slots(half)],
+                        rhs=v2_w[a][:, slots(half)].bitcast(FP8X4), rhs_scale=tab2_plane[:, a, slots(half)],
                         start=(a == 0 and e == 0), stop=(a == 1 and e == 1))
 
         def gated_sense(g, half):
@@ -312,23 +317,30 @@ def tile_list_crossword_clue_features_kernel(
                         rhs=h_codes[a, half][:].bitcast(FP8X4), rhs_scale=h_scales[a, half][:],
                         start=(a == 0 and e == 0), stop=(a == 1 and e == 1))
 
+        def parts(half, g):
+            width = HALF // 2 if (half, g) == (1, 1) else HALF
+            return [slice(first, first + width) for first in range(0, HALF, width)]
+
         def gain_and_store(half, g):
             y[half, g] = sbuf([P, PACK, HALF], F32, "y_%d_%d" % (half, g))
-            for t in range(PACK):
-                nc.scalar.activation(
-                    y[half, g][:, t, :], y_ps[half, g, t // 2][:, slots(t % 2)],
-                    ACT.Copy, scale=go_sb[:, g, t : t + 1])
+            for part in parts(half, g):
+                for t in range(PACK):
+                    nc.scalar.activation(
+                        y[half, g][:, t, part], two(y_ps[half, g, t // 2])[:, t % 2, part],
+                        ACT.Copy, scale=go_sb[:, g, t : t + 1])
             rows = out_0[G * g : G * (g + 1), slots(half)]
             nc.sync.dma_start(out=rows.rearrange("(p t) j -> p t j", t=PACK), in_=y[half, g][:])
 
         def quantise_y(half, g):
             y_bf[half, g] = sbuf([P, PACK * HALF], BF16, "y_bf_%d_%d" % (half, g))
-            nc.vector.tensor_copy(
-                out=y_bf[half, g][:].rearrange("p (c i t) -> p c t i", i=4, t=PACK),
-                in_=y[half, g][:].rearrange("p t (c i) -> p c t i", i=4))
             y_codes = sbuf([P, HALF], U32, "y_codes_%d_%d" % (half, g))
-            nc.vector.quantize_mx(
-                out=y_codes[:].bitcast(FP8X4), scales=y_scales[:, g, slots(half)], in_=y_bf[half, g][:])
+            for part in parts(half, g):
+                values = y_bf[half, g][:, PACK * part.start : PACK * part.stop]
+                nc.vector.tensor_copy(
+                    out=values.rearrange("p (c i t) -> p c t i", i=4, t=PACK),
+                    in_=y[half, g][:, :, part].rearrange("p t (c i) -> p c t i", i=4))
+                nc.vector.quantize_mx(
+                    out=y_codes[:, part].bitcast(FP8X4), scales=y_scales[:, g, slots(half)][:, part], in_=values)
             nc.sync.dma_start(
                 out=out_1[g, :, slots(half), :].rearrange("p m t -> p (m t)").bitcast(I32),
                 in_=y_codes[:].bitcast(I32))

@@ -92,7 +92,7 @@ def tile_list_crossword_clue_features_kernel(
 
         for tile in (tab_s, tab3_s):
             nc.vector.memset(tile[:].bitcast(I32), 0)
-        for tile in (tab2_s, w2_s):
+        for tile in (w2_s, tab2_s):
             nc.vector.memset(tile[:].rearrange("p a c -> p (a c)").bitcast(I32), 0)
 
         raw, picked = {}, {}
@@ -159,9 +159,9 @@ def tile_list_crossword_clue_features_kernel(
         for i in range(2):
             load_bias(i)
         nc.sync.dma_start(list2[:], offs2)
-        nc.sync.dma_start(out=tab2_s[0:P:8].bitcast(I32), in_=tab2_scales.bitcast(I32).rearrange("a q w -> q a w"))
-        load_words(tab_w[0], tab_words, 0)
         nc.sync.dma_start(out=w2_s[0:P:8].bitcast(I32), in_=w2_scales.bitcast(I32).rearrange("a q w -> q a w"))
+        load_words(tab_w[0], tab_words, 0)
+        nc.sync.dma_start(out=tab2_s[0:P:8].bitcast(I32), in_=tab2_scales.bitcast(I32).rearrange("a q w -> q a w"))
         pick_scales("tab", tab_s, list1, tab_plane)
         v3_w = gather(tab3_w, list3, U16, "v3_w")
         place_scales("tab", 0, (1, 2, 3), tab_plane, 0)
@@ -176,7 +176,7 @@ def tile_list_crossword_clue_features_kernel(
         picked_rows = picked2[:].rearrange("p a j -> p (a j)").bitcast(I32)
         plane_rows = tab2_plane[:].rearrange("p a j -> p (a j)").bitcast(I32)
         nc.vector.tensor_copy(out=plane_rows, in_=picked_rows)
-        w2_dealt_s = deal_w2(w2_s, U8, U16, "w2_dealt_s", nc.scalar.copy, 8)
+        w2_dealt_s = deal_w2(w2_s, U8, U16, "w2_dealt_s", nc.vector.tensor_copy, 8)
         dealt_rows = w2_dealt_s[:].rearrange("p x t m -> p (x t m)").bitcast(I32)
         for c in range(1, 4):
             nc.sync.dma_start(out=dealt_rows[c:P:32], in_=dealt_rows[8 * c : P : 32])
@@ -361,7 +361,7 @@ def tile_list_crossword_clue_features_kernel(
         for half in range(2):
             gather_half(v_w[1], tab_w[1], list1, half)
             word0_pass(1, half)
-        w2_dealt_w = [deal_w2(w2_w[0], U16, U32, "w2_dealt_w0", nc.scalar.copy, 4)]
+        w2_dealt_w = [deal_w2(w2_w[0], U16, U32, "w2_dealt_w0", nc.vector.tensor_copy, 4)]
         for half in range(2):
             for pair in range(2):
                 if half == 1 and pair == 1:
@@ -394,9 +394,9 @@ def tile_list_crossword_clue_features_kernel(
         quantise_weight("w1", 1, 1)
         word1_pass(1)
         finish_h(0, 1)
+        w2_dealt_w.append(deal_w2(w2_w[1], U16, U32, "w2_dealt_w1", nc.vector.tensor_copy, 4))
         for half in range(2):
             quantise_h(0, half)
-        w2_dealt_w.append(deal_w2(w2_w[1], U16, U32, "w2_dealt_w1", nc.scalar.copy, 4))
         bf_wo_split = sbuf([P, PACK * G], BF16, "bf_wo_1_0", bfs)
         rounded["wo", 1, 0] = [bf_wo_split]
         round_wo_part(bf_wo_split, 0, nc.scalar.copy)

from contextlib import ExitStack

import concourse.mybir as mybir

K, K3, H, N, T, T2, T3, S = 1024, 512, 1024, 1024, 2048, 2048, 1024, 512
FLOPS = 2 * S * (2 * K * H + K3 * H + H * N)

F32 = mybir.dt.float32
BF16 = mybir.dt.bfloat16
I32 = mybir.dt.int32
U32 = mybir.dt.uint32
U16 = mybir.dt.uint16
U8 = mybir.dt.uint8
FP8X4 = mybir.dt.float8_e4m3fn_x4
FP4X4 = mybir.dt.float4_e2m1fn_x4
ALU = mybir.AluOpType
ACT = mybir.ActivationFunctionType

P = 128
PACK = 4
G = P * PACK
HALF = S // 2
KIB = 1024

SHARED = {
    "bf_w3_0_1": 0, "h_bf_0_0": 0,
    "bf_w1_1_1_0": 4 * KIB, "bf_w1_1_1_1": 6 * KIB, "h_bf_0_1": 5 * KIB, "h_codes_0_0": 4 * KIB,
    "raw_wo_1_0_0": 8 * KIB, "word1": 8 * KIB,
    "raw_wo_0_0": 16 * KIB, "taken_1_0": 16 * KIB, "taken_1_1": 20 * KIB,
    "bf_wo_0_0": 24 * KIB, "codes_wo_1_0": 24 * KIB,
    "bf_wo_1_1": 28 * KIB, "h_bf_1_1": 28 * KIB, "y_bf_0_0": 28 * KIB,
    "raw_wo_1_1": 32 * KIB, "y_0_0": 32 * KIB,
    "tab_s": 72 * KIB, "v3_w": 72 * KIB,
    "tab_w0": 40 * KIB, "taken_0": 40 * KIB,
    "tab_w1": 48 * KIB, "gate_1": 48 * KIB,
    "tab2_w0": 56 * KIB, "gate_0_1_1": 56 * KIB, "y_0_1": 56 * KIB, "y_1_0": 60 * KIB,
    "tab2_w1": 64 * KIB, "y_1_1": 64 * KIB,
}

LOW, HIGH = (0, 1, 2, 3), (4, 5, 6, 7)


def tile_list_crossword_clue_features_kernel(
    tc, tab_words, tab_scales, tab2_words, tab2_scales, tab3_words, tab3_scales,
    offs, offs2, offs3, w1, w2_words, w2_scales, w3, bd, wo, go, out_0, out_1, out_2,
):
    nc = tc.nc
    with ExitStack() as ctx:
        lists = ctx.enter_context(tc.tile_pool(name="lists", bufs=1))
        keep = ctx.enter_context(tc.tile_pool(name="keep", bufs=1))
        raws = ctx.enter_context(tc.tile_pool(name="raws", bufs=3))
        bfs = ctx.enter_context(tc.tile_pool(name="bfs", bufs=3))
        shared = ctx.enter_context(tc.tile_pool(name="shared", bufs=1))
        psum = ctx.enter_context(tc.psum_pool(name="psum", bufs=1))

        def sbuf(shape, dtype, name, ring=None):
            if name in SHARED:
                return shared.tile(shape, dtype, name=name, align_bytes=64, offset=SHARED[name])
            if ring is not None:
                return ring.tile(shape, dtype, name="ring", align_bytes=64)
            return keep.tile(shape, dtype, name=name, align_bytes=64)

        def bank(b):
            return psum.tile([P, S], F32, name="bank%d" % b)

        def two(ps):
            return ps[:].rearrange("p (u j) -> p u j", u=2)

        def slots(half):
            return slice(HALF * half, HALF * (half + 1))

        def cols(t):
            return slice(P * t, P * (t + 1))

        list1 = lists.tile([P, S // 16], U16, name="list1")
        list2 = lists.tile([P, S // 16], U16, name="list2")
        list3 = lists.tile([P, S // 16], U16, name="list3")

        tab_w = [sbuf([P, T], U32, "tab_w%d" % a) for a in range(2)]
        tab2_w = [sbuf([P, T2], U32, "tab2_w%d" % a) for a in range(2)]
        tab3_w = sbuf([P, T3], U16, "tab3_w")
        tab_s = sbuf([P, T], U8, "tab_s")
        tab2_s = sbuf([P, 2, T2], U8, "tab2_s")
        tab3_s = sbuf([P, T3], U8, "tab3_s")
        tab_plane = sbuf([P, S], U8, "tab_plane")
        tab2_plane = sbuf([P, 2, S], U8, "tab2_plane")
        tab3_plane = sbuf([P, S], U8, "tab3_plane")
        w2_w = [sbuf([P, 2, G], U16, "w2_w%d" % g) for g in range(2)]
        w2_s = sbuf([P, 2, H], U8, "w2_s")
        go_sb = sbuf([P, 2, PACK], F32, "go_sb")
        bd_sb = sbuf([P, 2, 2 * PACK], F32, "bd_sb")

        for tile in (tab_s, tab3_s):
            nc.vector.memset(tile[:].bitcast(I32), 0)
        for tile in (w2_s, tab2_s):
            nc.vector.memset(tile[:].rearrange("p a c -> p (a c)").bitcast(I32), 0)

        raw, picked = {}, {}

        def load_weight(name, w, a, g):
            raw[name, a, g] = sbuf([P, PACK, G], F32, "raw_%s_%d_%d" % (name, a, g), raws)
            block = w[G * a : G * (a + 1), G * g : G * (g + 1)]
            nc.sync.dma_start(out=raw[name, a, g][:], in_=block.rearrange("(p j) c -> p j c", j=PACK))

        def load_wo(tile, a, first, width):
            rows = wo[G * a : G * (a + 1), first : first + width].rearrange("(u t i) c -> i u t c", t=PACK, i=2)
            for i in range(2):
                nc.sync.dma_start(out=tile[i:P:2], in_=rows[i])

        def load_words(dst, src, a):
            nc.sync.dma_start(out=dst[:].bitcast(I32), in_=src[a].rearrange("p c i -> p (c i)").bitcast(I32))

        def load_scale_rows(dst, src, a):
            nc.sync.dma_start(out=dst[4 * a : P : 8, :].bitcast(I32), in_=src[a].bitcast(I32))

        def load_bias(i):
            runs = bd.rearrange("(g u e) -> u g e", g=2, e=2 * PACK)[:, :, i : i + 7]
            nc.sync.dma_start(out=bd_sb[i:P:2, :, 0:7], in_=runs)

        def gather(window, offsets, dtype, name):
            dst = sbuf([P, S], dtype, name)
            nc.vector.tensor_copy(dst[:], window[:].indirect(offsets[:]))
            return dst

        def gather_half(dst, window, offsets, half):
            entries = slice(HALF // 16 * half, HALF // 16 * (half + 1))
            nc.vector.tensor_copy(dst[:, slots(half)], window[:].indirect(offsets[:, entries]))

        def pick_scales(name, window, offsets, plane):
            picked[name] = gather(window, offsets, U8, "picked_" + name)
            nc.vector.tensor_copy(out=plane[:].bitcast(I32), in_=picked[name][:].bitcast(I32))

        def place_scales(name, a, rows, plane, first):
            for c in rows:
                nc.sync.dma_start(
                    out=plane[first + c : P : 32, :].bitcast(I32),
                    in_=picked[name][8 * c + 4 * a : P : 32, :].bitcast(I32))

        def load_w2_words(g):
            rows = w2_words.bitcast(I32).rearrange("a p (g c) -> g p a c", g=2)
            nc.sync.dma_start(out=w2_w[g][:].bitcast(I32), in_=rows[g])

        def deal_w2(src, dtype, pair_dtype, name, copy, run):
            blocks = src.shape[1] * src.shape[2] // G
            dst = sbuf([P, blocks, PACK, P], dtype, name)
            pairs_in = src[:].rearrange("p a c -> p (a c)").bitcast(pair_dtype)
            copy(
                out=dst[:].bitcast(pair_dtype).rearrange("p x t (c i) -> p x c t i", i=run),
                in_=pairs_in.rearrange("p (x c i t) -> p x c t i", x=blocks, i=run, t=PACK))
            return dst

        nc.sync.dma_start(list3[:], offs3)
        nc.sync.dma_start(out=tab3_w[:].bitcast(I32), in_=tab3_words[0].bitcast(I32))
        nc.sync.dma_start(list1[:], offs)
        for a in range(2):
            load_scale_rows(tab_s, tab_scales, a)
        load_weight("w1", w1, 0, 0)
        load_scale_rows(tab3_s, tab3_scales, 0)
        for i in range(2):
            load_bias(i)
        nc.sync.dma_start(list2[:], offs2)
        nc.sync.dma_start(out=w2_s[0:P:8].bitcast(I32), in_=w2_scales.bitcast(I32).rearrange("a q w -> q a w"))
        load_words(tab_w[0], tab_words, 0)
        nc.sync.dma_start(out=tab2_s[0:P:8].bitcast(I32), in_=tab2_scales.bitcast(I32).rearrange("a q w -> q a w"))
        pick_scales("tab", tab_s, list1, tab_plane)
        v3_w = gather(tab3_w, list3, U16, "v3_w")
        place_scales("tab", 0, (1, 2, 3), tab_plane, 0)
        load_weight("w3", w3, 0, 0)
        place_scales("tab", 1, (1, 2, 3), tab_plane, 4)
        load_weight("w1", w1, 1, 0)
        pick_scales("tab3", tab3_s, list3, tab3_plane)
        place_scales("tab3", 0, (1, 2, 3), tab3_plane, 0)
        picked2 = sbuf([P, 2, S], U8, "picked_tab2")
        for a in range(2):
            nc.vector.tensor_copy(picked2[:, a, :], tab2_s[:, a, :].indirect(list2[:]))
        picked_rows = picked2[:].rearrange("p a j -> p (a j)").bitcast(I32)
        plane_rows = tab2_plane[:].rearrange("p a j -> p (a j)").bitcast(I32)
        nc.vector.tensor_copy(out=plane_rows, in_=picked_rows)
        w2_dealt_s = deal_w2(w2_s, U8, U16, "w2_dealt_s", nc.vector.tensor_copy, 8)
        dealt_rows = w2_dealt_s[:].rearrange("p x t m -> p (x t m)").bitcast(I32)
        for c in range(1, 4):
            nc.sync.dma_start(out=dealt_rows[c:P:32], in_=dealt_rows[8 * c : P : 32])
        load_words(tab_w[1], tab_words, 1)
        load_w2_words(0)
        for c in range(1, 4):
            nc.sync.dma_start(out=plane_rows[c:P:32], in_=picked_rows[8 * c : P : 32])
        load_words(tab2_w[0], tab2_words, 0)
        load_words(tab2_w[1], tab2_words, 1)
        load_weight("w3", w3, 0, 1)
        for a in range(2):
            load_weight("w1", w1, a, 1)
        load_w2_words(1)
        wo_split = [sbuf([P, PACK, G // 2], F32, "raw_wo_1_0_%d" % u) for u in range(2)]
        for u in range(2):
            load_wo(wo_split[u], 1, G // 2 * u, G // 2)
        for a, g in ((0, 0), (0, 1), (1, 1)):
            raw["wo", a, g] = sbuf([P, PACK, G], F32, "raw_wo_%d_%d" % (a, g), raws)
            load_wo(raw["wo", a, g], a, G * g, G)
        nc.sync.dma_start(out=go_sb[:], in_=go.rearrange("(g p t) -> p g t", p=P, t=PACK))

        rounded, codes, scales = {}, {}, {}

        def round_first_stage(*key):
            src = raw[key][:].rearrange("p j (u t i) -> p u t j i", t=PACK, i=2)
            tile = sbuf([P, PACK * G], BF16, "bf_%s_%d_%d" % key, bfs)
            nc.scalar.copy(out=tile[:].rearrange("p (t u i j) -> p u t j i", t=PACK, i=2, j=PACK), in_=src)
            rounded[key] = [tile]

        def round_on_both(*key):
            src = raw[key][:].rearrange("p j (u t i) -> p u t j i", t=PACK, i=2)
            tiles = [sbuf([P, 2 * G], BF16, "bf_%s_%d_%d_%d" % (key + (b,))) for b in range(2)]
            dsts = [tile[:].rearrange("p (t u i j) -> p u t j i", t=2, i=2, j=PACK) for tile in tiles]
            nc.scalar.copy(out=dsts[0], in_=src[:, :, 0:2])
            nc.vector.tensor_copy(out=dsts[1], in_=src[:, :, 2:4])
            rounded[key] = tiles

        def round_wo(a, g, copy):
            tile = sbuf([P, PACK * G], BF16, "bf_wo_%d_%d" % (a, g), bfs)
            copy(out=tile[:].rearrange("p (b e m j) -> p b m j e", b=2, e=2, j=PACK),
                 in_=raw["wo", a, g][:].rearrange("p j (m b e) -> p b m j e", b=2, e=2))
            rounded["wo", a, g] = [tile]

        def round_wo_part(tile, u, copy):
            dst = tile[:].rearrange("p (b e u m j) -> p u b m j e", b=2, e=2, u=2, j=PACK)
            copy(out=dst[:, u], in_=wo_split[u][:].rearrange("p j (m b e) -> p b m j e", b=2, e=2))

        def quantise_weight(*key):
            codes[key] = sbuf([P, G], U32, "codes_%s_%d_%d" % key)
            scales[key] = sbuf([P, G], U8, "scales_%s_%d_%d" % key)
            width = G // len(rounded[key])
            for b, part in enumerate(rounded[key]):
                span = slice(width * b, width * (b + 1))
                nc.vector.quantize_mx(out=codes[key][:, span].bitcast(FP8X4), scales=scales[key][:, span], in_=part[:])

        def weight(key, t):
            return dict(lhsT=codes[key][:, cols(t)].bitcast(FP8X4), lhsT_scale=scales[key][:, cols(t)])

        v_w = [sbuf([P, S], U32, "v_w%d" % a) for a in range(2)]
        v2_w = [sbuf([P, S], U32, "v2_w%d" % a) for a in range(2)]
        word = [sbuf([P, 2, PACK, HALF], F32, "word%d" % g) for g in range(2)]
        gate_1 = sbuf([P, 2, PACK, HALF], F32, "gate_1")
        gate = {}
        for half in range(2):
            for pair in range(2):
                gate[0, half, pair] = sbuf([P, 2, HALF], F32, "gate_0_%d_%d" % (half, pair))[:]
                gate[1, half, pair] = gate_1[:, half, 2 * pair : 2 * pair + 2, :]
        dom0 = sbuf([P, 2, PACK, HALF], F32, "dom0")
        y_scales = sbuf([P, 2, S], U8, "y_scales")
        word_ps, dom_ps, sense_ps, y_ps = {}, {}, {}, {}
        taken, h_bf, h_codes, h_scales, y, y_bf = {}, {}, {}, {}, {}, {}

        def domain(g):
            for t in range(PACK):
                dom_ps[g, t] = bank(HIGH[t])
                nc.tensor.matmul_mx(
                    out=dom_ps[g, t][:], **weight(("w3", 0, g), t),
                    rhs=v3_w[:].bitcast(FP4X4), rhs_scale=tab3_plane[:], start=True, stop=True)

        def word0_pass(a, half):
            for pair in range(2):
                if a == 0:
                    word_ps[0, half, pair] = bank(LOW[2 * half + pair])
                for e in range(2):
                    nc.tensor.matmul_mx(
                        out=word_ps[0, half, pair][:, slots(e)], **weight(("w1", a, 0), 2 * pair + e),
                        rhs=v_w[a][:, slots(half)].bitcast(FP8X4), rhs_scale=tab_plane[4 * a :, slots(half)],
                        start=(a == 0 and e == 0), stop=(a == 1 and e == 1))

        def word1_pass(a):
            for t in range(PACK):
                if a == 0:
                    word_ps[1, t] = bank(LOW[t])
                nc.tensor.matmul_mx(
                    out=word_ps[1, t][:], **weight(("w1", a, 1), t),
                    rhs=v_w[a][:].bitcast(FP8X4), rhs_scale=tab_plane[4 * a :, :], start=(a == 0), stop=(a == 1))

        def sense_pass(g, a, half, banks):
            for pair in range(2):
                if a == 0:
                    sense_ps[g, half, pair] = bank(banks[2 * half + pair])
                for e in range(2):
                    t = 2 * pair + e
                    nc.tensor.matmul_mx(
                        out=sense_ps[g, half, pair][:, slots(e)],
                        lhsT=w2_dealt_w[g][:, a, t, :].bitcast(FP4X4), lhsT_scale=w2_dealt_s[:, 2 * a + g, t, :],
                        rhs=v2_w[a][:, slots(half)].bitcast(FP8X4), rhs_scale=tab2_plane[:, a, slots(half)],
                        start=(a == 0 and e == 0), stop=(a == 1 and e == 1))

        def gated_sense(g, half):
            for pair in range(2):
                both = slice(2 * pair, 2 * pair + 2)
                nc.vector.tensor_tensor(
                    out=taken[g, half][:, both, :], in0=two(sense_ps[g, half, pair]),
                    in1=gate[g, half, pair], op=ALU.mult)

        def finish_h(g, half):
            h_bf[g, half] = sbuf([P, PACK * HALF], BF16, "h_bf_%d_%d" % (g, half))
            nc.vector.tensor_tensor(
                out=h_bf[g, half][:].rearrange("p (c i t) -> p c t i", i=4, t=PACK),
                in0=word[g][:, half].rearrange("p t (c i) -> p c t i", i=4),
                in1=taken[g, half].rearrange("p t (c i) -> p c t i", i=4),
                op=ALU.subtract)

        def quantise_h(g, half):
            h_codes[g, half] = sbuf([P, HALF], U32, "h_codes_%d_%d" % (g, half))
            h_scales[g, half] = sbuf([P, HALF], U8, "h_scales_%d_%d" % (g, half))
            nc.vector.quantize_mx(
                out=h_codes[g, half][:].bitcast(FP8X4), scales=h_scales[g, half][:], in_=h_bf[g, half][:])

        def out_pass(half, g, a):
            for pair in range(2):
                if a == 0:
                    y_ps[half, g, pair] = bank((HIGH, LOW)[half][2 * g + pair])
                for e in range(2):
                    nc.tensor.matmul_mx(
                        out=y_ps[half, g, pair][:, slots(e)], **weight(("wo", a, g), 2 * pair + e),
                        rhs=h_codes[a, half][:].bitcast(FP8X4), rhs_scale=h_scales[a, half][:],
                        start=(a == 0 and e == 0), stop=(a == 1 and e == 1))

        def parts(half, g):
            width = HALF // 2 if (half, g) == (1, 1) else HALF
            return [slice(first, first + width) for first in range(0, HALF, width)]

        def gain_and_store(half, g):
            y[half, g] = sbuf([P, PACK, HALF], F32, "y_%d_%d" % (half, g))
            for part in parts(half, g):
                for t in range(PACK):
                    nc.scalar.activation(
                        y[half, g][:, t, part], two(y_ps[half, g, t // 2])[:, t % 2, part],
                        ACT.Copy, scale=go_sb[:, g, t : t + 1])
            rows = out_0[G * g : G * (g + 1), slots(half)]
            nc.sync.dma_start(out=rows.rearrange("(p t) j -> p t j", t=PACK), in_=y[half, g][:])

        def quantise_y(half, g):
            y_bf[half, g] = sbuf([P, PACK * HALF], BF16, "y_bf_%d_%d" % (half, g))
            y_codes = sbuf([P, HALF], U32, "y_codes_%d_%d" % (half, g))
            for part in parts(half, g):
                values = y_bf[half, g][:, PACK * part.start : PACK * part.stop]
                nc.vector.tensor_copy(
                    out=values.rearrange("p (c i t) -> p c t i", i=4, t=PACK),
                    in_=y[half, g][:, :, part].rearrange("p t (c i) -> p c t i", i=4))
                nc.vector.quantize_mx(
                    out=y_codes[:, part].bitcast(FP8X4), scales=y_scales[:, g, slots(half)][:, part], in_=values)
            nc.sync.dma_start(
                out=out_1[g, :, slots(half), :].rearrange("p m t -> p (m t)").bitcast(I32),
                in_=y_codes[:].bitcast(I32))

        round_first_stage("w1", 0, 0)
        quantise_weight("w1", 0, 0)
        nc.vector.tensor_copy(v_w[0][:], tab_w[0][:].indirect(list1[:]))
        for half in range(2):
            word0_pass(0, half)
        round_first_stage("w3", 0, 0)
        quantise_weight("w3", 0, 0)
        domain(0)
        round_first_stage("w1", 1, 0)
        quantise_weight("w1", 1, 0)
        for t in range(PACK):
            nc.scalar.activation(
                dom0[:, :, t, :], two(dom_ps[0, t]), ACT.Identity, bias=bd_sb[:, 0, 2 * t : 2 * t + 1])
        for half in range(2):
            gather_half(v_w[1], tab_w[1], list1, half)
            word0_pass(1, half)
        w2_dealt_w = [deal_w2(w2_w[0], U16, U32, "w2_dealt_w0", nc.vector.tensor_copy, 4)]
        for half in range(2):
            for pair in range(2):
                if half == 1 and pair == 1:
                    for u in range(2):
                        gather_half(v2_w[0], tab2_w[0], list2, u)
                        sense_pass(0, 0, u, HIGH)
                nc.vector.tensor_tensor(
                    out=gate[0, half, pair], in0=two(word_ps[0, half, pair]),
                    in1=dom0[:, half, 2 * pair : 2 * pair + 2, :], op=ALU.mult)
                nc.scalar.activation(gate[0, half, pair], gate[0, half, pair], ACT.Tanh)
        for half in range(2):
            for pair in range(2):
                nc.scalar.copy(out=word[0][:, half, 2 * pair : 2 * pair + 2, :], in_=two(word_ps[0, half, pair]))
        for half in range(2):
            gather_half(v2_w[1], tab2_w[1], list2, half)
            sense_pass(0, 1, half, HIGH)
        taken_0 = sbuf([P, 2, PACK, HALF], F32, "taken_0")
        for half in range(2):
            taken[0, half] = taken_0[:, half]
            gated_sense(0, half)

        round_first_stage("w3", 0, 1)
        quantise_weight("w3", 0, 1)
        domain(1)
        finish_h(0, 0)
        round_first_stage("w1", 0, 1)
        quantise_weight("w1", 0, 1)
        word1_pass(0)
        round_on_both("w1", 1, 1)
        quantise_weight("w1", 1, 1)
        word1_pass(1)
        finish_h(0, 1)
        w2_dealt_w.append(deal_w2(w2_w[1], U16, U32, "w2_dealt_w1", nc.vector.tensor_copy, 4))
        for half in range(2):
            quantise_h(0, half)
        bf_wo_split = sbuf([P, PACK * G], BF16, "bf_wo_1_0", bfs)
        rounded["wo", 1, 0] = [bf_wo_split]
        round_wo_part(bf_wo_split, 0, nc.scalar.copy)
        for t in range(PACK):
            nc.scalar.copy(out=word[1][:, :, t, :], in_=two(word_ps[1, t]))
        for t in range(PACK):
            nc.vector.scalar_tensor_tensor(
                out=gate_1[:, :, t, :], in0=two(dom_ps[1, t]), scalar=bd_sb[:, 1, 2 * t : 2 * t + 1],
                in1=word[1][:, :, t, :], op0=ALU.add, op1=ALU.mult)
            nc.scalar.activation(gate_1[:, :, t, :], gate_1[:, :, t, :], ACT.Tanh)
        for half in range(2):
            for a in range(2):
                sense_pass(1, a, half, LOW)
        round_wo_part(bf_wo_split, 1, nc.scalar.copy)
        round_wo(0, 0, nc.vector.tensor_copy)
        for a in range(2):
            round_wo(a, 1, nc.scalar.copy)

        for half in range(2):
            taken[1, half] = sbuf([P, PACK, HALF], F32, "taken_1_%d" % half)[:]
        gated_sense(1, 0)
        quantise_weight("wo", 0, 0)
        for half in range(2):
            out_pass(half, 0, 0)
        finish_h(1, 0)
        quantise_weight("wo", 1, 0)
        quantise_h(1, 0)
        out_pass(0, 0, 1)
        gated_sense(1, 1)
        quantise_weight("wo", 0, 1)
        for half in range(2):
            out_pass(half, 1, 0)
        quantise_weight("wo", 1, 1)
        out_pass(0, 1, 1)
        finish_h(1, 1)
        quantise_h(1, 1)
        for g in range(2):
            out_pass(1, g, 1)
        for half in range(2):
            for g in range(2):
                gain_and_store(half, g)
        for half in range(2):
            for g in range(2):
                quantise_y(half, g)
        rows = out_2.bitcast(I32).rearrange("g (quad c) w -> c quad g w", c=4)
        for c in range(4):
            queue = nc.scalar if c % 2 else nc.sync
            queue.dma_start(out=rows[c], in_=y_scales[c:P:32].bitcast(I32))
